import numpy as np, ml_dtypes
CORES = [24,25,26,27,28,29,30,31]
N = 8
import mx_ref
BF = ml_dtypes.bfloat16
def entries(a):
    return np.ascontiguousarray(a.T).reshape(-1)
def table(e):
    return np.ascontiguousarray(np.reshape(e, (-1, 16)).T).astype(np.int32)
def pick(q, e):
    c = np.concatenate([q[0].reshape(128, -1, 4), np.zeros((128, 1, 4), np.uint8)], axis=1); s = np.concatenate([q[1], np.ones((16, 1), np.uint8)], axis=1)
    return (np.ascontiguousarray(c[:, e].reshape(128, -1)), np.ascontiguousarray(s[:, e]))
def join(*qs):
    return (np.concatenate([q[0] for q in qs], axis=1), np.concatenate([q[1] for q in qs], axis=1))
def put(q, e, v):
    c, s = q[0].reshape(128, -1, 4).copy(), q[1].copy(); c[:, e] = v[0].reshape(128, -1, 4); s[:, e] = v[1]
    return (c.reshape(128, -1), s)
def pk(c, s):
    return (np.ascontiguousarray(c), mx_ref.live(s))
def emit(q):
    return q[0], q[1]
def cut(t, i, w=512):
    return t[:, w * i:w * i + w]
def f(rng, *shape):
    return mx_ref.flush((rng.standard_normal(shape, dtype=np.float32) * np.exp2(rng.integers(-2, 3, shape[:-1] + (1,)))).astype(BF))
def wide(rng, *shape, cols=0):
    v = rng.standard_normal(shape, dtype=np.float32) * np.exp2(rng.integers(-12, 13, shape)).astype(np.float32)
    if cols: v *= np.repeat(np.exp2(rng.integers(-cols, cols + 1, shape[:-2] + (1, shape[-1] // 4))) * (rng.random(shape[:-2] + (1, shape[-1] // 4)) > 0.0625), 4, axis=-1).astype(np.float32)
    return mx_ref.flush(v.astype(BF))
P, K, R, LC = 256, 32, 3, 48
def near(nb):
    return np.stack([entries(nb[r]).reshape(P, 3) for r in range(N)]).astype(np.int64)
def play(x, bb, nb, u, v, a):
    n = near(nb)
    X = join(*[mx_ref.quantize(np.ascontiguousarray(x[r])) for r in range(N)])
    qu, qv = mx_ref.quantize(np.ascontiguousarray(u[0])), mx_ref.quantize(np.ascontiguousarray(v[0]))
    qa = [[mx_ref.quantize(np.ascontiguousarray(cut(a[r], i))) for i in range(4)] for r in range(N)]
    fixed = [mx_ref.matmul(qv, mx_ref.quantize(np.ascontiguousarray(bb[r])))[0] for r in range(N)]
    b = bb.astype(np.float32).reshape(N, 128, P, 4)
    done, res, made = np.zeros((N, R, K), np.int64), [], []
    for t in range(R):
        e = mx_ref.matmul(qu, X)[0]
        new = []
        for r in range(N):
            z = ((e[n[r, :, 0]] + e[n[r, :, 1]]) + e[n[r, :, 2]]) - fixed[r]
            j = np.argsort(-np.abs(z), kind="stable")[:K]
            nbs = pick(X, n[r, j].T.reshape(-1))
            s = []
            for i in range(4):
                m = mx_ref.matmul(qa[r][i], nbs)
                s.append((m[:, :K] + m[:, K:2 * K]) + m[:, 2 * K:])
            g = np.float32(0.05) * np.stack(s, axis=2) + b[r][:, j]
            new.append(mx_ref.quantize(np.ascontiguousarray(g.reshape(128, -1).astype(BF))))
            done[r, t] = j
            res.append(z)
            made.append(g)
        X = put(X, np.concatenate([P * r + done[r, t] for r in range(N)]), join(*new))
    return X, done, np.stack(res), np.stack(made)
def fit(z, g):
    top = np.abs(g.astype(BF).astype(np.float32)).reshape(-1, 16, 8, K, 4).max(axis=(2, 4))
    g = np.abs(g)
    return bool(np.isfinite(z).all() and np.isfinite(g).all() and ((g == 0) | (g >= 2.0 ** -60) & (g <= 2.0 ** 60)).all() and ((top == 0) | (top >= 2.0 ** -30) & (top <= 2.0 ** 30)).all())
def bf(v):
    return mx_ref.flush(np.asarray(v, np.float32).astype(BF))
def lone(c):
    t = np.zeros((N, 128, 512), BF)
    t[:, :, :4] = c
    return t
def few(rng, q, n, free, most):
    p = rng.permutation(free)[:most]
    return q * P + rng.permutation(np.concatenate([p, p[rng.integers(0, p.size, P)]])[:n])
def graph(rng, src=None, free=None, most=LC):
    n = np.zeros((N, P, 3), np.int64)
    if free is None: free = [np.arange(P)] * N
    for r in range(N):
        n[r, :, :2] = r * P + rng.choice(free[r], (P, 2))
        s = (r + rng.integers(1, N, P)) % N if src is None else np.full(P, src[r])
        for q in range(N):
            i = np.flatnonzero(s == q)
            n[r, i, 2] = few(rng, q, i.size, free[q], most)
    return n
def stored(n):
    return np.stack([table(n[r].reshape(-1)) for r in range(N)])
def setup_inputs(rng):
    return {"x": f(rng, N, 128, 4 * P), "bb": f(rng, N, 128, 4 * P), "nb": stored(graph(rng)), "u": lone(f(rng, 128, 4)), "v": lone(f(rng, 128, 4)),
            "a": bf(f(rng, N, 128, 2048).astype(np.float32) * np.float32(2.0 ** -4)), "w": f(rng, N, 128, 512)}
def signs(rng):
    return 1.0 - 2.0 * rng.integers(0, 2, (128, 4))
def signed(rng, sg, size):
    return bf(((1 + rng.random((N, 128, P, 4))) * size[:, None, :, None] * sg[:, None, :] + 0.0).reshape(N, 128, 4 * P))
def single(rng, sg, size):
    return lone(bf((1 + rng.random((128, 4))) * sg * size))
def setup_inputs_again(rng):
    d, sg, size, m = setup_inputs(rng), signs(rng), np.zeros((N, P)), K // 8
    o = np.stack([rng.permutation(P) for r in range(N)])
    rest = np.sort(o[:, 7 * m:], axis=1)
    hold = np.stack([rng.permutation(rest[r, -5:]) for r in range(N)])
    n = graph(rng, free=rest[:, :-5], most=LC - 2)
    large, small = (1 + rng.random((128, 4))) * sg * 2.0 ** 20, (1 + rng.random((128, 4))) * sg * 2.0 ** -8
    top = np.arange(128)[:, None] < 64
    five = np.stack([large * top, large * ~top, -large, large, small], axis=1) + 0.0
    x = np.zeros((N, 128, P, 4))
    for r in range(N):
        x[r][:, hold[r]] = five
        h, left, both, alone = o[r, :4 * m], o[r, 4 * m:5 * m], o[r, 5 * m:6 * m], o[r, 6 * m:7 * m]
        size[r, h] = 64
        size[r, left] = 64
        n[r, h, 0] = r * P + rng.permutation(h)
        n[r, left, 0], n[r, left, 1] = r * P + hold[r, 0], r * P + hold[r, 1]
        n[r, both, 0], n[r, both, 1] = r * P + hold[r, 3], r * P + hold[r, 2]
        for i, k in ((left, 2), (both, 4), (alone, 4)):
            q = n[r, i, 2] // P
            n[r, i, 2] = q * P + hold[q, k]
    bb = signed(rng, sg, size).reshape(N, 128, P, 4)
    for r in range(N): bb[r][8:, o[r, 4 * m:5 * m]] = 0
    d.update(x=bf(x.reshape(N, 128, 4 * P)), bb=bb.reshape(N, 128, 4 * P), nb=stored(n), u=single(rng, sg, 1.0), v=single(rng, sg, 4.0))
    return d
def setup_inputs_far(rng):
    h = int(rng.integers(0, N))
    src = np.full(N, h)
    src[h] = (h + int(rng.integers(1, N))) % N
    d, n, sg, size = setup_inputs(rng), graph(rng, src), signs(rng), np.full((N, P), 2.0 ** 20)
    for r in range(N):
        first = np.unique(n[r, :, 2], return_index=True)[1]
        size[r, rng.permutation(first)[:K]] = 2.0 ** 26
    d.update(x=signed(rng, sg, np.full((N, P), 2.0 ** 20)), bb=signed(rng, sg, size), nb=stored(n), u=single(rng, sg, 2.0 ** 23), v=single(rng, sg, 2.0 ** 29))
    return d
def setup_inputs_moved(rng):
    d, n, sg, size = setup_inputs(rng), np.zeros((N, P, 3), np.int64), signs(rng), np.full((N, P), 2.0 ** -4)
    o = [rng.permutation(P) for r in range(N)]
    for r in range(N):
        size[r, o[r][:K]] = 64
        n[r, :, :2] = r * P + rng.choice(o[r][K:], (P, 2))
        m = np.zeros(P, bool)
        m[rng.permutation(P)[:K + K // 2]] = True
        s = (r + rng.integers(1, N, P)) % N
        for q in range(N):
            hot, cold = rng.permutation(o[q][:K])[:LC // 2], rng.permutation(o[q][K:])[:LC - LC // 2]
            i, k = np.flatnonzero((s == q) & m), np.flatnonzero((s == q) & ~m)
            n[r, i, 2] = q * P + rng.choice(hot, i.size)
            n[r, k, 2] = q * P + rng.choice(cold, k.size)
    d.update(x=signed(rng, sg, np.full((N, P), 2.0 ** -6)), bb=signed(rng, sg, size), nb=stored(n), u=single(rng, sg, 16.0), v=single(rng, sg, 1.0))
    return d
def setup_inputs_spread(rng):
    d = setup_inputs(rng)
    d["x"] = wide(rng, N, 128, 4 * P, cols=4)
    d["bb"] = wide(rng, N, 128, 4 * P, cols=4)
    return d
def setup_inputs_ties(rng):
    d, n = setup_inputs(rng), np.zeros((N, P, 3), np.int64)
    kind = np.stack([rng.permutation(np.arange(P) % 4) for r in range(N)])
    for k in ("x", "bb"):
        c = f(rng, 128, 8).astype(np.float32).reshape(128, 2, 4)
        d[k] = np.stack([bf((c[:, kind[r] >> 1] * (1 - 2 * (kind[r] & 1))[None, :, None]).reshape(128, -1)) for r in range(N)])
    for r in range(N):
        s = (r + rng.integers(1, N, P)) % N
        for k in range(4):
            i = np.flatnonzero(kind[r] == k)
            n[r, i, 0] = r * P + rng.choice(i, i.size)
            n[r, i, 1] = r * P + rng.choice(np.flatnonzero(kind[r] == (k ^ 2)), i.size)
            for q in range(N):
                j = i[s[i] == q]
                n[r, j, 2] = q * P + rng.choice(rng.permutation(np.flatnonzero(kind[q] == k))[:LC // 4], j.size)
    d["nb"] = stored(n)
    return d
def check_inputs(d):
    b = []
    for k in ("x", "bb", "u", "v", "a", "w"):
        t = np.abs(d[k].astype(np.float32))
        if not (np.isfinite(t).all() and ((t == 0) | (t >= 2.0 ** -30) & (t <= 2.0 ** 30)).all()): b.append("a value of " + k)
    for k in ("u", "v"):
        t = d[k].astype(np.float32)
        if (t[:, :, 4:] != 0).any(): b.append(k + " has numbers behind its column 0")
        if (t != t[:1]).any(): b.append(k + " isn't the same on all ranks")
    n = near(d["nb"])
    at, own = n // P, np.arange(N)[:, None, None]
    if n.min() < 0 or n.max() >= N * P or (at[:, :, :2] != own).any() or (at[:, :, 2] == own[:, :, 0]).any(): b.append("nb")
    elif any(np.unique(n[r, :, 2][at[r, :, 2] == q]).size > LC for r in range(N) for q in range(N)): b.append("nb names too many columns of one rank")
    if not b:
        try:
            with np.errstate(all="ignore"):
                X, done, z, g = play(d["x"], d["bb"], d["nb"], d["u"], d["v"], d["a"])
                good = fit(z, g)
        except Exception:
            good = False
        if not good: b.append("a number that the rounds make")
    return b
def reference(x, bb, nb, u, v, a, w):
    X, done, z, g = play(x, bb, nb, u, v, a)
    oc, osc, y = np.zeros((N, 128, 4 * P), np.uint8), np.zeros((N, 16, P), np.uint8), np.zeros((N, 128, P), np.float32)
    for r in range(N):
        q = pick(X, np.arange(P * r, P * r + P))
        oc[r], osc[r] = emit(q)
        y[r] = mx_ref.matmul(mx_ref.quantize(np.ascontiguousarray(w[r])), q)
    return {"oc": oc, "osc": osc, "nd": done.astype(np.float32), "y": y}

@@ -1,0 +1,541 @@
+import numpy as np
+from concourse.bass import DstId, RemoteDMATransfer
+from concourse.mybir import dt, AluOpType, AxisListType, ActivationFunctionType
+
+A = AluOpType
+F = ActivationFunctionType
+P, K, R, LC = 256, 32, 3, 48
+FAR0 = P
+NEW0 = P + 7 * LC
+C05 = 13421773 * 2.0 ** -28
+THIRD = float(np.float32(1.0) / np.float32(3.0))
+KC = 1024 * 255
+TINY = 2.0 ** -110
+CODE, U8, BF, F32, I32, U16 = "float8_e4m3fn_x4", "uint8", "bfloat16", "float32", "int32", "uint16"
+
+
+def _sbuf(dtype, **cols):
+    return {n: ("sbuf", [128, c], dtype) for n, c in cols.items()}
+
+
+SCRATCH = {"pe": ("psum", [128, 512], F32), "pf": ("psum", [128, 512], F32), "ps": ("psum", [128, 2048], F32)}
+SCRATCH.update(_sbuf(F32, nbf=768, iot=2048, jr=256, cf=64, jo=2, ka0=256, ka=256, kat=64, bi=4, junk=256, junk2=256, junk3=256, ac=16, fa=16, nf=2,
+                     fx=64, fr=256, cx2=64, cr2=256, cc=128, lo=16, lsum=4, ea=1104, fn=256, fz=64, za=64, zb=64, zc=64, zd=64, z=256, zt=64, dd=128, jj=128, rk=4,
+                     cx=64, cr=64, cl=256, sw_=12, sel=4, soc=6, ng=96, nt=96, ndf=2, c4q=4, bbs=128, sc4=512, ndo=4,
+                     np0=2048, np1=2048, ndv=512, nl=1536, db=192, dt_=192, dbf=12, fl=256, lx=64, ol=256, od=96, og=256, ogt=256, yt=256))
+SCRATCH.update(_sbuf(I32, nb32=48, ci=16, fi=16, frf=256))
+SCRATCH.update(_sbuf(U16, nbt=48, lst=4, rl=24, rl2=128, rep=24, so=6, po=6, ndg=4, ndl=2, nda0=16, nda1=16, bo=8, dbt=12, dnb=12, of=36, frt=4, d8=16, oo=16))
+SCRATCH.update(_sbuf(BF, xb=1024, bb_t=1024, at=2048, wt=512, u4=4, v4=4, ones=128, ub=512, vb=512, mm_=512, xt=512))
+for _c, _s, _n in (("qx", "sx", 256), ("qb", "sb", 256), ("qu", "su", 128), ("qv", "sv", 128), ("qa", "sa", 512), ("qw", "sw", 128), ("slc", "sls", 336),
+                   ("g0", "h0", 592), ("g1", "h1", 944), ("g2", "h2", 1200), ("nq0", "ns0", 128), ("nq1", "ns1", 128), ("nq2", "ns2", 128),
+                   ("ow", "os_", 640), ("occ", "ocs", 256)):
+    SCRATCH.update({_c: ("sbuf", [128, _n], CODE), _s: ("sbuf", [128, _n], U8)})
+SEMAPHORES = ["cv", "cs", "ct", "cg"] + ["q%d" % i for i in range(60)] + ["arl", "ac0", "as0", "an0", "an1", "ac1", "as1", "ac2", "as2"]
+
+
+def r(name, c0, c1, step=1, p0=0, p1=128):
+    return (name, c0, c1, step, p0, p1)
+
+
+def rank_program(g, core, T, topo):
+    rank = T.rank_of(core)
+    if rank is None:
+        return
+    eng = {"v": g.vector, "s": g.scalar, "t": g.tensor, "g": g, "y": g.sync}
+    csem = {"v": "cv", "s": "cs", "t": "ct", "g": "cg"}
+    cnt, known, log, pool, snaps = {}, {q: {} for q in eng}, {}, [0], {}
+
+    def ap(x):
+        return T[x[0]][x[4]:x[5], x[1]:x[2]:x[3]] if x[3] != 1 else T[x[0]][x[4]:x[5], x[1]:x[2]]
+
+    def span(x):
+        if SCRATCH[x[0]][0] == "psum":
+            return x[1] // 512 * 512, (x[2] + 511) // 512 * 512, 0, 128
+        return x[1], x[2], x[4], x[5]
+
+    def learn(q, tok):
+        k, (sem, c) = known[q], tok
+        if k.get(sem, 0) >= c:
+            return
+        k[sem] = c
+        for n, m in snaps.get(tok, {}).items():
+            if k.get(n, 0) < m:
+                k[n] = m
+
+    def clash(a, b):
+        return not (a[3] == b[3] and a[3] > 1 and (a[1] - b[1]) % a[3])
+
+    def order(q, reads, writes, need=None):
+        need = need or {}
+        for x, w in [(x, 0) for x in reads] + [(x, 1) for x in writes]:
+            s = span(x)
+            bank = SCRATCH[x[0]][0] == "psum"
+            for y, t, w2, tok, q2 in log.get(x[0], []):
+                if (w or w2 or (bank and q2 != q)) and s[0] < t[1] and t[0] < s[1] and s[2] < t[3] and t[2] < s[3] and clash(x, y):
+                    need[tok[0]] = max(need.get(tok[0], 0), tok[1])
+        for sem, c in sorted(need.items(), key=lambda i: -sum(snaps.get(i, {}).values())):
+            if known[q].get(sem, 0) < c:
+                eng[q].wait_ge(T.sem[sem], c)
+                learn(q, (sem, c))
+
+    def note(q, reads, writes, tok):
+        for x in writes:
+            s = span(x)
+            if x[3] == 1:
+                log[x[0]] = [e for e in log.get(x[0], []) if not (s[0] <= e[1][0] and e[1][1] <= s[1] and s[2] <= e[1][2] and e[1][3] <= s[3])]
+            log.setdefault(x[0], []).append((x, s, 1, tok, q))
+        for x in reads:
+            log.setdefault(x[0], []).append((x, span(x), 0, tok, q))
+
+    def emit(q, fn, reads, writes):
+        sem = csem[q]
+        order(q, reads, writes, {sem: cnt[sem]} if q == "g" and sem in cnt else None)
+        cnt[sem] = cnt.get(sem, 0) + 1
+        tok = (sem, cnt[sem])
+        snaps[tok] = dict(known[q])
+        fn().then_inc(T.sem[sem], 1)
+        note(q, reads, writes, tok)
+
+    def newsem():
+        pool[0] += 1
+        return "q%d" % (pool[0] - 1)
+
+    def src(x):
+        if len(x) == 2:
+            return ap(x[0]).indirect(ap(x[1])), [x[0], x[1]]
+        return ap(x), [x]
+
+    def sc(x):
+        return (ap(x), [x]) if isinstance(x, tuple) else (x, [])
+
+    def copy(q, out, in_):
+        i, rd = src(in_)
+        if q == "v":
+            emit(q, lambda: g.vector.tensor_copy(ap(out), i), rd, [out])
+        else:
+            emit(q, lambda: g.scalar.activation(ap(out), i, F.Copy), rd, [out])
+
+    def scatter(win, off, in_):
+        emit("v", lambda: g.vector.tensor_copy(ap(win).indirect(ap(off)), ap(in_)), [in_, off], [win])
+
+    def act(out, in_, func, bias=0.0, scale=1.0, acc=None):
+        i, rd = src(in_)
+        b, rb = sc(bias)
+        s, rs = sc(scale)
+        if acc is None:
+            emit("s", lambda: g.scalar.activation(ap(out), i, func, bias=b, scale=s), rd + rb + rs, [out])
+        else:
+            emit("s", lambda: g.scalar.activation(ap(out), i, func, bias=b, scale=s, accum_out=ap(acc)), rd + rb + rs, [out, acc])
+
+    def ts(out, in_, s1, op0, s2=None, op1=None):
+        i, rd = src(in_)
+        a, ra = sc(s1)
+        b, rb = sc(s2)
+        if op1 is None:
+            emit("v", lambda: g.vector.tensor_scalar(ap(out), i, a, None, op0), rd + ra, [out])
+        else:
+            emit("v", lambda: g.vector.tensor_scalar(ap(out), i, a, b, op0, op1), rd + ra + rb, [out])
+
+    def tt(out, in0, in1, op):
+        i, rd = src(in0)
+        emit("v", lambda: g.vector.tensor_tensor(ap(out), i, ap(in1), op), rd + [in1], [out])
+
+    def red(out, in_):
+        emit("v", lambda: g.vector.tensor_reduce(ap(out), ap(in_), AxisListType.X, A.add), [in_], [out])
+
+    def tr(out, in_):
+        emit("v", lambda: g.vector.transpose(ap(out), ap(in_)), [in_], [out])
+
+    def fill(out, val):
+        emit("v", lambda: g.vector.memset(ap(out), val), [], [out])
+
+    def quant(q, s, in_):
+        emit("v", lambda: g.vector.quantize_mx(ap(q), ap(s), ap(in_)), [in_], [q, s])
+
+    def mm(out, wq, ws, xq, xs):
+        emit("t", lambda: g.tensor.matmul_mx(ap(out), ap(wq), ap(ws), ap(xq), ap(xs), True, True), [wq, ws, xq, xs], [out])
+
+    def iota(out, pattern, base, cm, flag=True):
+        if flag:
+            emit("g", lambda: g.iota(ap(out), pattern, base, cm, allow_small_or_imprecise_dtypes=True), [], [out])
+        else:
+            emit("g", lambda: g.iota(ap(out), pattern, base, cm), [], [out])
+
+    def pick(qo, so, win, wins, off):
+        emit("v", lambda: g.vector.tensor_copy(ap(qo).bitcast(dt.uint32), ap(win).bitcast(dt.uint32).indirect(ap(off))), [win, off], [qo])
+        emit("s", lambda: g.scalar.activation(ap(so), ap(wins).indirect(ap(off)), F.Copy), [wins, off], [so])
+
+    def side(x):
+        return ap(x).bitcast(dt.uint8) if SCRATCH[x[0]][2] == CODE else ap(x)
+
+    def dma(moves):
+        sem = newsem()
+        done, sn = [], {}
+        for q, out, in_ in moves:
+            wr = [out] if isinstance(out, tuple) else []
+            rd = [in_] if isinstance(in_, tuple) else []
+            order(q, rd, wr)
+            eng[q].dma_start(side(out) if wr else out, side(in_) if rd else in_).then_inc(T.sem[sem], 16)
+            done.append((q, rd, wr))
+        cnt[sem] = 16 * len(moves)
+        tok = (sem, cnt[sem])
+        for q, rd, wr in done:
+            for n, m in known[q].items():
+                sn[n] = max(sn.get(n, 0), m)
+        snaps[tok] = sn
+        for q, rd, wr in done:
+            note(q, rd, wr, tok)
+
+    peers = [(rank + 1 + i) % 8 for i in range(7)]
+    across = [d for d in peers if topo.die(T.cores[d]) != topo.die(core)]
+    masks = {}
+    for d in peers:
+        e = topo.engines(core, T.cores[d])
+        lane = e[0::2] if d in across else e[1::2]
+        k = (across if d in across else [s for s in peers if s not in across]).index(d)
+        masks[d] = sum(1 << x for x in lane[2 * k:2 * k + 2])
+
+    def send(moves, arr):
+        sem = newsem()
+        order("g", [m[1] for m in moves], [])
+        trs = []
+        for d, s, l in moves:
+            rid, pid, _ = topo.addr(T.cores[d])
+            trs.append(RemoteDMATransfer(dst_ids=[DstId(rid=rid, pnc=pid)], dma_engine_mask=masks[d], remote_sem=T.sem[arr], srcs=[side(s)], dsts=[side(l)]))
+        g.remote_dma_fused(trs, local_sem=T.sem[sem])
+        cnt[sem] = 2 * len(moves)
+        snaps[(sem, cnt[sem])] = dict(known["g"])
+        note("g", [m[1] for m in moves], [], (sem, cnt[sem]))
+
+    def lands(regions, arr):
+        cnt[arr] = 14
+        note("r", [], regions, (arr, 14))
+
+    def exchange(n, w=64):
+        for a in range(4):
+            b = (a + 1) % 4
+            copy("vs"[a % 2], r(n, w, 2 * w, 1, 32 * a, 32 * a + 32), r(n, 0, w, 1, 32 * b, 32 * b + 32))
+        copy("v", r(n, 2 * w, 4 * w, 1, 0, 64), r(n, 0, 2 * w, 1, 64, 128))
+        copy("s", r(n, 2 * w, 4 * w, 1, 64, 128), r(n, 0, 2 * w, 1, 0, 64))
+
+    def col(n, c, w=1):
+        return r(n, c, c + w)
+
+    def blk(n, c0, c1, a):
+        return r(n, c0, c1, 1, 32 * a, 32 * a + 32)
+
+    mv = []
+    for gr in range(8):
+        a = gr // 2
+        q = "ys"[gr % 2]
+        mv.append((q, r("nb32", 0, 48 - 12 * a, 1, 16 * gr, 16 * gr + 16), T.nb[:, 12 * a:48]))
+        if a:
+            mv.append((q, r("nb32", 48 - 12 * a, 48, 1, 16 * gr, 16 * gr + 16), T.nb[:, 0:12 * a]))
+    dma(mv)
+    dma([("y", r("xb", 0, 1024), T.x[:])])
+    dma([("s", r("u4", 0, 4), T.u[:, 0:4]), ("s", r("v4", 0, 4), T.v[:, 0:4])])
+    dma([("y", r("bb_t", 0, 1024), T.bb[:])])
+    dma([("y", r("at", 0, 2048), T.a[:])])
+    dma([("y", r("wt", 0, 512), T.w[:])])
+
+    iota(r("ci", 0, 1), [[0, 1]], 0, 1, False)
+    iota(r("iot", 0, 256), [[1, 256]], 0, 0)
+    iota(r("lo", 8, 11), [[4096, 3]], 0, 0)
+    iota(r("dbf", 0, 12), [[1, 3], [96, 2], [0, 2]], 0, 0)
+    iota(r("soc", 0, 6), [[1, 3], [0, 2]], 768, 0)
+    ts(r("ci", 1, 2), r("ci", 0, 1), 31, A.bitwise_and)
+    ts(r("ci", 2, 3), r("ci", 0, 1), 15, A.bitwise_and)
+    copy("v", r("cf", 0, 3), r("ci", 0, 3))
+    ts(col("cf", 26), col("cf", 0), col("cf", 1), A.subtract, 2.0, A.mult)
+    ts(r("iot", 256, 512), r("iot", 0, 256), 256.0, A.add)
+    act(r("iot", 512, 1024), r("iot", 0, 512), F.Copy, bias=512.0)
+    act(r("iot", 1024, 1536), r("iot", 0, 512), F.Copy, bias=1024.0)
+    act(r("iot", 1536, 2048), r("iot", 0, 512), F.Copy, bias=1536.0)
+    ts(r("frf", 0, 256), r("iot", 0, 256), col("cf", 26), A.add)
+    tt(col("jo", 0), col("cf", 26), col("cf", 1), A.add)
+    ts(r("frf", 0, 256), r("frf", 0, 256), 255, A.bitwise_and)
+    ts(col("jo", 1), col("jo", 0), 32.0, A.add)
+
+    copy("v", r("nbt", 0, 48), r("nb32", 0, 48))
+    copy("v", r("nbf", 0, 384), (r("iot", 0, 2048), r("nbt", 0, 24)))
+    copy("s", r("nbf", 384, 768), (r("iot", 0, 2048), r("nbt", 24, 48)))
+    copy("v", r("jr", 0, 256), r("frf", 0, 256))
+    C4096, CM128, C1024, CONE = r("cc", 0, 32), r("cc", 32, 64), r("cc", 64, 96), r("cc", 96, 128)
+    fill(C4096, 4096.0)
+    fill(CM128, -128.0)
+    act(r("ka0", 0, 256), r("nbf", 2, 768, 3), F.Copy, scale=256.0)
+    tt(r("ka", 0, 256), r("ka0", 0, 256), r("jr", 0, 256), A.add)
+    tr(r("kat", 0, 64), r("ka", 0, 64))
+    ts(r("bi", 0, 2), r("kat", 0, 64, 32), -1.0, A.mult, 0.5, A.add)
+    tt(r("bi", 2, 4), r("bi", 0, 2), r("jo", 0, 2), A.add)
+    for i in range(4):
+        act(r("junk", 0, 256), r("ka", 0, 256), F.Sign, bias=col("bi", i), acc=col("ac", i))
+    ts(r("fa", 0, 2), r("bi", 2, 4), 0.5, A.subtract, -1.0 / 256, A.mult)
+    ts(r("fa", 2, 4), r("fa", 0, 2), -1.0, A.mult, 0.5, A.add)
+    copy("v", r("fi", 0, 2), r("fa", 0, 2))
+    ts(r("fi", 2, 4), r("fi", 0, 2), 255, A.bitwise_and)
+    copy("v", r("fa", 4, 6), r("fi", 2, 4))
+    ts(col("cf", 17), col("cf", 0), col("cf", 2), A.subtract, 16.0, A.mult)
+    ts(col("cf", 18), col("cf", 2), 256.0, A.mult)
+    ts(r("lo", 0, 3), r("lo", 8, 11), col("cf", 18), A.add, 32768.0, A.add)
+    fill(col("cf", 20), 256.0)
+    tt(r("nf", 0, 2), r("ac", 0, 2), r("ac", 2, 4), A.not_equal)
+    ts(r("fx", 0, 32), C4096, col("nf", 0), A.mult, col("fa", 0), A.add)
+    act(r("fx", 32, 64), C4096, F.Identity, bias=col("fa", 1), scale=col("nf", 1))
+    tr(r("fr", 0, 64), r("fx", 0, 64))
+    exchange("fr")
+    for h in range(2):
+        act(r("junk", 0, 256), r("fr", 0, 256), F.Sign, bias=col("fa", 2 + h), acc=col("ac", 4 + h))
+    ts(r("junk2", 0, 256), r("fr", 0, 256), col("cf", 17), A.is_ge)
+    red(col("lsum", 3), r("junk2", 0, 256))
+    ts(r("fa", 6, 8), r("nf", 0, 2), 1048576.0, A.mult)
+    tt(r("fa", 8, 10), r("fa", 6, 8), r("fa", 4, 6), A.add)
+    ts(r("cx2", 0, 32), CM128, col("ac", 4), A.mult, col("fa", 8), A.add)
+    act(r("cx2", 32, 64), CM128, F.Identity, bias=col("fa", 9), scale=col("ac", 5))
+    tr(r("cr2", 0, 64), r("cx2", 0, 64))
+    exchange("cr2")
+    ts(col("cf", 19), col("lsum", 3), -256.0, A.mult)
+    ts(r("lo", 3, 6), r("lo", 0, 3), col("cf", 19), A.add)
+    ts(col("lo", 6), col("lo", 5), -1.0, A.mult)
+    ts(r("lo", 11, 14), r("lo", 3, 6), 256.0, A.add)
+    act(r("junk", 0, 256), r("cr2", 0, 256), F.Relu, bias=col("lo", 6))
+    act(r("junk3", 0, 256), r("junk", 0, 256), F.Relu, bias=col("cf", 20), scale=-1.0, acc=col("lsum", 2))
+    ts(r("cf", 21, 23), r("lo", 3, 5), -255.0, A.mult, -32512.0, A.add)
+    ts(col("cf", 23), col("lo", 5), 33024.0, A.add)
+    for c in range(2):
+        ts(r("junk2", 0, 256), r("cr2", 0, 256), col("lo", 3 + c), A.max, col("lo", 11 + c), A.min)
+        red(col("lsum", c), r("junk2", 0, 256))
+    ts(col("cf", 24), col("lsum", 2), -1.0, A.mult, col("cf", 23), A.add)
+    ts(col("lst", 2), col("cf", 24), 255.0, A.min)
+    for c in range(2):
+        ts(col("lst", c), col("lsum", c), col("cf", 21 + c), A.add, 255.0, A.min)
+    send([(d, r("lst", 0, 3), r("rl", 3 * ((rank - d - 1) % 8), 3 * ((rank - d - 1) % 8) + 3)) for d in peers], "arl")
+    lands([r("rl", 0, 21)], "arl")
+
+    quant(r("qx", 0, 256), r("sx", 0, 256), r("xb", 0, 1024))
+    fill(r("ones", 0, 128), 1.0)
+    for i in range(4):
+        ts(r("ub", i, 512, 4), r("ones", 0, 128), col("u4", i), A.mult)
+    quant(r("qu", 0, 128), r("su", 0, 128), r("ub", 0, 512))
+    mm(r("pe", 0, 256), r("qu", 0, 128), r("su", 0, 128), r("qx", 0, 256), r("sx", 0, 256))
+    dma([("y", r("g0", 0, 256), r("qx", 0, 256)), ("y", r("h0", 0, 256), r("sx", 0, 256))])
+    dma([("y", r("ow", 0, 256), r("qx", 0, 256)), ("y", r("os_", 0, 256), r("sx", 0, 256))])
+
+    fill(CONE, 1.0)
+    ts(r("fi", 4, 6), r("fi", 0, 2), 8, A.arith_shift_right)
+    copy("v", r("fa", 10, 12), r("fi", 4, 6))
+    ts(r("fa", 12, 14), r("fa", 10, 12), -256.0, A.mult, 0.5, A.add)
+    for h in range(2):
+        act(r("junk", 0, 256), r("fr", 0, 256), F.Sign, bias=col("fa", 12 + h), acc=col("ac", 8 + h))
+    ts(r("fi", 6, 8), r("fi", 4, 6), float(7 - rank), A.add)
+    ts(r("fi", 8, 10), r("fi", 6, 8), 7, A.bitwise_and)
+    ts(r("fa", 14, 16), r("fi", 8, 10), float(LC), A.mult, float(FAR0), A.add)
+    for k in range(2):
+        ts(r("nl", k, 768, 3), r("nbf", k, 768, 3), -256.0 * rank, A.add)
+    tt(r("ac", 10, 12), r("ac", 8, 10), r("ac", 4, 6), A.subtract)
+    ts(r("ac", 12, 14), r("ac", 10, 12), 0.5, A.mult)
+    tt(r("ac", 14, 16), r("ac", 12, 14), r("fa", 14, 16), A.add)
+    ts(r("lx", 0, 32), CONE, col("ac", 14), A.mult)
+    act(r("lx", 32, 64), CONE, F.Copy, scale=col("ac", 15))
+    tr(r("fl", 0, 64), r("lx", 0, 64))
+    exchange("fl")
+    copy("s", r("nl", 2, 768, 3), r("fl", 0, 256))
+    copy("s", r("ea", 0, 256), r("pe", 0, 256))
+    fill(r("rl2", 0, 128), 0)
+
+    copy("v", r("rl2", 0, 21), r("rl", 0, 21))
+    tr(r("rl2", 32, 64), r("rl2", 0, 32))
+    o = 32 + 16 * (rank % 2)
+    copy("v", r("rl2", 64, 80), r("rl2", o, o + 16))
+    copy("v", r("rl2", 80, 96), r("rl2", o, o + 16))
+    tr(r("rl2", 96, 128), r("rl2", 64, 96))
+    for a in range(4):
+        copy("v", blk("rep", 0, 21, a), blk("rl2", 96, 117, rank // 2))
+    pick(r("slc", 0, 336), r("sls", 0, 336), r("qx", 0, 256), r("sx", 0, 256), r("rep", 0, 21))
+    for s, l, arr in (("slc", "g0", "ac0"), ("sls", "h0", "as0")):
+        mvs = []
+        for i, d in enumerate(peers):
+            q = FAR0 + LC * ((rank - d - 1) % 8)
+            mvs.append((d, r(s, LC * i, LC * i + LC), r(l, q, q + LC)))
+        send(mvs, arr)
+    lands([r("g0", FAR0, NEW0)], "ac0")
+    lands([r("h0", FAR0, NEW0)], "as0")
+    w0 = 32 * ((rank + 1) % 8)
+    iota(r("ndv", w0, 256), [[1, 256 - w0]], NEW0, 0)
+    if w0:
+        iota(r("ndv", 0, w0), [[1, w0]], NEW0 + 256 - w0, 0)
+    iota(r("np0", 0, 2048), [[0, 2048]], 0, 0)
+    iota(r("od", 0, 96), [[128, 3], [1, 32]], P, 0)
+
+    ts(col("cf", 25), col("cf", 1), 3.0, A.mult)
+    ts(r("dbt", 0, 12), r("dbf", 0, 12), col("cf", 25), A.add)
+    copy("v", r("db", 0, 192), (r("nl", 0, 768), r("dbt", 0, 12)))
+    tr(r("dt_", 0, 192), r("db", 0, 192))
+    copy("v", r("of", 0, 12), r("dt_", 0, 192, 16))
+    quant(r("qb", 0, 256), r("sb", 0, 256), r("bb_t", 0, 1024))
+    for i in range(4):
+        ts(r("vb", i, 512, 4), r("ones", 0, 128), col("v4", i), A.mult)
+    quant(r("qv", 0, 128), r("sv", 0, 128), r("vb", 0, 512))
+    mm(r("pf", 0, 256), r("qv", 0, 128), r("sv", 0, 128), r("qb", 0, 256), r("sb", 0, 256))
+    copy("s", r("fn", 0, 256), r("pf", 0, 256))
+    ts(col("cf", 27), col("cf", 26), col("cf", 2), A.add)
+    ts(r("frt", 0, 4), r("iot", 0, 64, 16), col("cf", 27), A.add)
+    copy("s", r("za", 0, 64), (r("ea", 0, 256), r("of", 0, 4)))
+    tt(r("zb", 0, 64), (r("ea", 0, 256), r("of", 4, 8)), r("za", 0, 64), A.add)
+    copy("s", r("fz", 0, 64), (r("fn", 0, 256), r("frt", 0, 4)))
+    fill(C1024, 1024.0)
+    fill(col("cf", 35), 1024.0)
+    fill(r("cf", 32, 35), 0.0)
+    fill(r("cf", 32, 33, 1, 96, 128), -TINY)
+    fill(r("cf", 33, 34, 1, 64, 128), -TINY)
+    fill(r("cf", 34, 35, 1, 64, 128), -TINY)
+    fill(r("cf", 34, 35, 1, 32, 64), -TINY)
+    ts(col("cf", 3), col("cf", 1), 1024.0, A.mult)
+    ts(col("cf", 4), col("cf", 3), 1024.0, A.add)
+    ts(col("cf", 12), col("cf", 1), 1.0, A.add, -float(KC), A.mult)
+    ts(r("cf", 15, 17), r("jo", 0, 2), 3.0, A.mult)
+    ts(r("jj", 0, 64), r("jr", 0, 64), col("jo", 0), A.is_lt, -TINY, A.mult)
+    ts(r("jj", 64, 128), r("jr", 0, 64), col("jo", 1), A.is_lt, TINY, A.mult)
+    ts(col("cf", 28), col("cf", 26), -3.0, A.mult, col("cf", 12), A.add)
+    ts(r("soc", 0, 6), r("soc", 0, 6), col("cf", 28), A.add)
+    ts(col("cf", 5), col("cf", 2), 1024.0, A.mult)
+    ts(col("cf", 6), col("cf", 5), 1024.0, A.add)
+    ts(col("cf", 7), col("cf", 5), -1.0, A.mult, -16384.0, A.add)
+    ts(col("cf", 13), col("cf", 2), 1.0, A.add, -float(KC), A.mult)
+    ts(col("cf", 14), col("cf", 2), 17.0, A.add, 1024.0, A.mult)
+    copy("s", r("nl", 768, 1536), r("nl", 0, 768))
+    copy("s", r("ol", 0, 256), r("iot", 0, 256))
+    ts(r("c4q", 0, 4), r("iot", 0, 4), 0.25, A.mult)
+    fill(r("xt", 0, 512), 0.0)
+    quant(r("qa", 0, 512), r("sa", 0, 512), r("at", 0, 2048))
+    for t in range(3):
+        quant(r("nq%d" % t, 0, 128), r("ns%d" % t, 0, 128), r("xb", 0, 512))
+    for k in range(3):
+        tr(r("dt_", 64 * k, 64 * k + 64), r("nbf", k, 192, 3))
+    copy("v", r("dnb", 0, 12), r("dt_", 0, 192, 16))
+
+    def places(t):
+        copy("v", r("ndl", 0, 2), r("ndf", 0, 2))
+        scatter(r("ol", 0, 256), r("ndl", 0, 2), r("od", 32 * t, 32 * t + 32))
+
+    def q32(i, b):
+        return r("sc4", 128 * i + 32 * b, 128 * i + 32 * b + 32)
+
+    for t in range(R):
+        gq, gs, W, oz = "g%d" % t, "h%d" % t, NEW0 + 256 * t, 12 * t
+        e0, e1 = (W - 256, W) if t else (FAR0, NEW0)
+        em = (e0 + e1) // 2
+        mm(r("pe", 0, em - e0), r("qu", 0, 128), r("su", 0, 128), r(gq, e0, em), r(gs, e0, em))
+        mm(r("pf", 0, e1 - em), r("qu", 0, 128), r("su", 0, 128), r(gq, em, e1), r(gs, em, e1))
+        copy("v", r("ea", e0, em), r("pe", 0, em - e0))
+        copy("s", r("ea", em, e1), r("pf", 0, e1 - em))
+        if t:
+            copy("s", r("za", 0, 64), (r("ea", 0, W), r("of", oz, oz + 4)))
+            tt(r("zb", 0, 64), (r("ea", 0, W), r("of", oz + 4, oz + 8)), r("za", 0, 64), A.add)
+        tt(r("zc", 0, 64), (r("ea", 0, W), r("of", oz + 8, oz + 12)), r("zb", 0, 64), A.add)
+        tt(r("zd", 0, 64), r("zc", 0, 64), r("fz", 0, 64), A.subtract)
+        act(r("z", 0, 64), r("zd", 0, 64), F.Abs)
+        exchange("z")
+        tr(r("zt", 0, 64), r("z", 0, 64))
+        ts(r("dd", 0, 64), r("z", 0, 64), col("zt", 0), A.subtract)
+        act(r("dd", 64, 128), r("z", 0, 64), F.Identity, bias=col("zt", 32), scale=-1.0)
+        for h in range(2):
+            o = 256 * h
+            for d in range(1, 4):
+                ts(r("mm_", o + 64 * d, o + 64 * d + 64), r("z", 64 * d, 64 * d + 64), col("zt", 32 * h), A.subtract, col("cf", 31 + d), A.is_gt)
+            tt(r("mm_", o, o + 64), r("dd", 64 * h, 64 * h + 64), r("jj", 64 * h, 64 * h + 64), A.is_lt if h else A.is_gt)
+            if h == 0:
+                act(r("junk3", 0, 256), r("mm_", 0, 256), F.Copy, acc=col("rk", 0))
+                act(r("cx", 0, 32), C1024, F.Identity, bias=col("cf", 15), scale=col("rk", 0))
+        red(col("rk", 1), r("mm_", 256, 512))
+        ts(r("cx", 32, 64), C1024, col("rk", 1), A.mult, col("cf", 16), A.add)
+        tr(r("cr", 0, 64), r("cx", 0, 64))
+        ts(r("cl", 0, 64), r("cr", 0, 64), col("cf", 3), A.max, col("cf", 4), A.min)
+        act(r("cl", 128, 192), r("cr", 0, 64), F.Relu, bias=col("cf", 7))
+        ts(r("cl", 64, 128), r("cr", 0, 64), col("cf", 5), A.max, col("cf", 6), A.min)
+        act(r("cl", 192, 256), r("cl", 128, 192), F.Relu, bias=col("cf", 35), scale=-1.0, acc=col("sw_", 2))
+        red(col("sw_", 0), r("cl", 0, 64))
+        red(col("sw_", 1), r("cl", 64, 128))
+        exchange("sw_", 3)
+        red(col("sel", 0), r("sw_", 0, 12, 3))
+        ts(r("so", 0, 6), r("soc", 0, 6), col("sel", 0), A.add)
+        copy("v", r("ng", 0, 96), (r("nl", 0, 1536), r("so", 0, 6)))
+        tr(r("nt", 0, 96), r("ng", 0, 96))
+        copy("v", r("po", 0, 6), r("nt", 0, 96, 16))
+        nq, ns = "nq%d" % t, "ns%d" % t
+        pick(r(nq, 0, 96), r(ns, 0, 96), r(gq, 0, W), r(gs, 0, W), r("po", 0, 6))
+        for b in range(4):
+            mm(r("ps", 512 * b, 512 * b + 128), r("qa", 128 * b, 128 * b + 128), r("sa", 128 * b, 128 * b + 128), r(nq, 0, 128), r(ns, 0, 128))
+        red(col("sel", 1), r("sw_", 1, 12, 3))
+        red(col("sel", 2), r("sw_", 2, 12, 3))
+        ts(col("ndf", 0), col("sel", 1), col("cf", 13), A.add, THIRD, A.mult)
+        ts(col("ndf", 1), col("sel", 2), col("cf", 14), A.subtract, -THIRD, A.mult)
+        if t < 2:
+            nd, na = r("ndg", 2 * t, 2 * t + 2), "nda%d" % t
+            ts(nd, r("ndf", 0, 2), 256.0 * rank, A.add)
+            send([(d, nd, r(na, 2 * rank, 2 * rank + 2)) for d in peers], "an%d" % t)
+            lands([r(na, 2 * s, 2 * s + 2) for s in peers], "an%d" % t)
+            dma([("y", r(na, 2 * rank, 2 * rank + 2), nd)])
+        for c in range(2):
+            ts(r("bo", c, 8, 2), r("c4q", 0, 4), col("ndf", c), A.add, 4.0, A.mult)
+        for b in range(4):
+            copy("s", q32(0, b), r("ps", 512 * b, 512 * b + 32))
+        for k, b in ((1, 0), (1, 1), (2, 0), (1, 2), (2, 1), (1, 3), (2, 2), (2, 3)):
+            tt(q32(k, b), q32(k - 1, b), r("ps", 512 * b + 32 * k, 512 * b + 32 * k + 32), A.add)
+        if t == 2:
+            places(t)
+        copy("s", r("bbs", 0, 128), (r("bb_t", 0, 1024), r("bo", 0, 8)))
+        for b in range(4):
+            act(q32(3, b), q32(2, b), F.Copy, scale=C05)
+            tt(r("xt", b, 128, 4), q32(3, b), r("bbs", 32 * b, 32 * b + 32), A.add)
+        if t == 2:
+            copy("s", r("og", 0, 256), (r("ol", 0, 256), r("d8", 0, 16)))
+        o0 = P + 128 * t
+        if t < 2:
+            nq, ns, at = "g%d" % (t + 1), "h%d" % (t + 1), W + 224
+            quant(r(nq, at, at + 128), r(ns, at, at + 128), r("xt", 0, 512))
+            for n, arr in ((nq, "ac%d" % (t + 1)), (ns, "as%d" % (t + 1))):
+                mvs = []
+                for d in peers:
+                    q = W + 32 * ((rank - d - 1) % 8)
+                    mvs.append((d, r(n, at, at + 32), r(n, q, q + 32)))
+                send(mvs, arr)
+                lands([r(n, W, at)], arr)
+        quant(r("ow", o0, o0 + 128), r("os_", o0, o0 + 128), r("xt", 0, 512))
+        if t == 0:
+            iota(r("np1", 0, 2048), [[0, 2048]], 0, 0)
+            dma([("y", r("g1", 0, NEW0), r("g0", 0, NEW0)), ("y", r("h1", 0, NEW0), r("h0", 0, NEW0))])
+            dma([("y", r("g2", 0, NEW0), r("g0", 0, NEW0)), ("y", r("h2", 0, NEW0), r("h0", 0, NEW0))])
+            ts(r("ndv", 256, 512), r("ndv", 0, 256), 256.0, A.add)
+        ts(col("ndo", t), col("sel", 0), col("cf", 12), A.add, THIRD, A.mult)
+        dma([("y", T.nd[t:t + 1, 0:32], r("ndo", t, t + 1, 1, 0, 32))])
+        if t < 2:
+            places(t)
+        if t == 1:
+            dma([("y", r("g2", NEW0, NEW0 + 256), r("g1", NEW0, NEW0 + 256)), ("y", r("h2", NEW0, NEW0 + 256), r("h1", NEW0, NEW0 + 256))])
+            quant(r("qw", 0, 128), r("sw", 0, 128), r("wt", 0, 512))
+            ts(r("frf", 0, 16), r("iot", 0, 256, 16), 0.0, A.add)
+            ts(r("frf", 0, 16), r("frf", 0, 16), 224, A.bitwise_and)
+            ts(r("d8", 0, 16), r("frf", 0, 16), col("cf", 1), A.add)
+        if t < 2:
+            npn = r("np%d" % t, 0, 2048)
+            scatter(npn, r(na, 0, 16), r("ndv", 256 * t, 256 * t + 256))
+            tt(r("db", 0, 192), (npn, r("dnb", 0, 12)), r("db", 0, 192), A.max)
+            tr(r("dt_", 0, 192), r("db", 0, 192))
+            copy("v", r("of", 12 * t + 12, 12 * t + 24), r("dt_", 0, 192, 16))
+            tt(r("nl", 0, 768), (npn, r("nbt", 0, 48)), r("nl", 0, 768), A.max)
+            copy("s", r("nl", 768, 1536), r("nl", 0, 768))
+
+    tr(r("ogt", 0, 256), r("og", 0, 256))
+    copy("v", r("oo", 0, 16), r("ogt", 0, 256, 16))
+    pick(r("occ", 0, 256), r("ocs", 0, 256), r("ow", 0, 640), r("os_", 0, 640), r("oo", 0, 16))
+    dma([("y", T.oc[:], r("occ", 0, 256))])
+    dma([("y", T.osc[4 * k:4 * k + 4, :], r("ocs", 0, 256, 1, 32 * k, 32 * k + 4)) for k in range(4)])
+    for h, ps in ((0, "pe"), (1, "pf")):
+        mm(r(ps, 0, 128), r("qw", 0, 128), r("sw", 0, 128), r("occ", 128 * h, 128 * h + 128), r("ocs", 128 * h, 128 * h + 128))
+    copy("v", r("yt", 0, 128), r("pe", 0, 128))
+    copy("s", r("yt", 128, 256), r("pf", 0, 128))
+    dma([("s", T.y[:], r("yt", 0, 256))])
+    for sem, c in cnt.items():
+        if known["g"].get(sem, 0) < c:
+            g.wait_ge(T.sem[sem], c)

@@ -10,6 +10,7 @@ NEW0 = P + 7 * LC
 C05 = 13421773 * 2.0 ** -28
 THIRD = float(np.float32(1.0) / np.float32(3.0))
 KC = 1024 * 255
+WAKE, SLACK = 0.15, 0.3
 TINY = 2.0 ** -110
 CODE, U8, BF, F32, I32, U16 = "float8_e4m3fn_x4", "uint8", "bfloat16", "float32", "int32", "uint16"
 
@@ -19,12 +20,12 @@ def _sbuf(dtype, **cols):
 
 
 SCRATCH = {"pe": ("psum", [128, 512], F32), "pf": ("psum", [128, 512], F32), "ps": ("psum", [128, 2048], F32)}
-SCRATCH.update(_sbuf(F32, nbf=768, iot=2048, jr=256, cf=64, jo=2, ka0=256, ka=256, kat=64, bi=4, junk=256, junk2=256, junk3=256, ac=16, fa=16, nf=2,
+SCRATCH.update(_sbuf(F32, nbf=768, iot=2048, jr=256, cf=64, jo=2, ka0=256, ka=256, kat=64, bi=4, junk=2560, junk2=256, junk3=256, ac=16, fa=16, nf=2,
                      fx=64, fr=256, cx2=64, cr2=256, cc=128, lo=16, lsum=4, ea=1104, fn=256, fz=64, za=64, zb=64, zc=64, zd=64, z=256, zt=64, dd=128, jj=128, rk=4,
-                     cx=64, cr=64, cl=256, sw_=12, sel=4, soc=6, ng=96, nt=96, ndf=2, c4q=4, bbs=128, sc4=512, ndo=4,
+                     cx=64, cr=64, cl=256, sw_=12, sel=16, soc=6, ng=96, nt=96, ndf=2, c4q=4, bbs=128, sc4=512, ndo=4, ndg=4, nda0=16, nda1=16,
                      np0=2048, np1=2048, ndv=512, nl=1536, db=192, dt_=192, dbf=12, fl=256, lx=64, ol=256, od=96, og=256, ogt=256, yt=256))
 SCRATCH.update(_sbuf(I32, nb32=48, ci=16, fi=16, frf=256))
-SCRATCH.update(_sbuf(U16, nbt=48, lst=4, rl=24, rl2=128, rep=24, so=6, po=6, ndg=4, ndl=2, nda0=16, nda1=16, bo=8, dbt=12, dnb=12, of=36, frt=4, d8=16, oo=16))
+SCRATCH.update(_sbuf(U16, nbt=48, lst=4, rl=24, rl2=128, rep=24, so=6, po=6, ndl=2, nai=16, bo=8, dbt=12, dnb=12, of=36, frt=4, d8=16, oo=16))
 SCRATCH.update(_sbuf(BF, xb=1024, bb_t=1024, at=2048, wt=512, u4=4, v4=4, ones=128, ub=512, vb=512, mm_=512, xt=512))
 for _c, _s, _n in (("qx", "sx", 256), ("qb", "sb", 256), ("qu", "su", 128), ("qv", "sv", 128), ("qa", "sa", 512), ("qw", "sw", 128), ("slc", "sls", 336),
                    ("g0", "h0", 592), ("g1", "h1", 944), ("g2", "h2", 1200), ("nq0", "ns0", 128), ("nq1", "ns1", 128), ("nq2", "ns2", 128),
@@ -43,7 +44,7 @@ def rank_program(g, core, T, topo):
         return
     eng = {"v": g.vector, "s": g.scalar, "t": g.tensor, "g": g, "y": g.sync}
     csem = {"v": "cv", "s": "cs", "t": "ct", "g": "cg"}
-    cnt, known, log, pool, snaps = {}, {q: {} for q in eng}, {}, [0], {}
+    cnt, known, log, pool, snaps, ops = {}, {q: {} for q in eng}, {}, [0], {}, []
 
     def ap(x):
         return T[x[0]][x[4]:x[5], x[1]:x[2]:x[3]] if x[3] != 1 else T[x[0]][x[4]:x[5], x[1]:x[2]]
@@ -65,36 +66,101 @@ def rank_program(g, core, T, topo):
     def clash(a, b):
         return not (a[3] == b[3] and a[3] > 1 and (a[1] - b[1]) % a[3])
 
-    def order(q, reads, writes, need=None):
-        need = need or {}
+    def meets(reads, writes, q):
+        deps = set()
         for x, w in [(x, 0) for x in reads] + [(x, 1) for x in writes]:
             s = span(x)
             bank = SCRATCH[x[0]][0] == "psum"
-            for y, t, w2, tok, q2 in log.get(x[0], []):
+            for y, t, w2, i, q2 in log.get(x[0], []):
                 if (w or w2 or (bank and q2 != q)) and s[0] < t[1] and t[0] < s[1] and s[2] < t[3] and t[2] < s[3] and clash(x, y):
-                    need[tok[0]] = max(need.get(tok[0], 0), tok[1])
-        for sem, c in sorted(need.items(), key=lambda i: -sum(snaps.get(i, {}).values())):
-            if known[q].get(sem, 0) < c:
-                eng[q].wait_ge(T.sem[sem], c)
-                learn(q, (sem, c))
+                    deps.add(i)
+        return deps
 
-    def note(q, reads, writes, tok):
+    def note(q, reads, writes, i):
         for x in writes:
             s = span(x)
             if x[3] == 1:
                 log[x[0]] = [e for e in log.get(x[0], []) if not (s[0] <= e[1][0] and e[1][1] <= s[1] and s[2] <= e[1][2] and e[1][3] <= s[3])]
-            log.setdefault(x[0], []).append((x, s, 1, tok, q))
+            log.setdefault(x[0], []).append((x, s, 1, i, q))
         for x in reads:
-            log.setdefault(x[0], []).append((x, span(x), 0, tok, q))
+            log.setdefault(x[0], []).append((x, span(x), 0, i, q))
 
-    def emit(q, fn, reads, writes):
-        sem = csem[q]
-        order(q, reads, writes, {sem: cnt[sem]} if q == "g" and sem in cnt else None)
-        cnt[sem] = cnt.get(sem, 0) + 1
-        tok = (sem, cnt[sem])
-        snaps[tok] = dict(known[q])
-        fn().then_inc(T.sem[sem], 1)
-        note(q, reads, writes, tok)
+    def put(q, fn, reads, writes, cost, late=0.0, sem=None, inc=1, deps=()):
+        i = len(ops)
+        ops.append({"q": q, "fn": fn, "deps": meets(reads, writes, q) | set(deps), "cost": cost, "late": late, "sem": sem, "inc": inc, "users": [], "peers": [i]})
+        note(q, reads, writes, i)
+        return i
+
+    def emit(q, fn, reads, writes, cycles, fixed=0.0):
+        put(q, fn, reads, writes, fixed + max(64, cycles) * 0.001)
+
+    def width(x):
+        return -(-(x[2] - x[1]) // x[3])
+
+    def flush():
+        for i, o in enumerate(ops):
+            for k in list(o["deps"]):
+                o["deps"] |= set(ops[k]["peers"])
+            o["deps"].discard(i)
+            for k in o["deps"]:
+                ops[k]["users"].append(i)
+        for o in reversed(ops):
+            o["rank"] = o["cost"] + o["late"] + max([WAKE + ops[k]["rank"] for k in o["users"]] or [0])
+        left = [len(o["deps"]) for o in ops]
+        ready = {q: [] for q in "vstgyr"}
+        clock = {q: 0.0 for q in ready}
+        for i, o in enumerate(ops):
+            o["est"] = 0.0
+            if not left[i]:
+                ready[o["q"]].append(i)
+        out = []
+        while any(ready.values()):
+            best = None
+            for q, l in ready.items():
+                if not l:
+                    continue
+                est = {i: max(clock[q], ops[i]["est"]) for i in l}
+                t0 = min(est.values())
+                c = max([i for i in l if est[i] <= t0 + 0.001], key=lambda i: ops[i]["rank"])
+                for i in l:
+                    if est[i] < t0 + ops[c]["cost"] and ops[i]["rank"] > ops[c]["rank"] + SLACK:
+                        c = i
+                if best is None or est[c] < best[0]:
+                    best = (est[c], c)
+            t, i = best
+            o = ops[i]
+            ready[o["q"]].remove(i)
+            clock[o["q"]] = t + o["cost"]
+            out.append(i)
+            for k in o["users"]:
+                left[k] -= 1
+                ops[k]["est"] = max(ops[k]["est"], t + o["cost"] + o["late"] + WAKE)
+                if not left[k]:
+                    ready[ops[k]["q"]].append(k)
+        tok = {}
+        for i in out:
+            o = ops[i]
+            q = o["q"]
+            need = {}
+            if q == "g" and o["sem"] is None and "cg" in cnt:
+                need["cg"] = cnt["cg"]
+            for k in o["deps"]:
+                need[tok[k][0]] = max(need.get(tok[k][0], 0), tok[k][1])
+            if q != "r":
+                for sem, c in sorted(need.items(), key=lambda e: -sum(snaps.get(e, {}).values())):
+                    if known[q].get(sem, 0) < c:
+                        eng[q].wait_ge(T.sem[sem], c)
+                        learn(q, (sem, c))
+            sem = o["sem"] or csem[q]
+            cnt[sem] = cnt.get(sem, 0) + 1 if o["sem"] is None else o["inc"]
+            tok[i] = (sem, cnt[sem])
+            if q != "r":
+                s = snaps.setdefault(tok[i], {})
+                for n, m in known[q].items():
+                    s[n] = max(s.get(n, 0), m)
+                c = o["fn"]()
+                if o["sem"] is None:
+                    c.then_inc(T.sem[sem], 1)
 
     def newsem():
         pool[0] += 1
@@ -110,83 +176,85 @@ def rank_program(g, core, T, topo):
 
     def copy(q, out, in_):
         i, rd = src(in_)
+        n = width(out) * (1.5 if len(in_) == 2 else 1)
         if q == "v":
-            emit(q, lambda: g.vector.tensor_copy(ap(out), i), rd, [out])
+            emit(q, lambda: g.vector.tensor_copy(ap(out), i), rd, [out], n)
         else:
-            emit(q, lambda: g.scalar.activation(ap(out), i, F.Copy), rd, [out])
+            emit(q, lambda: g.scalar.activation(ap(out), i, F.Copy), rd, [out], n)
 
     def scatter(win, off, in_):
-        emit("v", lambda: g.vector.tensor_copy(ap(win).indirect(ap(off)), ap(in_)), [in_, off], [win])
+        emit("v", lambda: g.vector.tensor_copy(ap(win).indirect(ap(off)), ap(in_)), [in_, off], [win], 3 * width(in_))
 
     def act(out, in_, func, bias=0.0, scale=1.0, acc=None):
         i, rd = src(in_)
         b, rb = sc(bias)
         s, rs = sc(scale)
         if acc is None:
-            emit("s", lambda: g.scalar.activation(ap(out), i, func, bias=b, scale=s), rd + rb + rs, [out])
+            emit("s", lambda: g.scalar.activation(ap(out), i, func, bias=b, scale=s), rd + rb + rs, [out], width(out))
         else:
-            emit("s", lambda: g.scalar.activation(ap(out), i, func, bias=b, scale=s, accum_out=ap(acc)), rd + rb + rs, [out, acc])
+            emit("s", lambda: g.scalar.activation(ap(out), i, func, bias=b, scale=s, accum_out=ap(acc)), rd + rb + rs, [out, acc], width(out))
 
     def ts(out, in_, s1, op0, s2=None, op1=None):
         i, rd = src(in_)
         a, ra = sc(s1)
         b, rb = sc(s2)
         if op1 is None:
-            emit("v", lambda: g.vector.tensor_scalar(ap(out), i, a, None, op0), rd + ra, [out])
+            emit("v", lambda: g.vector.tensor_scalar(ap(out), i, a, None, op0), rd + ra, [out], width(out))
         else:
-            emit("v", lambda: g.vector.tensor_scalar(ap(out), i, a, b, op0, op1), rd + ra + rb, [out])
+            emit("v", lambda: g.vector.tensor_scalar(ap(out), i, a, b, op0, op1), rd + ra + rb, [out], width(out))
 
     def tt(out, in0, in1, op):
         i, rd = src(in0)
-        emit("v", lambda: g.vector.tensor_tensor(ap(out), i, ap(in1), op), rd + [in1], [out])
+        emit("v", lambda: g.vector.tensor_tensor(ap(out), i, ap(in1), op), rd + [in1], [out], 2 * width(out))
 
     def red(out, in_):
-        emit("v", lambda: g.vector.tensor_reduce(ap(out), ap(in_), AxisListType.X, A.add), [in_], [out])
+        emit("v", lambda: g.vector.tensor_reduce(ap(out), ap(in_), AxisListType.X, A.add), [in_], [out], width(in_))
+
+    def least(out, in_):
+        emit("v", lambda: g.vector.tensor_reduce(ap(out), ap(in_), AxisListType.X, A.min, apply_absolute_value=True), [in_], [out], width(in_))
 
     def tr(out, in_):
-        emit("v", lambda: g.vector.transpose(ap(out), ap(in_)), [in_], [out])
+        emit("v", lambda: g.vector.transpose(ap(out), ap(in_)), [in_], [out], width(out))
 
     def fill(out, val):
-        emit("v", lambda: g.vector.memset(ap(out), val), [], [out])
+        emit("v", lambda: g.vector.memset(ap(out), val), [], [out], width(out))
 
     def quant(q, s, in_):
-        emit("v", lambda: g.vector.quantize_mx(ap(q), ap(s), ap(in_)), [in_], [q, s])
+        emit("v", lambda: g.vector.quantize_mx(ap(q), ap(s), ap(in_)), [in_], [q, s], width(in_) // 4)
 
     def mm(out, wq, ws, xq, xs):
-        emit("t", lambda: g.tensor.matmul_mx(ap(out), ap(wq), ap(ws), ap(xq), ap(xs), True, True), [wq, ws, xq, xs], [out])
+        emit("t", lambda: g.tensor.matmul_mx(ap(out), ap(wq), ap(ws), ap(xq), ap(xs), True, True), [wq, ws, xq, xs], [out], width(out))
 
     def iota(out, pattern, base, cm, flag=True):
         if flag:
-            emit("g", lambda: g.iota(ap(out), pattern, base, cm, allow_small_or_imprecise_dtypes=True), [], [out])
+            emit("g", lambda: g.iota(ap(out), pattern, base, cm, allow_small_or_imprecise_dtypes=True), [], [out], 2 * width(out), 0.13)
         else:
-            emit("g", lambda: g.iota(ap(out), pattern, base, cm), [], [out])
+            emit("g", lambda: g.iota(ap(out), pattern, base, cm), [], [out], 2 * width(out), 0.13)
 
     def pick(qo, so, win, wins, off):
-        emit("v", lambda: g.vector.tensor_copy(ap(qo).bitcast(dt.uint32), ap(win).bitcast(dt.uint32).indirect(ap(off))), [win, off], [qo])
-        emit("s", lambda: g.scalar.activation(ap(so), ap(wins).indirect(ap(off)), F.Copy), [wins, off], [so])
+        emit("v", lambda: g.vector.tensor_copy(ap(qo).bitcast(dt.uint32), ap(win).bitcast(dt.uint32).indirect(ap(off))), [win, off], [qo], 1.5 * width(qo))
+        emit("s", lambda: g.scalar.activation(ap(so), ap(wins).indirect(ap(off)), F.Copy), [wins, off], [so], 1.5 * width(so))
 
     def side(x):
         return ap(x).bitcast(dt.uint8) if SCRATCH[x[0]][2] == CODE else ap(x)
 
     def dma(moves):
         sem = newsem()
-        done, sn = [], {}
+        made = []
         for q, out, in_ in moves:
             wr = [out] if isinstance(out, tuple) else []
             rd = [in_] if isinstance(in_, tuple) else []
-            order(q, rd, wr)
-            eng[q].dma_start(side(out) if wr else out, side(in_) if rd else in_).then_inc(T.sem[sem], 16)
-            done.append((q, rd, wr))
-        cnt[sem] = 16 * len(moves)
-        tok = (sem, cnt[sem])
-        for q, rd, wr in done:
-            for n, m in known[q].items():
-                sn[n] = max(sn.get(n, 0), m)
-        snaps[tok] = sn
-        for q, rd, wr in done:
-            note(q, rd, wr, tok)
+            o, i = side(out) if wr else out, side(in_) if rd else in_
+            made.append(put(q, lambda q=q, o=o, i=i: eng[q].dma_start(o, i).then_inc(T.sem[sem], 16), rd, wr, 0.07, 2.2, sem, 16 * len(moves)))
+        for k in made:
+            ops[k]["peers"] = made
 
     peers = [(rank + 1 + i) % 8 for i in range(7)]
+    ids = {}
+    for d in peers:
+        rid, pid, _ = topo.addr(T.cores[d])
+        ids[d] = DstId(rid=rid, pnc=pid)
+    full = topo.engines(core, T.cores[peers[0]])
     across = [d for d in peers if topo.die(T.cores[d]) != topo.die(core)]
     masks = {}
     for d in peers:
@@ -195,21 +263,19 @@ def rank_program(g, core, T, topo):
         k = (across if d in across else [s for s in peers if s not in across]).index(d)
         masks[d] = sum(1 << x for x in lane[2 * k:2 * k + 2])
 
-    def send(moves, arr):
+    def issue(trs, reads, total):
         sem = newsem()
-        order("g", [m[1] for m in moves], [])
-        trs = []
-        for d, s, l in moves:
-            rid, pid, _ = topo.addr(T.cores[d])
-            trs.append(RemoteDMATransfer(dst_ids=[DstId(rid=rid, pnc=pid)], dma_engine_mask=masks[d], remote_sem=T.sem[arr], srcs=[side(s)], dsts=[side(l)]))
-        g.remote_dma_fused(trs, local_sem=T.sem[sem])
-        cnt[sem] = 2 * len(moves)
-        snaps[(sem, cnt[sem])] = dict(known["g"])
-        note("g", [m[1] for m in moves], [], (sem, cnt[sem]))
+        return put("g", lambda: g.remote_dma_fused(trs, local_sem=T.sem[sem]), reads, [], 1.0, 0.7, sem, total)
 
-    def lands(regions, arr):
-        cnt[arr] = 14
-        note("r", [], regions, (arr, 14))
+    def send_each(moves, arr, regions):
+        i = issue([RemoteDMATransfer(dst_ids=[ids[d]], dma_engine_mask=masks[d], remote_sem=T.sem[arr], srcs=[side(s)], dsts=[side(l)]) for d, s, l in moves],
+                  [m[1] for m in moves], 2 * len(moves))
+        put("r", None, [], regions, 0.0, 1.0, arr, 2 * 7, [i])
+
+    def send_all(s, land, arr, regions):
+        i = issue([RemoteDMATransfer(dst_ids=[ids[d] for d in peers], dma_engine_mask=sum(1 << x for x in full), remote_sem=T.sem[arr], srcs=[side(s)],
+                                     dsts=[side(land(d)) for d in peers])], [s], len(full))
+        put("r", None, [], regions, 0.0, 0.7, arr, len(full) * 7, [i])
 
     def exchange(n, w=64):
         for a in range(4):
@@ -223,6 +289,9 @@ def rank_program(g, core, T, topo):
 
     def blk(n, c0, c1, a):
         return r(n, c0, c1, 1, 32 * a, 32 * a + 32)
+
+    def junk(i):
+        return r("junk", 256 * i, 256 * i + 256)
 
     mv = []
     for gr in range(8):
@@ -263,54 +332,59 @@ def rank_program(g, core, T, topo):
     C4096, CM128, C1024, CONE = r("cc", 0, 32), r("cc", 32, 64), r("cc", 64, 96), r("cc", 96, 128)
     fill(C4096, 4096.0)
     fill(CM128, -128.0)
-    act(r("ka0", 0, 256), r("nbf", 2, 768, 3), F.Copy, scale=256.0)
+    act(r("ka0", 0, 256), r("nbf", 2, 768, 3), F.Copy, scale=512.0)
     tt(r("ka", 0, 256), r("ka0", 0, 256), r("jr", 0, 256), A.add)
     tr(r("kat", 0, 64), r("ka", 0, 64))
-    ts(r("bi", 0, 2), r("kat", 0, 64, 32), -1.0, A.mult, 0.5, A.add)
-    tt(r("bi", 2, 4), r("bi", 0, 2), r("jo", 0, 2), A.add)
-    for i in range(4):
-        act(r("junk", 0, 256), r("ka", 0, 256), F.Sign, bias=col("bi", i), acc=col("ac", i))
-    ts(r("fa", 0, 2), r("bi", 2, 4), 0.5, A.subtract, -1.0 / 256, A.mult)
-    ts(r("fa", 2, 4), r("fa", 0, 2), -1.0, A.mult, 0.5, A.add)
+    tt(r("bi", 0, 2), r("jo", 0, 2), r("kat", 0, 64, 32), A.subtract)
+    act(junk(0), r("ka", 0, 256), F.Identity, bias=col("bi", 0))
+    act(r("junk3", 0, 256), r("ka", 0, 256), F.Identity, bias=col("bi", 1))
+    ts(r("fa", 0, 2), r("bi", 0, 2), -1.0 / 512, A.mult)
+    ts(r("fa", 2, 4), r("bi", 0, 2), 1.0 / 512, A.mult, 0.5, A.add)
+    least(col("ac", 0), junk(0))
     copy("v", r("fi", 0, 2), r("fa", 0, 2))
+    least(col("ac", 1), r("junk3", 0, 256))
     ts(r("fi", 2, 4), r("fi", 0, 2), 255, A.bitwise_and)
+    tt(r("nf", 0, 2), r("ac", 0, 2), r("jo", 0, 2), A.not_equal)
     copy("v", r("fa", 4, 6), r("fi", 2, 4))
-    ts(col("cf", 17), col("cf", 0), col("cf", 2), A.subtract, 16.0, A.mult)
-    ts(col("cf", 18), col("cf", 2), 256.0, A.mult)
-    ts(r("lo", 0, 3), r("lo", 8, 11), col("cf", 18), A.add, 32768.0, A.add)
-    fill(col("cf", 20), 256.0)
-    tt(r("nf", 0, 2), r("ac", 0, 2), r("ac", 2, 4), A.not_equal)
     ts(r("fx", 0, 32), C4096, col("nf", 0), A.mult, col("fa", 0), A.add)
     act(r("fx", 32, 64), C4096, F.Identity, bias=col("fa", 1), scale=col("nf", 1))
+    ts(col("cf", 17), col("cf", 0), col("cf", 2), A.subtract, 16.0, A.mult)
     tr(r("fr", 0, 64), r("fx", 0, 64))
     exchange("fr")
     for h in range(2):
-        act(r("junk", 0, 256), r("fr", 0, 256), F.Sign, bias=col("fa", 2 + h), acc=col("ac", 4 + h))
+        act(junk(1 + h), r("fr", 0, 256), F.Sign, bias=col("fa", 2 + h), acc=col("ac", 4 + h))
     ts(r("junk2", 0, 256), r("fr", 0, 256), col("cf", 17), A.is_ge)
-    red(col("lsum", 3), r("junk2", 0, 256))
     ts(r("fa", 6, 8), r("nf", 0, 2), 1048576.0, A.mult)
+    red(col("lsum", 3), r("junk2", 0, 256))
     tt(r("fa", 8, 10), r("fa", 6, 8), r("fa", 4, 6), A.add)
     ts(r("cx2", 0, 32), CM128, col("ac", 4), A.mult, col("fa", 8), A.add)
     act(r("cx2", 32, 64), CM128, F.Identity, bias=col("fa", 9), scale=col("ac", 5))
+    ts(col("cf", 18), col("cf", 2), 256.0, A.mult)
     tr(r("cr2", 0, 64), r("cx2", 0, 64))
+    ts(r("lo", 0, 3), r("lo", 8, 11), col("cf", 18), A.add, 32768.0, A.add)
     exchange("cr2")
     ts(col("cf", 19), col("lsum", 3), -256.0, A.mult)
+    fill(col("cf", 20), 256.0)
     ts(r("lo", 3, 6), r("lo", 0, 3), col("cf", 19), A.add)
     ts(col("lo", 6), col("lo", 5), -1.0, A.mult)
     ts(r("lo", 11, 14), r("lo", 3, 6), 256.0, A.add)
-    act(r("junk", 0, 256), r("cr2", 0, 256), F.Relu, bias=col("lo", 6))
-    act(r("junk3", 0, 256), r("junk", 0, 256), F.Relu, bias=col("cf", 20), scale=-1.0, acc=col("lsum", 2))
-    ts(r("cf", 21, 23), r("lo", 3, 5), -255.0, A.mult, -32512.0, A.add)
+    act(junk(0), r("cr2", 0, 256), F.Relu, bias=col("lo", 6))
     ts(col("cf", 23), col("lo", 5), 33024.0, A.add)
-    for c in range(2):
-        ts(r("junk2", 0, 256), r("cr2", 0, 256), col("lo", 3 + c), A.max, col("lo", 11 + c), A.min)
-        red(col("lsum", c), r("junk2", 0, 256))
-    ts(col("cf", 24), col("lsum", 2), -1.0, A.mult, col("cf", 23), A.add)
-    ts(col("lst", 2), col("cf", 24), 255.0, A.min)
+    ts(r("ka0", 0, 256), r("cr2", 0, 256), col("lo", 3), A.max, col("lo", 11), A.min)
+    ts(r("junk2", 0, 256), r("cr2", 0, 256), col("lo", 4), A.max, col("lo", 12), A.min)
+    act(junk(5), junk(0), F.Relu, bias=col("cf", 20), scale=-1.0, acc=col("lsum", 2))
+    act(junk(6), r("ka0", 0, 256), F.Copy, acc=col("lsum", 0))
+    act(col("cf", 24), col("lsum", 2), F.Identity, bias=col("cf", 23), scale=-1.0)
+    ts(r("cf", 21, 23), r("lo", 3, 5), -255.0, A.mult, -32512.0, A.add)
+    red(col("lsum", 1), r("junk2", 0, 256))
     for c in range(2):
         ts(col("lst", c), col("lsum", c), col("cf", 21 + c), A.add, 255.0, A.min)
-    send([(d, r("lst", 0, 3), r("rl", 3 * ((rank - d - 1) % 8), 3 * ((rank - d - 1) % 8) + 3)) for d in peers], "arl")
-    lands([r("rl", 0, 21)], "arl")
+    ts(col("lst", 2), col("cf", 24), 255.0, A.min)
+
+    def slot(d, w, base=0):
+        q = base + w * ((rank - d - 1) % 8)
+        return q, q + w
+    send_all(r("lst", 0, 3), lambda d: r("rl", *slot(d, 3)), "arl", [r("rl", 0, 21)])
 
     quant(r("qx", 0, 256), r("sx", 0, 256), r("xb", 0, 1024))
     fill(r("ones", 0, 128), 1.0)
@@ -326,7 +400,7 @@ def rank_program(g, core, T, topo):
     copy("v", r("fa", 10, 12), r("fi", 4, 6))
     ts(r("fa", 12, 14), r("fa", 10, 12), -256.0, A.mult, 0.5, A.add)
     for h in range(2):
-        act(r("junk", 0, 256), r("fr", 0, 256), F.Sign, bias=col("fa", 12 + h), acc=col("ac", 8 + h))
+        act(junk(3 + h), r("fr", 0, 256), F.Sign, bias=col("fa", 12 + h), acc=col("ac", 8 + h))
     ts(r("fi", 6, 8), r("fi", 4, 6), float(7 - rank), A.add)
     ts(r("fi", 8, 10), r("fi", 6, 8), 7, A.bitwise_and)
     ts(r("fa", 14, 16), r("fi", 8, 10), float(LC), A.mult, float(FAR0), A.add)
@@ -353,13 +427,7 @@ def rank_program(g, core, T, topo):
         copy("v", blk("rep", 0, 21, a), blk("rl2", 96, 117, rank // 2))
     pick(r("slc", 0, 336), r("sls", 0, 336), r("qx", 0, 256), r("sx", 0, 256), r("rep", 0, 21))
     for s, l, arr in (("slc", "g0", "ac0"), ("sls", "h0", "as0")):
-        mvs = []
-        for i, d in enumerate(peers):
-            q = FAR0 + LC * ((rank - d - 1) % 8)
-            mvs.append((d, r(s, LC * i, LC * i + LC), r(l, q, q + LC)))
-        send(mvs, arr)
-    lands([r("g0", FAR0, NEW0)], "ac0")
-    lands([r("h0", FAR0, NEW0)], "as0")
+        send_each([(d, r(s, LC * i, LC * i + LC), r(l, *slot(d, LC, FAR0))) for i, d in enumerate(peers)], arr, [r(l, FAR0, NEW0)])
     w0 = 32 * ((rank + 1) % 8)
     iota(r("ndv", w0, 256), [[1, 256 - w0]], NEW0, 0)
     if w0:
@@ -403,6 +471,7 @@ def rank_program(g, core, T, topo):
     ts(col("cf", 7), col("cf", 5), -1.0, A.mult, -16384.0, A.add)
     ts(col("cf", 13), col("cf", 2), 1.0, A.add, -float(KC), A.mult)
     ts(col("cf", 14), col("cf", 2), 17.0, A.add, 1024.0, A.mult)
+    ts(r("cf", 29, 31), r("cf", 13, 15), 768.0 * rank, A.add)
     copy("s", r("nl", 768, 1536), r("nl", 0, 768))
     copy("s", r("ol", 0, 256), r("iot", 0, 256))
     ts(r("c4q", 0, 4), r("iot", 0, 4), 0.25, A.mult)
@@ -445,7 +514,7 @@ def rank_program(g, core, T, topo):
                 ts(r("mm_", o + 64 * d, o + 64 * d + 64), r("z", 64 * d, 64 * d + 64), col("zt", 32 * h), A.subtract, col("cf", 31 + d), A.is_gt)
             tt(r("mm_", o, o + 64), r("dd", 64 * h, 64 * h + 64), r("jj", 64 * h, 64 * h + 64), A.is_lt if h else A.is_gt)
             if h == 0:
-                act(r("junk3", 0, 256), r("mm_", 0, 256), F.Copy, acc=col("rk", 0))
+                act(junk(7 + t), r("mm_", 0, 256), F.Copy, acc=col("rk", 0))
                 act(r("cx", 0, 32), C1024, F.Identity, bias=col("cf", 15), scale=col("rk", 0))
         red(col("rk", 1), r("mm_", 256, 512))
         ts(r("cx", 32, 64), C1024, col("rk", 1), A.mult, col("cf", 16), A.add)
@@ -462,29 +531,29 @@ def rank_program(g, core, T, topo):
         copy("v", r("ng", 0, 96), (r("nl", 0, 1536), r("so", 0, 6)))
         tr(r("nt", 0, 96), r("ng", 0, 96))
         copy("v", r("po", 0, 6), r("nt", 0, 96, 16))
+        act(r("sel", 4, 8), r("sw_", 1, 12, 3), F.Copy, acc=col("sel", 1))
+        act(r("sel", 8, 12), r("sw_", 2, 12, 3), F.Copy, acc=col("sel", 2))
+        act(col("sel", 12), col("sel", 1), F.Identity, bias=col("cf", 29))
+        act(col("sel", 13), col("sel", 2), F.Identity, bias=col("cf", 30), scale=-1.0)
+        nd, na = r("ndg", 0, 2) if t % 2 else r("ndg", 2, 4), "nda%d" % t
+        act(nd, r("sel", 12, 14), F.Copy, scale=THIRD)
+        if t < 2:
+            send_all(nd, lambda d: r(na, 2 * rank, 2 * rank + 2), "an%d" % t, [r(na, 2 * s, 2 * s + 2) for s in peers])
+            dma([("y", r(na, 2 * rank, 2 * rank + 2), nd)])
+        act(r("ndf", 0, 2), nd, F.Copy, bias=-256.0 * rank)
         nq, ns = "nq%d" % t, "ns%d" % t
         pick(r(nq, 0, 96), r(ns, 0, 96), r(gq, 0, W), r(gs, 0, W), r("po", 0, 6))
         for b in range(4):
             mm(r("ps", 512 * b, 512 * b + 128), r("qa", 128 * b, 128 * b + 128), r("sa", 128 * b, 128 * b + 128), r(nq, 0, 128), r(ns, 0, 128))
-        red(col("sel", 1), r("sw_", 1, 12, 3))
-        red(col("sel", 2), r("sw_", 2, 12, 3))
-        ts(col("ndf", 0), col("sel", 1), col("cf", 13), A.add, THIRD, A.mult)
-        ts(col("ndf", 1), col("sel", 2), col("cf", 14), A.subtract, -THIRD, A.mult)
-        if t < 2:
-            nd, na = r("ndg", 2 * t, 2 * t + 2), "nda%d" % t
-            ts(nd, r("ndf", 0, 2), 256.0 * rank, A.add)
-            send([(d, nd, r(na, 2 * rank, 2 * rank + 2)) for d in peers], "an%d" % t)
-            lands([r(na, 2 * s, 2 * s + 2) for s in peers], "an%d" % t)
-            dma([("y", r(na, 2 * rank, 2 * rank + 2), nd)])
         for c in range(2):
             ts(r("bo", c, 8, 2), r("c4q", 0, 4), col("ndf", c), A.add, 4.0, A.mult)
+        copy("s", r("bbs", 0, 128), (r("bb_t", 0, 1024), r("bo", 0, 8)))
         for b in range(4):
             copy("s", q32(0, b), r("ps", 512 * b, 512 * b + 32))
         for k, b in ((1, 0), (1, 1), (2, 0), (1, 2), (2, 1), (1, 3), (2, 2), (2, 3)):
             tt(q32(k, b), q32(k - 1, b), r("ps", 512 * b + 32 * k, 512 * b + 32 * k + 32), A.add)
         if t == 2:
             places(t)
-        copy("s", r("bbs", 0, 128), (r("bb_t", 0, 1024), r("bo", 0, 8)))
         for b in range(4):
             act(q32(3, b), q32(2, b), F.Copy, scale=C05)
             tt(r("xt", b, 128, 4), q32(3, b), r("bbs", 32 * b, 32 * b + 32), A.add)
@@ -495,12 +564,7 @@ def rank_program(g, core, T, topo):
             nq, ns, at = "g%d" % (t + 1), "h%d" % (t + 1), W + 224
             quant(r(nq, at, at + 128), r(ns, at, at + 128), r("xt", 0, 512))
             for n, arr in ((nq, "ac%d" % (t + 1)), (ns, "as%d" % (t + 1))):
-                mvs = []
-                for d in peers:
-                    q = W + 32 * ((rank - d - 1) % 8)
-                    mvs.append((d, r(n, at, at + 32), r(n, q, q + 32)))
-                send(mvs, arr)
-                lands([r(n, W, at)], arr)
+                send_all(r(n, at, at + 32), lambda d: r(n, *slot(d, 32, W)), arr, [r(n, W, at)])
         quant(r("ow", o0, o0 + 128), r("os_", o0, o0 + 128), r("xt", 0, 512))
         if t == 0:
             iota(r("np1", 0, 2048), [[0, 2048]], 0, 0)
@@ -519,7 +583,8 @@ def rank_program(g, core, T, topo):
             ts(r("d8", 0, 16), r("frf", 0, 16), col("cf", 1), A.add)
         if t < 2:
             npn = r("np%d" % t, 0, 2048)
-            scatter(npn, r(na, 0, 16), r("ndv", 256 * t, 256 * t + 256))
+            copy("v", r("nai", 0, 16), r(na, 0, 16))
+            scatter(npn, r("nai", 0, 16), r("ndv", 256 * t, 256 * t + 256))
             tt(r("db", 0, 192), (npn, r("dnb", 0, 12)), r("db", 0, 192), A.max)
             tr(r("dt_", 0, 192), r("db", 0, 192))
             copy("v", r("of", 12 * t + 12, 12 * t + 24), r("dt_", 0, 192, 16))
@@ -536,6 +601,7 @@ def rank_program(g, core, T, topo):
     copy("v", r("yt", 0, 128), r("pe", 0, 128))
     copy("s", r("yt", 128, 256), r("pf", 0, 128))
     dma([("s", T.y[:], r("yt", 0, 256))])
+    flush()
     for sem, c in cnt.items():
         if known["g"].get(sem, 0) < c:
             g.wait_ge(T.sem[sem], c)

@@ -10,8 +10,9 @@ NEW0 = P + 7 * LC
 C05 = 13421773 * 2.0 ** -28
 THIRD = float(np.float32(1.0) / np.float32(3.0))
 KC = 1024 * 255
-WAKE, SLACK = 0.15, 0.3
 TINY = 2.0 ** -110
+WAKE, SLACK, SLIP = 0.15, 0.3, 0.1
+CYC, HOLD, FLY, FIRST, LOAD = 0.001, 0.25, 2.4, 2.0, 2.2
 CODE, U8, BF, F32, I32, U16 = "float8_e4m3fn_x4", "uint8", "bfloat16", "float32", "int32", "uint16"
 
 
@@ -20,18 +21,19 @@ def _sbuf(dtype, **cols):
 
 
 SCRATCH = {"pe": ("psum", [128, 512], F32), "pf": ("psum", [128, 512], F32), "ps": ("psum", [128, 2048], F32)}
-SCRATCH.update(_sbuf(F32, nbf=768, iot=2048, jr=256, cf=64, jo=2, ka0=256, ka=256, kat=64, bi=4, junk=2560, junk2=256, junk3=256, ac=16, fa=16, nf=2,
-                     fx=64, fr=256, cx2=64, cr2=256, cc=128, lo=16, lsum=4, ea=1104, fn=256, fz=64, za=64, zb=64, zc=64, zd=64, z=256, zt=64, dd=128, jj=128, rk=4,
-                     cx=64, cr=64, cl=256, sw_=12, sel=16, soc=6, ng=96, nt=96, ndf=2, c4q=4, bbs=128, sc4=512, ndo=4, ndg=4, nda0=16, nda1=16,
-                     np0=2048, np1=2048, ndv=512, nl=1536, db=192, dt_=192, dbf=12, fl=256, lx=64, ol=256, od=96, og=256, ogt=256, yt=256))
-SCRATCH.update(_sbuf(I32, nb32=48, ci=16, fi=16, frf=256))
-SCRATCH.update(_sbuf(U16, nbt=48, lst=4, rl=24, rl2=128, rep=24, so=6, po=6, ndl=2, nai=16, bo=8, dbt=12, dnb=12, of=36, frt=4, d8=16, oo=16))
-SCRATCH.update(_sbuf(BF, xb=1024, bb_t=1024, at=2048, wt=512, u4=4, v4=4, ones=128, ub=512, vb=512, mm_=512, xt=512))
+SCRATCH.update(_sbuf(F32, nbf=768, iot=2048, jr=256, jf=256, cf=64, jo=6, ka=256, kat=64, junk=2560, cq=1024, cz=512, ac=32, fa=28,
+                     sp=192, ex=768, cc=128, lo=16, ea=1104, fn=256, z=256, zt=64, dd=128, jj=128, zs=256, d0z=256, d1z=256, cx=320, cr=64,
+                     cl=256, sa_=4, sb_=8, sel=24, kk=264, ng=96, nt=96, nd_=12, bbs=128, sc4=512, nda0=16, nda1=16,
+                     np0=2048, ndv=512, nl=1536, db=192, dbz=192, dt_=192, dtz=192, ol=256, od=96, og=256, ogt=256, yt=256,
+                     ep=2, er=14, es=448, est=1792))
+SCRATCH.update(_sbuf(I32, nb32=48, ci=16, fi=16, frf=256, gi=24))
+SCRATCH.update(_sbuf(U16, nbt=48, far16=16, pm=16, lst=4, rl=24, rl2=128, rep=24, so=6, po=6, ndl=2, nai=16, bo=8, dbt=12, dnb=12, of=36, frt=4, d8=16, oo=16))
+SCRATCH.update(_sbuf(BF, xb=1024, bb_t=1024, at=2048, wt=512, u4=4, v4=4, ones=128, ub=512, vb=512, mm_=640, xt=512))
 for _c, _s, _n in (("qx", "sx", 256), ("qb", "sb", 256), ("qu", "su", 128), ("qv", "sv", 128), ("qa", "sa", 512), ("qw", "sw", 128), ("slc", "sls", 336),
                    ("g0", "h0", 592), ("g1", "h1", 944), ("g2", "h2", 1200), ("nq0", "ns0", 128), ("nq1", "ns1", 128), ("nq2", "ns2", 128),
                    ("ow", "os_", 640), ("occ", "ocs", 256)):
     SCRATCH.update({_c: ("sbuf", [128, _n], CODE), _s: ("sbuf", [128, _n], U8)})
-SEMAPHORES = ["cv", "cs", "ct", "cg"] + ["q%d" % i for i in range(60)] + ["arl", "ac0", "as0", "an0", "an1", "ac1", "as1", "ac2", "as2"]
+SEMAPHORES = ["cv", "cs", "ct", "cg"] + ["q%d" % i for i in range(60)] + ["aer", "arl", "ac0", "as0", "an0", "an1", "ac1", "as1", "ac2", "as2"]
 
 
 def r(name, c0, c1, step=1, p0=0, p1=128):
@@ -91,8 +93,8 @@ def rank_program(g, core, T, topo):
         note(q, reads, writes, i)
         return i
 
-    def emit(q, fn, reads, writes, cycles, fixed=0.0):
-        put(q, fn, reads, writes, fixed + max(64, cycles) * 0.001)
+    def emit(q, fn, reads, writes, cycles, fixed=0.0, deps=()):
+        put(q, fn, reads, writes, fixed + max(64, cycles) * CYC, deps=deps)
 
     def width(x):
         return -(-(x[2] - x[1]) // x[3])
@@ -109,27 +111,43 @@ def rank_program(g, core, T, topo):
         left = [len(o["deps"]) for o in ops]
         ready = {q: [] for q in "vstgyr"}
         clock = {q: 0.0 for q in ready}
+        todo = {q: {i for i, o in enumerate(ops) if o["q"] == q} for q in ready}
         for i, o in enumerate(ops):
             o["est"] = 0.0
             if not left[i]:
                 ready[o["q"]].append(i)
-        out = []
+        out, done, low = [], [False] * len(ops), [0.0] * len(ops)
+
+        def soonest():
+            for i, o in enumerate(ops):
+                if not done[i]:
+                    low[i] = max([o["est"]] + [low[k] + ops[k]["cost"] + ops[k]["late"] + WAKE for k in o["deps"] if not done[k]])
+
+        stamp = [-1]
         while any(ready.values()):
-            best = None
+            best, spare = None, None
             for q, l in ready.items():
                 if not l:
                     continue
                 est = {i: max(clock[q], ops[i]["est"]) for i in l}
                 t0 = min(est.values())
-                c = max([i for i in l if est[i] <= t0 + 0.001], key=lambda i: ops[i]["rank"])
-                for i in l:
-                    if est[i] < t0 + ops[c]["cost"] and ops[i]["rank"] > ops[c]["rank"] + SLACK:
-                        c = i
-                if best is None or est[c] < best[0]:
+                for c in sorted(l, key=lambda i: (est[i] > t0 + 0.001, -ops[i]["rank"] if est[i] <= t0 + 0.001 else est[i])):
+                    if spare is None or est[c] < spare[0]:
+                        spare = (est[c], c)
+                    if best is not None and est[c] >= best[0]:
+                        break
+                    if stamp[0] != len(out):
+                        soonest()
+                        stamp[0] = len(out)
+                    if q != "r" and any(low[j] < est[c] + ops[c]["cost"] - SLIP and ops[j]["rank"] > ops[c]["rank"] + SLACK for j in todo[q]):
+                        continue
                     best = (est[c], c)
-            t, i = best
+                    break
+            t, i = best or spare
             o = ops[i]
             ready[o["q"]].remove(i)
+            todo[o["q"]].discard(i)
+            done[i] = True
             clock[o["q"]] = t + o["cost"]
             out.append(i)
             for k in o["users"]:
@@ -174,9 +192,12 @@ def rank_program(g, core, T, topo):
     def sc(x):
         return (ap(x), [x]) if isinstance(x, tuple) else (x, [])
 
+    def by(in_):
+        return 1.5 if len(in_) == 2 else 1
+
     def copy(q, out, in_):
         i, rd = src(in_)
-        n = width(out) * (1.5 if len(in_) == 2 else 1)
+        n = width(out) * by(in_)
         if q == "v":
             emit(q, lambda: g.vector.tensor_copy(ap(out), i), rd, [out], n)
         else:
@@ -189,10 +210,17 @@ def rank_program(g, core, T, topo):
         i, rd = src(in_)
         b, rb = sc(bias)
         s, rs = sc(scale)
+        n = width(out) * by(in_)
         if acc is None:
-            emit("s", lambda: g.scalar.activation(ap(out), i, func, bias=b, scale=s), rd + rb + rs, [out], width(out))
+            emit("s", lambda: g.scalar.activation(ap(out), i, func, bias=b, scale=s), rd + rb + rs, [out], n)
         else:
-            emit("s", lambda: g.scalar.activation(ap(out), i, func, bias=b, scale=s, accum_out=ap(acc)), rd + rb + rs, [out, acc], width(out))
+            emit("s", lambda: g.scalar.activation(ap(out), i, func, bias=b, scale=s, accum_out=ap(acc)), rd + rb + rs, [out, acc], n)
+
+    def const(out, val):
+        act(out, r("iot", 0, width(out), 1, out[4], out[5]), F.Copy, bias=val, scale=0.0)
+
+    def lin(out, in_, scale, bias):
+        act(out, in_, F.Identity if isinstance(bias, tuple) else F.Copy, bias=bias, scale=scale)
 
     def ts(out, in_, s1, op0, s2=None, op1=None):
         i, rd = src(in_)
@@ -205,10 +233,11 @@ def rank_program(g, core, T, topo):
 
     def tt(out, in0, in1, op):
         i, rd = src(in0)
-        emit("v", lambda: g.vector.tensor_tensor(ap(out), i, ap(in1), op), rd + [in1], [out], 2 * width(out))
+        emit("v", lambda: g.vector.tensor_tensor(ap(out), i, ap(in1), op), rd + [in1], [out], (1.5 if len(in0) == 2 else 2) * width(out))
 
-    def red(out, in_):
-        emit("v", lambda: g.vector.tensor_reduce(ap(out), ap(in_), AxisListType.X, A.add), [in_], [out], width(in_))
+    def scan(out, d0, d1, initial, op0, op1):
+        a, ra = sc(initial)
+        emit("v", lambda: g.vector.tensor_tensor_scan(ap(out), ap(d0), ap(d1), a, op0, op1), [d0, d1] + ra, [out], width(out))
 
     def least(out, in_):
         emit("v", lambda: g.vector.tensor_reduce(ap(out), ap(in_), AxisListType.X, A.min, apply_absolute_value=True), [in_], [out], width(in_))
@@ -225,11 +254,11 @@ def rank_program(g, core, T, topo):
     def mm(out, wq, ws, xq, xs):
         emit("t", lambda: g.tensor.matmul_mx(ap(out), ap(wq), ap(ws), ap(xq), ap(xs), True, True), [wq, ws, xq, xs], [out], width(out))
 
-    def iota(out, pattern, base, cm, flag=True):
+    def iota(out, pattern, base, cm, flag=True, after=()):
         if flag:
-            emit("g", lambda: g.iota(ap(out), pattern, base, cm, allow_small_or_imprecise_dtypes=True), [], [out], 2 * width(out), 0.13)
+            emit("g", lambda: g.iota(ap(out), pattern, base, cm, allow_small_or_imprecise_dtypes=True), [], [out], 2 * width(out), 0.13, after)
         else:
-            emit("g", lambda: g.iota(ap(out), pattern, base, cm), [], [out], 2 * width(out), 0.13)
+            emit("g", lambda: g.iota(ap(out), pattern, base, cm), [], [out], 2 * width(out), 0.13, after)
 
     def pick(qo, so, win, wins, off):
         emit("v", lambda: g.vector.tensor_copy(ap(qo).bitcast(dt.uint32), ap(win).bitcast(dt.uint32).indirect(ap(off))), [win, off], [qo], 1.5 * width(qo))
@@ -238,14 +267,14 @@ def rank_program(g, core, T, topo):
     def side(x):
         return ap(x).bitcast(dt.uint8) if SCRATCH[x[0]][2] == CODE else ap(x)
 
-    def dma(moves):
+    def dma(moves, late=LOAD):
         sem = newsem()
         made = []
         for q, out, in_ in moves:
             wr = [out] if isinstance(out, tuple) else []
             rd = [in_] if isinstance(in_, tuple) else []
             o, i = side(out) if wr else out, side(in_) if rd else in_
-            made.append(put(q, lambda q=q, o=o, i=i: eng[q].dma_start(o, i).then_inc(T.sem[sem], 16), rd, wr, 0.07, 2.2, sem, 16 * len(moves)))
+            made.append(put(q, lambda q=q, o=o, i=i: eng[q].dma_start(o, i).then_inc(T.sem[sem], 16), rd, wr, 0.07, late, sem, 16 * len(moves)))
         for k in made:
             ops[k]["peers"] = made
 
@@ -265,24 +294,25 @@ def rank_program(g, core, T, topo):
 
     def issue(trs, reads, total):
         sem = newsem()
-        return put("g", lambda: g.remote_dma_fused(trs, local_sem=T.sem[sem]), reads, [], 1.0, 0.7, sem, total)
+        return put("g", lambda: g.remote_dma_fused(trs, local_sem=T.sem[sem]), reads, [], HOLD, FLY - 0.5, sem, total)
 
     def send_each(moves, arr, regions):
         i = issue([RemoteDMATransfer(dst_ids=[ids[d]], dma_engine_mask=masks[d], remote_sem=T.sem[arr], srcs=[side(s)], dsts=[side(l)]) for d, s, l in moves],
                   [m[1] for m in moves], 2 * len(moves))
-        put("r", None, [], regions, 0.0, 1.0, arr, 2 * 7, [i])
+        put("r", None, [], regions, 0.0, 2.0, arr, 2 * 7, [i])
 
-    def send_all(s, land, arr, regions):
+    def send_all(s, land, arr, regions, more=0.0):
         i = issue([RemoteDMATransfer(dst_ids=[ids[d] for d in peers], dma_engine_mask=sum(1 << x for x in full), remote_sem=T.sem[arr], srcs=[side(s)],
                                      dsts=[side(land(d)) for d in peers])], [s], len(full))
-        put("r", None, [], regions, 0.0, 0.7, arr, len(full) * 7, [i])
+        put("r", None, [], regions, 0.0, 0.5 + more, arr, len(full) * 7, [i])
+        return i
 
-    def exchange(n, w=64):
+    def exchange(n, w=64, o=0):
         for a in range(4):
             b = (a + 1) % 4
-            copy("vs"[a % 2], r(n, w, 2 * w, 1, 32 * a, 32 * a + 32), r(n, 0, w, 1, 32 * b, 32 * b + 32))
-        copy("v", r(n, 2 * w, 4 * w, 1, 0, 64), r(n, 0, 2 * w, 1, 64, 128))
-        copy("s", r(n, 2 * w, 4 * w, 1, 64, 128), r(n, 0, 2 * w, 1, 0, 64))
+            copy("vs"[a % 2], r(n, o + w, o + 2 * w, 1, 32 * a, 32 * a + 32), r(n, o, o + w, 1, 32 * b, 32 * b + 32))
+        copy("v", r(n, o + 2 * w, o + 4 * w, 1, 0, 64), r(n, o, o + 2 * w, 1, 64, 128))
+        copy("s", r(n, o + 2 * w, o + 4 * w, 1, 64, 128), r(n, o, o + 2 * w, 1, 0, 64))
 
     def col(n, c, w=1):
         return r(n, c, c + w)
@@ -292,6 +322,10 @@ def rank_program(g, core, T, topo):
 
     def junk(i):
         return r("junk", 256 * i, 256 * i + 256)
+
+    def total(i, x, c):
+        scan(r("cz", 128 * i, 128 * i + 128), r(x, c, c + 128), r(x, c + 128, c + 256), 0.0, A.add, A.add)
+        return col("cz", 128 * i + 127)
 
     mv = []
     for gr in range(8):
@@ -307,114 +341,193 @@ def rank_program(g, core, T, topo):
     dma([("y", r("at", 0, 2048), T.a[:])])
     dma([("y", r("wt", 0, 512), T.w[:])])
 
+    C4096, CM128, C1024, CONE = r("cc", 0, 32), r("cc", 32, 64), r("cc", 64, 96), r("cc", 96, 128)
     iota(r("ci", 0, 1), [[0, 1]], 0, 1, False)
     iota(r("iot", 0, 256), [[1, 256]], 0, 0)
+    iota(r("kk", 24, 72), [[0, 16], [1, 3]], 0, 0)
+    iota(r("iot", 1536, 2048), [[1, 512]], 1536, 0)
     iota(r("lo", 8, 11), [[4096, 3]], 0, 0)
-    iota(r("dbf", 0, 12), [[1, 3], [96, 2], [0, 2]], 0, 0)
-    iota(r("soc", 0, 6), [[1, 3], [0, 2]], 768, 0)
+    iota(r("kk", 6, 18), [[1, 3], [96, 2], [0, 2]], 0, 0)
+    iota(r("kk", 0, 6), [[1, 3], [0, 2]], 768, 0)
     ts(r("ci", 1, 2), r("ci", 0, 1), 31, A.bitwise_and)
     ts(r("ci", 2, 3), r("ci", 0, 1), 15, A.bitwise_and)
     copy("v", r("cf", 0, 3), r("ci", 0, 3))
+    ts(r("ci", 3, 4), r("ci", 2, 3), 11.0, A.mult)
+    ts(r("ci", 4, 5), r("ci", 3, 4), 5, A.arith_shift_right)
+    ts(col("cf", 40), r("ci", 4, 5), -3.0, A.mult, col("cf", 2), A.add)
+    ts(r("kk", 72, 120), r("kk", 24, 72), col("cf", 40), A.add, 2.0, A.is_equal)
+    ts(r("kk", 120, 168), r("kk", 24, 72), 0.5, A.is_gt)
     ts(col("cf", 26), col("cf", 0), col("cf", 1), A.subtract, 2.0, A.mult)
     ts(r("iot", 256, 512), r("iot", 0, 256), 256.0, A.add)
     act(r("iot", 512, 1024), r("iot", 0, 512), F.Copy, bias=512.0)
     act(r("iot", 1024, 1536), r("iot", 0, 512), F.Copy, bias=1024.0)
-    act(r("iot", 1536, 2048), r("iot", 0, 512), F.Copy, bias=1536.0)
     ts(r("frf", 0, 256), r("iot", 0, 256), col("cf", 26), A.add)
     tt(col("jo", 0), col("cf", 26), col("cf", 1), A.add)
     ts(r("frf", 0, 256), r("frf", 0, 256), 255, A.bitwise_and)
     ts(col("jo", 1), col("jo", 0), 32.0, A.add)
-
-    copy("v", r("nbt", 0, 48), r("nb32", 0, 48))
-    copy("v", r("nbf", 0, 384), (r("iot", 0, 2048), r("nbt", 0, 24)))
-    copy("s", r("nbf", 384, 768), (r("iot", 0, 2048), r("nbt", 24, 48)))
+    ts(r("jo", 2, 4), r("jo", 0, 2), 1.0 / 512, A.mult)
     copy("v", r("jr", 0, 256), r("frf", 0, 256))
-    C4096, CM128, C1024, CONE = r("cc", 0, 32), r("cc", 32, 64), r("cc", 64, 96), r("cc", 96, 128)
+    lin(r("jf", 0, 256), r("jr", 0, 256), 1.0 / 512, 0.0)
+
+    tt(r("kk", 168, 216), r("nb32", 0, 48), r("kk", 72, 120), A.mult)
+    scan(r("kk", 216, 264), r("kk", 120, 168), r("kk", 168, 216), 0.0, A.mult, A.add)
+    copy("v", r("far16", 0, 16), r("kk", 218, 264, 3))
+    tt(r("ka", 0, 256), (r("iot", 0, 2048), r("far16", 0, 16)), r("jf", 0, 256), A.add)
     fill(C4096, 4096.0)
     fill(CM128, -128.0)
-    act(r("ka0", 0, 256), r("nbf", 2, 768, 3), F.Copy, scale=512.0)
-    tt(r("ka", 0, 256), r("ka0", 0, 256), r("jr", 0, 256), A.add)
     tr(r("kat", 0, 64), r("ka", 0, 64))
-    tt(r("bi", 0, 2), r("jo", 0, 2), r("kat", 0, 64, 32), A.subtract)
-    act(junk(0), r("ka", 0, 256), F.Identity, bias=col("bi", 0))
-    act(r("junk3", 0, 256), r("ka", 0, 256), F.Identity, bias=col("bi", 1))
-    ts(r("fa", 0, 2), r("bi", 0, 2), -1.0 / 512, A.mult)
-    ts(r("fa", 2, 4), r("bi", 0, 2), 1.0 / 512, A.mult, 0.5, A.add)
+    tt(r("jo", 4, 6), r("jo", 2, 4), r("kat", 0, 64, 32), A.subtract)
+    act(junk(0), r("ka", 0, 256), F.Identity, bias=col("jo", 4))
+    ts(junk(6), r("ka", 0, 256), col("jo", 5), A.add)
+    ts(r("fa", 0, 2), r("jo", 4, 6), -1.0, A.mult)
+    ts(r("fa", 2, 4), r("jo", 4, 6), 0.5, A.add)
     least(col("ac", 0), junk(0))
     copy("v", r("fi", 0, 2), r("fa", 0, 2))
-    least(col("ac", 1), r("junk3", 0, 256))
+    least(col("ac", 1), junk(6))
     ts(r("fi", 2, 4), r("fi", 0, 2), 255, A.bitwise_and)
-    tt(r("nf", 0, 2), r("ac", 0, 2), r("jo", 0, 2), A.not_equal)
+    tt(r("ac", 6, 8), r("ac", 0, 2), r("jo", 2, 4), A.not_equal)
     copy("v", r("fa", 4, 6), r("fi", 2, 4))
-    ts(r("fx", 0, 32), C4096, col("nf", 0), A.mult, col("fa", 0), A.add)
-    act(r("fx", 32, 64), C4096, F.Identity, bias=col("fa", 1), scale=col("nf", 1))
+    ts(r("sp", 0, 32), C4096, col("ac", 6), A.mult, col("fa", 0), A.add)
+    act(r("sp", 32, 64), C4096, F.Identity, bias=col("fa", 1), scale=col("ac", 7))
     ts(col("cf", 17), col("cf", 0), col("cf", 2), A.subtract, 16.0, A.mult)
-    tr(r("fr", 0, 64), r("fx", 0, 64))
-    exchange("fr")
+    tr(r("ex", 0, 64), r("sp", 0, 64))
+    exchange("ex", 64, 0)
+    FR, CR2, FL = r("ex", 0, 256), r("ex", 256, 512), r("ex", 512, 768)
     for h in range(2):
-        act(junk(1 + h), r("fr", 0, 256), F.Sign, bias=col("fa", 2 + h), acc=col("ac", 4 + h))
-    ts(r("junk2", 0, 256), r("fr", 0, 256), col("cf", 17), A.is_ge)
-    ts(r("fa", 6, 8), r("nf", 0, 2), 1048576.0, A.mult)
-    red(col("lsum", 3), r("junk2", 0, 256))
+        act(junk(1 + h), FR, F.Sign, bias=col("fa", 2 + h), acc=col("ac", 4 + h))
+    ts(r("cq", 768, 1024), FR, col("cf", 17), A.is_ge)
+    ts(r("fa", 6, 8), r("ac", 6, 8), 1048576.0, A.mult)
+    below = total(3, "cq", 768)
     tt(r("fa", 8, 10), r("fa", 6, 8), r("fa", 4, 6), A.add)
-    ts(r("cx2", 0, 32), CM128, col("ac", 4), A.mult, col("fa", 8), A.add)
-    act(r("cx2", 32, 64), CM128, F.Identity, bias=col("fa", 9), scale=col("ac", 5))
+    ts(r("sp", 64, 96), CM128, col("ac", 4), A.mult, col("fa", 8), A.add)
+    act(r("sp", 96, 128), CM128, F.Identity, bias=col("fa", 9), scale=col("ac", 5))
     ts(col("cf", 18), col("cf", 2), 256.0, A.mult)
-    tr(r("cr2", 0, 64), r("cx2", 0, 64))
+    tr(r("ex", 256, 320), r("sp", 64, 128))
     ts(r("lo", 0, 3), r("lo", 8, 11), col("cf", 18), A.add, 32768.0, A.add)
-    exchange("cr2")
-    ts(col("cf", 19), col("lsum", 3), -256.0, A.mult)
-    fill(col("cf", 20), 256.0)
+    exchange("ex", 64, 256)
+    ts(col("cf", 19), below, -256.0, A.mult)
     ts(r("lo", 3, 6), r("lo", 0, 3), col("cf", 19), A.add)
-    ts(col("lo", 6), col("lo", 5), -1.0, A.mult)
     ts(r("lo", 11, 14), r("lo", 3, 6), 256.0, A.add)
-    act(junk(0), r("cr2", 0, 256), F.Relu, bias=col("lo", 6))
-    ts(col("cf", 23), col("lo", 5), 33024.0, A.add)
-    ts(r("ka0", 0, 256), r("cr2", 0, 256), col("lo", 3), A.max, col("lo", 11), A.min)
-    ts(r("junk2", 0, 256), r("cr2", 0, 256), col("lo", 4), A.max, col("lo", 12), A.min)
-    act(junk(5), junk(0), F.Relu, bias=col("cf", 20), scale=-1.0, acc=col("lsum", 2))
-    act(junk(6), r("ka0", 0, 256), F.Copy, acc=col("lsum", 0))
-    act(col("cf", 24), col("lsum", 2), F.Identity, bias=col("cf", 23), scale=-1.0)
-    ts(r("cf", 21, 23), r("lo", 3, 5), -255.0, A.mult, -32512.0, A.add)
-    red(col("lsum", 1), r("junk2", 0, 256))
-    for c in range(2):
-        ts(col("lst", c), col("lsum", c), col("cf", 21 + c), A.add, 255.0, A.min)
-    ts(col("lst", 2), col("cf", 24), 255.0, A.min)
+    ts(r("cf", 21, 24), r("lo", 3, 6), -255.0, A.mult, -32512.0, A.add)
+    sums = [col("ac", 16)]
+    for c in range(3):
+        ts(r("cq", 256 * c, 256 * c + 256), CR2, col("lo", 3 + c), A.max, col("lo", 11 + c), A.min)
+    act(junk(5), r("cq", 0, 256), F.Copy, acc=sums[0])
+    for c in range(1, 3):
+        sums.append(total(c, "cq", 256 * c))
+    for c in range(3):
+        ts(col("lst", c), sums[c], col("cf", 21 + c), A.add, 255.0, A.min)
 
     def slot(d, w, base=0):
         q = base + w * ((rank - d - 1) % 8)
         return q, q + w
-    send_all(r("lst", 0, 3), lambda d: r("rl", *slot(d, 3)), "arl", [r("rl", 0, 21)])
 
     quant(r("qx", 0, 256), r("sx", 0, 256), r("xb", 0, 1024))
     fill(r("ones", 0, 128), 1.0)
     for i in range(4):
         ts(r("ub", i, 512, 4), r("ones", 0, 128), col("u4", i), A.mult)
     quant(r("qu", 0, 128), r("su", 0, 128), r("ub", 0, 512))
+    for h in range(2):
+        mm(r("ps", 512 * h, 512 * h + 128), r("qx", 128 * h, 128 * h + 128), r("sx", 128 * h, 128 * h + 128), r("qu", 0, 128), r("su", 0, 128))
+        copy("s", col("ep", h), col("ps", 512 * h))
+    send_all(r("ep", 0, 2), lambda d: r("er", *slot(d, 2)), "aer", [r("er", 0, 14)], FIRST)
+    asked = send_all(r("lst", 0, 3), lambda d: r("rl", *slot(d, 3)), "arl", [r("rl", 0, 21)])
     mm(r("pe", 0, 256), r("qu", 0, 128), r("su", 0, 128), r("qx", 0, 256), r("sx", 0, 256))
+    copy("s", r("ea", 0, 256), r("pe", 0, 256))
     dma([("y", r("g0", 0, 256), r("qx", 0, 256)), ("y", r("h0", 0, 256), r("sx", 0, 256))])
     dma([("y", r("ow", 0, 256), r("qx", 0, 256)), ("y", r("os_", 0, 256), r("sx", 0, 256))])
 
+    copy("v", r("nbt", 0, 48), r("nb32", 0, 48))
+    for i in range(0, 48, 12):
+        copy("s", r("nbf", 16 * i, 16 * i + 192), (r("iot", 0, 2048), r("nbt", i, i + 12)))
+    ts(col("cf", 25), col("cf", 1), 3.0, A.mult)
+    ts(r("dbt", 0, 12), r("kk", 6, 18), col("cf", 25), A.add)
+    copy("v", r("dbz", 0, 192), (r("nbf", 0, 768), r("dbt", 0, 12)))
+    tr(r("dtz", 0, 192), r("dbz", 0, 192))
+    ts(r("of", 0, 8), r("dtz", 0, 128, 16), -256.0 * rank, A.add)
+    ts(r("gi", 0, 4), r("dtz", 128, 192, 16), 2048.0 - 256.0 * (rank + 1), A.add)
+    ts(r("gi", 4, 8), r("gi", 0, 4), 2, A.arith_shift_right, 480, A.bitwise_and)
+    ts(r("gi", 8, 12), r("gi", 0, 4), 127, A.bitwise_and)
+    ts(col("cf", 42), col("cf", 26), -0.5, A.mult, 128.0, A.add)
+    ts(r("gi", 12, 16), r("gi", 8, 12), col("cf", 42), A.add)
+    ts(r("gi", 16, 20), r("gi", 12, 16), 127, A.bitwise_and)
+    ts(r("gi", 20, 24), r("gi", 12, 16), 5, A.arith_shift_right, 3, A.bitwise_and)
+    tt(r("fa", 16, 20), r("gi", 4, 8), r("gi", 16, 20), A.add)
+    ts(r("fa", 20, 24), r("gi", 20, 24), 416.0, A.mult)
+    tt(r("fa", 24, 28), r("fa", 16, 20), r("fa", 20, 24), A.add)
+    copy("v", r("of", 8, 12), r("fa", 24, 28))
+
     fill(CONE, 1.0)
+    for c in range(14):
+        o = r("es", 32 * c, 32 * c + 32)
+        if c % 2:
+            ts(o, CONE, col("er", c), A.mult)
+        else:
+            act(o, CONE, F.Copy, scale=col("er", c))
+    tr(r("est", 0, 448), r("es", 0, 448))
+    mv = []
+    for d in range(1, 4):
+        mv.append(("y", r("est", 448 * d, 448 * d + 448, 1, 0, 128 - 32 * d), r("est", 0, 448, 1, 32 * d, 128)))
+        mv.append(("y", r("est", 448 * d, 448 * d + 448, 1, 128 - 32 * d, 128), r("est", 0, 448, 1, 0, 32 * d)))
+    dma(mv, LOAD + 1.2)
+
+    for h in range(2):
+        quant(r("qb", 128 * h, 128 * h + 128), r("sb", 128 * h, 128 * h + 128), r("bb_t", 512 * h, 512 * h + 512))
+    for i in range(4):
+        ts(r("vb", i, 512, 4), r("ones", 0, 128), col("v4", i), A.mult)
+    quant(r("qv", 0, 128), r("sv", 0, 128), r("vb", 0, 512))
+    mm(r("pf", 0, 256), r("qv", 0, 128), r("sv", 0, 128), r("qb", 0, 256), r("sb", 0, 256))
+    copy("s", r("fn", 0, 256), r("pf", 0, 256))
+    ts(col("cf", 27), col("cf", 26), col("cf", 2), A.add)
+    ts(r("frt", 0, 4), r("iot", 0, 64, 16), col("cf", 27), A.add)
+    act(r("d1z", 3, 256, 4), (r("fn", 0, 256), r("frt", 0, 4)), F.Copy, scale=-1.0)
+    const(r("d0z", 0, 256), 1.0)
+    act(r("d0z", 0, 256, 4), r("iot", 0, 64), F.Copy, scale=0.0)
+    for i in range(4):
+        const(r("mm_", 160 * i + 128, 160 * i + 160), 0.0)
+    const(col("cf", 35), 1024.0)
+    const(r("cf", 32, 35), 0.0)
+    const(r("cf", 32, 33, 1, 96, 128), -TINY)
+    const(r("cf", 33, 34, 1, 64, 128), -TINY)
+    const(r("cf", 34, 35, 1, 64, 128), -TINY)
+    const(r("cf", 34, 35, 1, 32, 64), -TINY)
+    lin(col("cf", 4), col("cf", 1), 1.0, 1.0)
+    lin(col("cf", 6), col("cf", 2), 1.0, 1.0)
+    lin(col("cf", 7), col("cf", 2), -1.0, -16.0)
+    lin(col("cf", 12), col("cf", 1), -float(KC), -float(KC))
+    lin(r("cf", 15, 17), r("jo", 0, 2), 3.0 / 1024, 0.0)
+    ts(r("jj", 0, 64), r("jr", 0, 64), col("jo", 0), A.is_lt, -TINY, A.mult)
+    ts(r("jj", 64, 128), r("jr", 0, 64), col("jo", 1), A.is_lt, TINY, A.mult)
+    lin(col("cf", 28), col("cf", 26), -3.0, col("cf", 12))
+    SOC = r("kk", 0, 6)
+    lin(SOC, SOC, 1.0, col("cf", 28))
+    lin(col("cf", 29), col("cf", 2), -float(KC), 768.0 * rank - KC)
+    lin(col("cf", 30), col("cf", 2), 1024.0, 768.0 * rank + 17 * 1024)
+    lin(r("kk", 18, 22), r("iot", 0, 4), 0.25, 0.0)
+    copy("s", r("ol", 0, 256), r("iot", 0, 256))
+
     ts(r("fi", 4, 6), r("fi", 0, 2), 8, A.arith_shift_right)
     copy("v", r("fa", 10, 12), r("fi", 4, 6))
     ts(r("fa", 12, 14), r("fa", 10, 12), -256.0, A.mult, 0.5, A.add)
     for h in range(2):
-        act(junk(3 + h), r("fr", 0, 256), F.Sign, bias=col("fa", 12 + h), acc=col("ac", 8 + h))
+        act(junk(3 + h), FR, F.Sign, bias=col("fa", 12 + h), acc=col("ac", 8 + h))
     ts(r("fi", 6, 8), r("fi", 4, 6), float(7 - rank), A.add)
     ts(r("fi", 8, 10), r("fi", 6, 8), 7, A.bitwise_and)
     ts(r("fa", 14, 16), r("fi", 8, 10), float(LC), A.mult, float(FAR0), A.add)
     for k in range(2):
-        ts(r("nl", k, 768, 3), r("nbf", k, 768, 3), -256.0 * rank, A.add)
+        lin(r("nl", k, 768, 3), r("nbf", k, 768, 3), 1.0, -256.0 * rank)
     tt(r("ac", 10, 12), r("ac", 8, 10), r("ac", 4, 6), A.subtract)
     ts(r("ac", 12, 14), r("ac", 10, 12), 0.5, A.mult)
     tt(r("ac", 14, 16), r("ac", 12, 14), r("fa", 14, 16), A.add)
-    ts(r("lx", 0, 32), CONE, col("ac", 14), A.mult)
-    act(r("lx", 32, 64), CONE, F.Copy, scale=col("ac", 15))
-    tr(r("fl", 0, 64), r("lx", 0, 64))
-    exchange("fl")
-    copy("s", r("nl", 2, 768, 3), r("fl", 0, 256))
-    copy("s", r("ea", 0, 256), r("pe", 0, 256))
+    ts(r("sp", 128, 160), CONE, col("ac", 14), A.mult)
+    act(r("sp", 160, 192), CONE, F.Copy, scale=col("ac", 15))
+    tr(r("ex", 512, 576), r("sp", 128, 192))
+    exchange("ex", 64, 512)
+    ts(r("ci", 5, 6), r("ci", 2, 3), 3.0, A.mult, 2.0, A.add)
+    ts(r("ci", 6, 7), r("ci", 5, 6), 15, A.bitwise_and)
+    copy("v", col("cf", 41), r("ci", 6, 7))
+    ts(r("pm", 0, 16), r("iot", 0, 256, 16), col("cf", 41), A.add)
+    copy("s", r("nl", 2, 768, 3), (FL, r("pm", 0, 16)))
     fill(r("rl2", 0, 128), 0)
 
     copy("v", r("rl2", 0, 21), r("rl", 0, 21))
@@ -432,51 +545,16 @@ def rank_program(g, core, T, topo):
     iota(r("ndv", w0, 256), [[1, 256 - w0]], NEW0, 0)
     if w0:
         iota(r("ndv", 0, w0), [[1, w0]], NEW0 + 256 - w0, 0)
-    iota(r("np0", 0, 2048), [[0, 2048]], 0, 0)
+    for i in range(4):
+        iota(r("np0", 512 * i, 512 * i + 512), [[0, 512]], 0, 0, after=[asked])
     iota(r("od", 0, 96), [[128, 3], [1, 32]], P, 0)
 
-    ts(col("cf", 25), col("cf", 1), 3.0, A.mult)
-    ts(r("dbt", 0, 12), r("dbf", 0, 12), col("cf", 25), A.add)
+    for i in range(0, 768, 256):
+        copy("s", r("nl", 768 + i, 1024 + i), r("nl", i, i + 256))
     copy("v", r("db", 0, 192), (r("nl", 0, 768), r("dbt", 0, 12)))
-    tr(r("dt_", 0, 192), r("db", 0, 192))
-    copy("v", r("of", 0, 12), r("dt_", 0, 192, 16))
-    quant(r("qb", 0, 256), r("sb", 0, 256), r("bb_t", 0, 1024))
-    for i in range(4):
-        ts(r("vb", i, 512, 4), r("ones", 0, 128), col("v4", i), A.mult)
-    quant(r("qv", 0, 128), r("sv", 0, 128), r("vb", 0, 512))
-    mm(r("pf", 0, 256), r("qv", 0, 128), r("sv", 0, 128), r("qb", 0, 256), r("sb", 0, 256))
-    copy("s", r("fn", 0, 256), r("pf", 0, 256))
-    ts(col("cf", 27), col("cf", 26), col("cf", 2), A.add)
-    ts(r("frt", 0, 4), r("iot", 0, 64, 16), col("cf", 27), A.add)
-    copy("s", r("za", 0, 64), (r("ea", 0, 256), r("of", 0, 4)))
-    tt(r("zb", 0, 64), (r("ea", 0, 256), r("of", 4, 8)), r("za", 0, 64), A.add)
-    copy("s", r("fz", 0, 64), (r("fn", 0, 256), r("frt", 0, 4)))
-    fill(C1024, 1024.0)
-    fill(col("cf", 35), 1024.0)
-    fill(r("cf", 32, 35), 0.0)
-    fill(r("cf", 32, 33, 1, 96, 128), -TINY)
-    fill(r("cf", 33, 34, 1, 64, 128), -TINY)
-    fill(r("cf", 34, 35, 1, 64, 128), -TINY)
-    fill(r("cf", 34, 35, 1, 32, 64), -TINY)
-    ts(col("cf", 3), col("cf", 1), 1024.0, A.mult)
-    ts(col("cf", 4), col("cf", 3), 1024.0, A.add)
-    ts(col("cf", 12), col("cf", 1), 1.0, A.add, -float(KC), A.mult)
-    ts(r("cf", 15, 17), r("jo", 0, 2), 3.0, A.mult)
-    ts(r("jj", 0, 64), r("jr", 0, 64), col("jo", 0), A.is_lt, -TINY, A.mult)
-    ts(r("jj", 64, 128), r("jr", 0, 64), col("jo", 1), A.is_lt, TINY, A.mult)
-    ts(col("cf", 28), col("cf", 26), -3.0, A.mult, col("cf", 12), A.add)
-    ts(r("soc", 0, 6), r("soc", 0, 6), col("cf", 28), A.add)
-    ts(col("cf", 5), col("cf", 2), 1024.0, A.mult)
-    ts(col("cf", 6), col("cf", 5), 1024.0, A.add)
-    ts(col("cf", 7), col("cf", 5), -1.0, A.mult, -16384.0, A.add)
-    ts(col("cf", 13), col("cf", 2), 1.0, A.add, -float(KC), A.mult)
-    ts(col("cf", 14), col("cf", 2), 17.0, A.add, 1024.0, A.mult)
-    ts(r("cf", 29, 31), r("cf", 13, 15), 768.0 * rank, A.add)
-    copy("s", r("nl", 768, 1536), r("nl", 0, 768))
-    copy("s", r("ol", 0, 256), r("iot", 0, 256))
-    ts(r("c4q", 0, 4), r("iot", 0, 4), 0.25, A.mult)
     fill(r("xt", 0, 512), 0.0)
-    quant(r("qa", 0, 512), r("sa", 0, 512), r("at", 0, 2048))
+    for b in range(4):
+        quant(r("qa", 128 * b, 128 * b + 128), r("sa", 128 * b, 128 * b + 128), r("at", 512 * b, 512 * b + 512))
     for t in range(3):
         quant(r("nq%d" % t, 0, 128), r("ns%d" % t, 0, 128), r("xb", 0, 512))
     for k in range(3):
@@ -484,7 +562,7 @@ def rank_program(g, core, T, topo):
     copy("v", r("dnb", 0, 12), r("dt_", 0, 192, 16))
 
     def places(t):
-        copy("v", r("ndl", 0, 2), r("ndf", 0, 2))
+        copy("v", r("ndl", 0, 2), r("nd_", 0, 2))
         scatter(r("ol", 0, 256), r("ndl", 0, 2), r("od", 32 * t, 32 * t + 32))
 
     def q32(i, b):
@@ -498,55 +576,57 @@ def rank_program(g, core, T, topo):
         mm(r("pf", 0, e1 - em), r("qu", 0, 128), r("su", 0, 128), r(gq, em, e1), r(gs, em, e1))
         copy("v", r("ea", e0, em), r("pe", 0, em - e0))
         copy("s", r("ea", em, e1), r("pf", 0, e1 - em))
-        if t:
-            copy("s", r("za", 0, 64), (r("ea", 0, W), r("of", oz, oz + 4)))
-            tt(r("zb", 0, 64), (r("ea", 0, W), r("of", oz + 4, oz + 8)), r("za", 0, 64), A.add)
-        tt(r("zc", 0, 64), (r("ea", 0, W), r("of", oz + 8, oz + 12)), r("zb", 0, 64), A.add)
-        tt(r("zd", 0, 64), r("zc", 0, 64), r("fz", 0, 64), A.subtract)
-        act(r("z", 0, 64), r("zd", 0, 64), F.Abs)
+        win = r("ea", 0, W) if t else r("ea", 0, 256)
+        copy("s", r("d1z", 0, 256, 4), (win, r("of", oz, oz + 4)))
+        copy("v", r("d1z", 1, 256, 4), (win, r("of", oz + 4, oz + 8)))
+        copy("v", r("d1z", 2, 256, 4), (win if t else r("est", 0, 1792), r("of", oz + 8, oz + 12)))
+        scan(r("zs", 0, 256), r("d0z", 0, 256), r("d1z", 0, 256), 0.0, A.mult, A.add)
+        act(r("z", 0, 64), r("zs", 3, 256, 4), F.Abs)
         exchange("z")
         tr(r("zt", 0, 64), r("z", 0, 64))
         ts(r("dd", 0, 64), r("z", 0, 64), col("zt", 0), A.subtract)
         act(r("dd", 64, 128), r("z", 0, 64), F.Identity, bias=col("zt", 32), scale=-1.0)
         for h in range(2):
-            o = 256 * h
-            for d in range(1, 4):
-                ts(r("mm_", o + 64 * d, o + 64 * d + 64), r("z", 64 * d, 64 * d + 64), col("zt", 32 * h), A.subtract, col("cf", 31 + d), A.is_gt)
+            o = 320 * h
             tt(r("mm_", o, o + 64), r("dd", 64 * h, 64 * h + 64), r("jj", 64 * h, 64 * h + 64), A.is_lt if h else A.is_gt)
-            if h == 0:
-                act(junk(7 + t), r("mm_", 0, 256), F.Copy, acc=col("rk", 0))
-                act(r("cx", 0, 32), C1024, F.Identity, bias=col("cf", 15), scale=col("rk", 0))
-        red(col("rk", 1), r("mm_", 256, 512))
-        ts(r("cx", 32, 64), C1024, col("rk", 1), A.mult, col("cf", 16), A.add)
-        tr(r("cr", 0, 64), r("cx", 0, 64))
-        ts(r("cl", 0, 64), r("cr", 0, 64), col("cf", 3), A.max, col("cf", 4), A.min)
+            for d in range(1, 4):
+                o2 = o + (0, 64, 160, 224)[d]
+                ts(r("mm_", o2, o2 + 64), r("z", 64 * d, 64 * d + 64), col("zt", 32 * h), A.subtract, col("cf", 31 + d), A.is_gt)
+            scan(r("cx", 160 * h, 160 * h + 160), r("mm_", o, o + 160), r("mm_", o + 160, o + 320), col("cf", 15 + h), A.add, A.add)
+            tr(r("cr", 32 * h, 32 * h + 32), r("cx", 160 * h + 128, 160 * h + 160))
+        ts(r("cl", 0, 64), r("cr", 0, 64), col("cf", 1), A.max, col("cf", 4), A.min)
+        ts(r("cl", 64, 128), r("cr", 0, 64), col("cf", 2), A.max, col("cf", 6), A.min)
+        act(r("junk", 1792, 1856), r("cl", 0, 64), F.Copy, scale=1024.0, acc=col("sa_", 0))
         act(r("cl", 128, 192), r("cr", 0, 64), F.Relu, bias=col("cf", 7))
-        ts(r("cl", 64, 128), r("cr", 0, 64), col("cf", 5), A.max, col("cf", 6), A.min)
-        act(r("cl", 192, 256), r("cl", 128, 192), F.Relu, bias=col("cf", 35), scale=-1.0, acc=col("sw_", 2))
-        red(col("sw_", 0), r("cl", 0, 64))
-        red(col("sw_", 1), r("cl", 64, 128))
-        exchange("sw_", 3)
-        red(col("sel", 0), r("sw_", 0, 12, 3))
-        ts(r("so", 0, 6), r("soc", 0, 6), col("sel", 0), A.add)
+        act(r("junk", 1856, 1920), r("cl", 64, 128), F.Copy, scale=1024.0, acc=col("sb_", 0))
+        act(r("cl", 192, 256), r("cl", 128, 192), F.Relu, bias=col("cf", 35), scale=-1024.0, acc=col("sb_", 1))
+        for a in range(4):
+            copy("vs"[a % 2], blk("sa_", 1, 2, a), blk("sa_", 0, 1, (a + 1) % 4))
+        PRE = r("sel", 16, 22)
+        ts(PRE, SOC, col("sa_", 0), A.add, col("sa_", 1), A.add)
+        act(r("sa_", 2, 3, 1, 0, 64), r("sa_", 0, 1, 1, 64, 128), F.Identity, bias=r("sa_", 1, 2, 1, 64, 128))
+        ts(r("sa_", 2, 3, 1, 64, 128), r("sa_", 0, 1, 1, 0, 64), r("sa_", 1, 2, 1, 0, 64), A.add)
+        ts(r("so", 0, 6), PRE, col("sa_", 2), A.add)
         copy("v", r("ng", 0, 96), (r("nl", 0, 1536), r("so", 0, 6)))
         tr(r("nt", 0, 96), r("ng", 0, 96))
         copy("v", r("po", 0, 6), r("nt", 0, 96, 16))
-        act(r("sel", 4, 8), r("sw_", 1, 12, 3), F.Copy, acc=col("sel", 1))
-        act(r("sel", 8, 12), r("sw_", 2, 12, 3), F.Copy, acc=col("sel", 2))
+        exchange("sb_", 2)
+        act(r("sel", 4, 8), r("sb_", 0, 8, 2), F.Copy, acc=col("sel", 1))
+        act(r("sel", 8, 12), r("sb_", 1, 8, 2), F.Copy, acc=col("sel", 2))
         act(col("sel", 12), col("sel", 1), F.Identity, bias=col("cf", 29))
         act(col("sel", 13), col("sel", 2), F.Identity, bias=col("cf", 30), scale=-1.0)
-        nd, na = r("ndg", 0, 2) if t % 2 else r("ndg", 2, 4), "nda%d" % t
+        nd, na = r("nd_", 4 + 2 * (t % 2), 6 + 2 * (t % 2)), "nda%d" % t
         act(nd, r("sel", 12, 14), F.Copy, scale=THIRD)
         if t < 2:
             send_all(nd, lambda d: r(na, 2 * rank, 2 * rank + 2), "an%d" % t, [r(na, 2 * s, 2 * s + 2) for s in peers])
             dma([("y", r(na, 2 * rank, 2 * rank + 2), nd)])
-        act(r("ndf", 0, 2), nd, F.Copy, bias=-256.0 * rank)
+        act(r("nd_", 0, 2), nd, F.Copy, bias=-256.0 * rank)
         nq, ns = "nq%d" % t, "ns%d" % t
         pick(r(nq, 0, 96), r(ns, 0, 96), r(gq, 0, W), r(gs, 0, W), r("po", 0, 6))
         for b in range(4):
             mm(r("ps", 512 * b, 512 * b + 128), r("qa", 128 * b, 128 * b + 128), r("sa", 128 * b, 128 * b + 128), r(nq, 0, 128), r(ns, 0, 128))
         for c in range(2):
-            ts(r("bo", c, 8, 2), r("c4q", 0, 4), col("ndf", c), A.add, 4.0, A.mult)
+            ts(r("bo", c, 8, 2), r("kk", 18, 22), col("nd_", c), A.add, 4.0, A.mult)
         copy("s", r("bbs", 0, 128), (r("bb_t", 0, 1024), r("bo", 0, 8)))
         for b in range(4):
             copy("s", q32(0, b), r("ps", 512 * b, 512 * b + 32))
@@ -564,15 +644,15 @@ def rank_program(g, core, T, topo):
             nq, ns, at = "g%d" % (t + 1), "h%d" % (t + 1), W + 224
             quant(r(nq, at, at + 128), r(ns, at, at + 128), r("xt", 0, 512))
             for n, arr in ((nq, "ac%d" % (t + 1)), (ns, "as%d" % (t + 1))):
-                send_all(r(n, at, at + 32), lambda d: r(n, *slot(d, 32, W)), arr, [r(n, W, at)])
+                send_all(r(n, at, at + 32), lambda d: r(n, *slot(d, 32, W)), arr, [r(n, W, at)], 1.2)
         quant(r("ow", o0, o0 + 128), r("os_", o0, o0 + 128), r("xt", 0, 512))
         if t == 0:
-            iota(r("np1", 0, 2048), [[0, 2048]], 0, 0)
             dma([("y", r("g1", 0, NEW0), r("g0", 0, NEW0)), ("y", r("h1", 0, NEW0), r("h0", 0, NEW0))])
             dma([("y", r("g2", 0, NEW0), r("g0", 0, NEW0)), ("y", r("h2", 0, NEW0), r("h0", 0, NEW0))])
             ts(r("ndv", 256, 512), r("ndv", 0, 256), 256.0, A.add)
-        ts(col("ndo", t), col("sel", 0), col("cf", 12), A.add, THIRD, A.mult)
-        dma([("y", T.nd[t:t + 1, 0:32], r("ndo", t, t + 1, 1, 0, 32))])
+        ts(col("sel", 0), col("sa_", 0), col("sa_", 1), A.add, col("sa_", 2), A.add)
+        ts(col("nd_", 8 + t), col("sel", 0), col("cf", 12), A.add, THIRD, A.mult)
+        dma([("y", T.nd[t:t + 1, 0:32], r("nd_", 8 + t, 9 + t, 1, 0, 32))])
         if t < 2:
             places(t)
         if t == 1:
@@ -582,14 +662,16 @@ def rank_program(g, core, T, topo):
             ts(r("frf", 0, 16), r("frf", 0, 16), 224, A.bitwise_and)
             ts(r("d8", 0, 16), r("frf", 0, 16), col("cf", 1), A.add)
         if t < 2:
-            npn = r("np%d" % t, 0, 2048)
+            npn = r("np0", 0, 2048)
             copy("v", r("nai", 0, 16), r(na, 0, 16))
             scatter(npn, r("nai", 0, 16), r("ndv", 256 * t, 256 * t + 256))
             tt(r("db", 0, 192), (npn, r("dnb", 0, 12)), r("db", 0, 192), A.max)
             tr(r("dt_", 0, 192), r("db", 0, 192))
             copy("v", r("of", 12 * t + 12, 12 * t + 24), r("dt_", 0, 192, 16))
-            tt(r("nl", 0, 768), (npn, r("nbt", 0, 48)), r("nl", 0, 768), A.max)
-            copy("s", r("nl", 768, 1536), r("nl", 0, 768))
+            for i in range(0, 48, 8):
+                tt(r("nl", 16 * i, 16 * i + 128), (npn, r("nbt", i, i + 8)), r("nl", 16 * i, 16 * i + 128), A.max)
+            for i in range(0, 768, 256):
+                copy("s", r("nl", 768 + i, 1024 + i), r("nl", i, i + 256))
 
     tr(r("ogt", 0, 256), r("og", 0, 256))
     copy("v", r("oo", 0, 16), r("ogt", 0, 256, 16))

@@ -11,8 +11,28 @@ C05 = 13421773 * 2.0 ** -28
 THIRD = float(np.float32(1.0) / np.float32(3.0))
 KC = 1024 * 255
 TINY = 2.0 ** -110
-WAKE, SLACK, SLIP = 0.15, 0.3, 0.1
 CYC, HOLD, FLY, FIRST, LOAD = 0.001, 0.25, 2.4, 2.0, 2.2
+ORDER = """
+21 282 14 15 4 11 12 7 1 6 10 5 13 0 3 9 2 8 16 20 36 28 22 37 27 30 29 272 31 35 84 200 32 39 23 34 209 33 41 211 38 108 44 292 17 110
+46 124 40 127 45 50 18 291 47 42 288 135 256 109 125 48 19 43 111 128 289 112 287 49 290 210 126 188 129 113 52 51 136 114 53 55 56 116
+54 57 122 58 144 115 117 60 217 185 118 186 64 59 187 63 25 119 61 67 153 148 131 66 137 68 271 69 138 62 70 73 71v 72s 205 183 139 24
+74 75 195 65 79 218 184 77 189 81 76 78 190 83 86 132 147 82 80 130 145 85 93 146 87s 88v 90 89 206 94 92v 91s 95 401 98 97 101 99 102
+216 96 100 104 106 140 105 103 107 123 227 141 120 212 150 191 149 121 142 235 228 276 219 143 229 236 196 249 226v 202 151 284 230 199
+232 152 197 250 198 273 165 158s 251 166s 160s 233 167s 162 164s 163 161s 154 159 156s 155 168 234 157s 224 170 231 169 213 204 252 283
+201 220 172s 277 171 257 237 174 253 178 258 181s 26 259 175s 238 179s 254 177s 182 260 173s 180v 223 176v 203 261 214 264 263 262 304
+266 265 305 208 269 306s 239 221 312 308s 270 309 267 307 240 241s 314 310 268 274 311 242 313 316 322 245s 318 243s 315 244 225 323 246
+324 248 317 321 247s 319 207 255 325 320 275 298 133 222 326 280 134 327 279v 329 333 334 215 192 335s 336v 330 339 328 338 337 278 285
+340 193 332 331 341 347 344 345 346s 342 296 349 348s 343 360 359 399 351 350 281 353 361 352 293 363 354 528 286 368 362 357 355 358
+370 372 364 297 366 356 369 374 301 299 365 371 402 380 375 294 373 367 377 378 376 379 300 405 384 381 382 386 295 385 383 387 302 388
+303 406 194 389 394 398 400 391 390 392 407 403 408 529 417 409 410 414 527 413 421 526 393 411 404 422 397 423 395 416 424 425v 427s
+426s 412 428 530 415 429 436 432s 431 433v 430s 437 438 434s 440 435 445 420 439 441 442 418 446 448 447 443 419 449 444 450 451 454 452
+453 456 458v 457s 459s 460v 463 461 462 455 464 468s 470 469v 471v 465s 473v 472s 466 521 474 475 467 522 476 483 484 477 485 478 488
+479 482 481 396 523 492 486 489 480 495 487 496 493 501 490 494 503 497 498 499 510 491 500 502 504 506 511 508 505 507 509 512 513 517
+518 515 514 516 531 532 533 537 540 534 535 536 545 539 546 547 519 541 548 550 551s 549 538 542 552 544v 553 560 557 554s 555v 556s 562
+561 559 570 558s 563 543 569 571 572 566 565 564 573 567 574 568 575 578 576 577 580 582v 581s 583s 584v 579 587 585 586 592 594s 593v
+595 588 597 596 589 599 598 590 601 639 600 591 524 602 604 605 525 603 520 608 625 609 626 615 606 616 620 607 635 610 611 622 623 640
+624 613 612v 614 633 617 631 618 634 619 621 642 627 629 632 628 630 643 636 637 644 645 638 648 651 652 647 649 641 646 650 653
+"""
 CODE, U8, BF, F32, I32, U16 = "float8_e4m3fn_x4", "uint8", "bfloat16", "float32", "int32", "uint16"
 
 
@@ -20,18 +40,18 @@ def _sbuf(dtype, **cols):
     return {n: ("sbuf", [128, c], dtype) for n, c in cols.items()}
 
 
-SCRATCH = {"pe": ("psum", [128, 512], F32), "pf": ("psum", [128, 512], F32), "ps": ("psum", [128, 2048], F32)}
+SCRATCH = {"pe": ("psum", [128, 512], F32), "pf": ("psum", [128, 512], F32), "ps": ("psum", [128, 2048], F32), "py": ("psum", [128, 512], F32)}
 SCRATCH.update(_sbuf(F32, nbf=768, iot=2048, jr=256, jf=256, cf=64, jo=6, ka=256, kat=64, junk=2560, cq=1024, cz=512, ac=32, fa=28,
                      sp=192, ex=768, cc=128, lo=16, ea=1104, fn=256, z=256, zt=64, dd=128, jj=128, zs=256, d0z=256, d1z=256, cx=320, cr=64,
                      cl=256, sa_=4, sb_=8, sel=24, kk=264, ng=96, nt=96, nd_=12, bbs=128, sc4=512, nda0=16, nda1=16,
                      np0=2048, ndv=512, nl=1536, db=192, dbz=192, dt_=192, dtz=192, ol=256, od=96, og=256, ogt=256, yt=256,
-                     ep=2, er=14, es=448, est=1792))
-SCRATCH.update(_sbuf(I32, nb32=48, ci=16, fi=16, frf=256, gi=24))
-SCRATCH.update(_sbuf(U16, nbt=48, far16=16, pm=16, lst=4, rl=24, rl2=128, rep=24, so=6, po=6, ndl=2, nai=16, bo=8, dbt=12, dnb=12, of=36, frt=4, d8=16, oo=16))
-SCRATCH.update(_sbuf(BF, xb=1024, bb_t=1024, at=2048, wt=512, u4=4, v4=4, ones=128, ub=512, vb=512, mm_=640, xt=512))
+                     ep=2, er=14, es=448, est=480, fz=256, d0r=448, d1r=448, zr=448, rl=32, rl2=96, lst=4, yw=352))
+SCRATCH.update(_sbuf(I32, nb32=48, ci=16, fi=16, frf=256, gi=128))
+SCRATCH.update(_sbuf(U16, nbt=48, far16=16, pm=16, rep=24, so=6, po=6, ndl=2, nai=16, bo=8, dbt=12, dnb=12, of=36, frt=36, d8=16, oo=16))
+SCRATCH.update(_sbuf(BF, xb=1024, bb_t=1024, at=2048, wt=512, u4=4, v4=4, ub=512, vb=512, mm_=640, xt=512))
 for _c, _s, _n in (("qx", "sx", 256), ("qb", "sb", 256), ("qu", "su", 128), ("qv", "sv", 128), ("qa", "sa", 512), ("qw", "sw", 128), ("slc", "sls", 336),
                    ("g0", "h0", 592), ("g1", "h1", 944), ("g2", "h2", 1200), ("nq0", "ns0", 128), ("nq1", "ns1", 128), ("nq2", "ns2", 128),
-                   ("ow", "os_", 640), ("occ", "ocs", 256)):
+                   ("ow", "os_", 448), ("occ", "ocs", 256)):
     SCRATCH.update({_c: ("sbuf", [128, _n], CODE), _s: ("sbuf", [128, _n], U8)})
 SEMAPHORES = ["cv", "cs", "ct", "cg"] + ["q%d" % i for i in range(60)] + ["aer", "arl", "ac0", "as0", "an0", "an1", "ac1", "as1", "ac2", "as2"]
 
@@ -87,14 +107,14 @@ def rank_program(g, core, T, topo):
         for x in reads:
             log.setdefault(x[0], []).append((x, span(x), 0, i, q))
 
-    def put(q, fn, reads, writes, cost, late=0.0, sem=None, inc=1, deps=()):
+    def put(q, fn, reads, writes, cost, late=0.0, sem=None, inc=1, deps=(), alt=False):
         i = len(ops)
-        ops.append({"q": q, "fn": fn, "deps": meets(reads, writes, q) | set(deps), "cost": cost, "late": late, "sem": sem, "inc": inc, "users": [], "peers": [i]})
+        ops.append({"q": q, "fn": fn, "deps": meets(reads, writes, q) | set(deps), "cost": cost, "late": late, "sem": sem, "inc": inc, "alt": alt, "peers": [i]})
         note(q, reads, writes, i)
         return i
 
-    def emit(q, fn, reads, writes, cycles, fixed=0.0, deps=()):
-        put(q, fn, reads, writes, fixed + max(64, cycles) * CYC, deps=deps)
+    def emit(q, fn, reads, writes, cycles, fixed=0.0, deps=(), alt=False):
+        put(q, fn, reads, writes, fixed + max(64, cycles) * CYC, deps=deps, alt=alt)
 
     def width(x):
         return -(-(x[2] - x[1]) // x[3])
@@ -104,57 +124,10 @@ def rank_program(g, core, T, topo):
             for k in list(o["deps"]):
                 o["deps"] |= set(ops[k]["peers"])
             o["deps"].discard(i)
-            for k in o["deps"]:
-                ops[k]["users"].append(i)
-        for o in reversed(ops):
-            o["rank"] = o["cost"] + o["late"] + max([WAKE + ops[k]["rank"] for k in o["users"]] or [0])
-        left = [len(o["deps"]) for o in ops]
-        ready = {q: [] for q in "vstgyr"}
-        clock = {q: 0.0 for q in ready}
-        todo = {q: {i for i, o in enumerate(ops) if o["q"] == q} for q in ready}
-        for i, o in enumerate(ops):
-            o["est"] = 0.0
-            if not left[i]:
-                ready[o["q"]].append(i)
-        out, done, low = [], [False] * len(ops), [0.0] * len(ops)
-
-        def soonest():
-            for i, o in enumerate(ops):
-                if not done[i]:
-                    low[i] = max([o["est"]] + [low[k] + ops[k]["cost"] + ops[k]["late"] + WAKE for k in o["deps"] if not done[k]])
-
-        stamp = [-1]
-        while any(ready.values()):
-            best, spare = None, None
-            for q, l in ready.items():
-                if not l:
-                    continue
-                est = {i: max(clock[q], ops[i]["est"]) for i in l}
-                t0 = min(est.values())
-                for c in sorted(l, key=lambda i: (est[i] > t0 + 0.001, -ops[i]["rank"] if est[i] <= t0 + 0.001 else est[i])):
-                    if spare is None or est[c] < spare[0]:
-                        spare = (est[c], c)
-                    if best is not None and est[c] >= best[0]:
-                        break
-                    if stamp[0] != len(out):
-                        soonest()
-                        stamp[0] = len(out)
-                    if q != "r" and any(low[j] < est[c] + ops[c]["cost"] - SLIP and ops[j]["rank"] > ops[c]["rank"] + SLACK for j in todo[q]):
-                        continue
-                    best = (est[c], c)
-                    break
-            t, i = best or spare
-            o = ops[i]
-            ready[o["q"]].remove(i)
-            todo[o["q"]].discard(i)
-            done[i] = True
-            clock[o["q"]] = t + o["cost"]
-            out.append(i)
-            for k in o["users"]:
-                left[k] -= 1
-                ops[k]["est"] = max(ops[k]["est"], t + o["cost"] + o["late"] + WAKE)
-                if not left[k]:
-                    ready[ops[k]["q"]].append(k)
+        out = [int(x.rstrip("vs")) for x in ORDER.split()] or list(range(len(ops)))
+        for x in ORDER.split():
+            if x[-1] in "vs":
+                ops[int(x[:-1])]["q"] = x[-1]
         tok = {}
         for i in out:
             o = ops[i]
@@ -176,7 +149,7 @@ def rank_program(g, core, T, topo):
                 s = snaps.setdefault(tok[i], {})
                 for n, m in known[q].items():
                     s[n] = max(s.get(n, 0), m)
-                c = o["fn"]()
+                c = o["fn"](q) if o["alt"] else o["fn"]()
                 if o["sem"] is None:
                     c.then_inc(T.sem[sem], 1)
 
@@ -198,10 +171,14 @@ def rank_program(g, core, T, topo):
     def copy(q, out, in_):
         i, rd = src(in_)
         n = width(out) * by(in_)
-        if q == "v":
-            emit(q, lambda: g.vector.tensor_copy(ap(out), i), rd, [out], n)
-        else:
-            emit(q, lambda: g.scalar.activation(ap(out), i, F.Copy), rd, [out], n)
+        names = [out[0]] + [x[0] for x in rd]
+        flex = all(SCRATCH[k][0] == "sbuf" and SCRATCH[k][2] in (F32, BF) for k in names[:2])
+        fns = {"v": lambda: g.vector.tensor_copy(ap(out), i), "s": lambda: g.scalar.activation(ap(out), i, F.Copy)}
+        emit(q, (lambda e: fns[e]()) if flex else fns[q], rd, [out], n, alt=flex)
+
+    def times(out, in_, c):
+        fns = {"v": lambda: g.vector.tensor_scalar(ap(out), ap(in_), ap(c), None, A.mult), "s": lambda: g.scalar.activation(ap(out), ap(in_), F.Copy, scale=ap(c))}
+        emit("v", lambda e: fns[e](), [in_, c], [out], width(out), alt=True)
 
     def scatter(win, off, in_):
         emit("v", lambda: g.vector.tensor_copy(ap(win).indirect(ap(off)), ap(in_)), [in_, off], [win], 3 * width(in_))
@@ -377,15 +354,17 @@ def rank_program(g, core, T, topo):
     fill(CM128, -128.0)
     tr(r("kat", 0, 64), r("ka", 0, 64))
     tt(r("jo", 4, 6), r("jo", 2, 4), r("kat", 0, 64, 32), A.subtract)
-    act(junk(0), r("ka", 0, 256), F.Identity, bias=col("jo", 4))
-    ts(junk(6), r("ka", 0, 256), col("jo", 5), A.add)
+    ts(junk(0), r("ka", 0, 256), col("jo", 4), A.add)
+    act(junk(6), r("ka", 0, 256), F.Sign, bias=col("kat", 32), scale=-1.0, acc=col("ac", 1))
+    ts(col("ac", 17), col("kat", 32), -0.5, A.add)
+    act(junk(8), r("ka", 0, 256), F.Sign, bias=col("ac", 17), scale=-1.0, acc=col("ac", 18))
     ts(r("fa", 0, 2), r("jo", 4, 6), -1.0, A.mult)
     ts(r("fa", 2, 4), r("jo", 4, 6), 0.5, A.add)
     least(col("ac", 0), junk(0))
     copy("v", r("fi", 0, 2), r("fa", 0, 2))
-    least(col("ac", 1), junk(6))
     ts(r("fi", 2, 4), r("fi", 0, 2), 255, A.bitwise_and)
-    tt(r("ac", 6, 8), r("ac", 0, 2), r("jo", 2, 4), A.not_equal)
+    tt(col("ac", 6), col("ac", 0), col("jo", 2), A.not_equal)
+    ts(col("ac", 7), col("ac", 1), col("ac", 18), A.subtract, 1.0, A.not_equal)
     copy("v", r("fa", 4, 6), r("fi", 2, 4))
     ts(r("sp", 0, 32), C4096, col("ac", 6), A.mult, col("fa", 0), A.add)
     act(r("sp", 32, 64), C4096, F.Identity, bias=col("fa", 1), scale=col("ac", 7))
@@ -409,23 +388,23 @@ def rank_program(g, core, T, topo):
     ts(r("lo", 3, 6), r("lo", 0, 3), col("cf", 19), A.add)
     ts(r("lo", 11, 14), r("lo", 3, 6), 256.0, A.add)
     ts(r("cf", 21, 24), r("lo", 3, 6), -255.0, A.mult, -32512.0, A.add)
-    sums = [col("ac", 16)]
-    for c in range(3):
+    ts(col("lo", 14), col("lo", 3), -1.0, A.mult)
+    ts(col("lo", 15), col("lo", 3), 33024.0, A.add)
+    act(junk(5), CR2, F.Relu, bias=col("lo", 14))
+    act(r("cq", 0, 256), junk(5), F.Relu, bias=256.0, scale=-1.0, acc=col("ac", 16))
+    for c in (1, 2):
         ts(r("cq", 256 * c, 256 * c + 256), CR2, col("lo", 3 + c), A.max, col("lo", 11 + c), A.min)
-    act(junk(5), r("cq", 0, 256), F.Copy, acc=sums[0])
-    for c in range(1, 3):
-        sums.append(total(c, "cq", 256 * c))
-    for c in range(3):
-        ts(col("lst", c), sums[c], col("cf", 21 + c), A.add, 255.0, A.min)
+    act(col("lst", 0), col("ac", 16), F.Identity, bias=col("lo", 15), scale=-1.0)
+    for c in (1, 2):
+        ts(col("lst", c), total(c, "cq", 256 * c), col("cf", 21 + c), A.add)
 
     def slot(d, w, base=0):
         q = base + w * ((rank - d - 1) % 8)
         return q, q + w
 
     quant(r("qx", 0, 256), r("sx", 0, 256), r("xb", 0, 1024))
-    fill(r("ones", 0, 128), 1.0)
     for i in range(4):
-        ts(r("ub", i, 512, 4), r("ones", 0, 128), col("u4", i), A.mult)
+        act(r("ub", i, 512, 4), r("iot", 0, 128), F.Identity, bias=col("u4", i), scale=0.0)
     quant(r("qu", 0, 128), r("su", 0, 128), r("ub", 0, 512))
     for h in range(2):
         mm(r("ps", 512 * h, 512 * h + 128), r("qx", 128 * h, 128 * h + 128), r("sx", 128 * h, 128 * h + 128), r("qu", 0, 128), r("su", 0, 128))
@@ -442,45 +421,57 @@ def rank_program(g, core, T, topo):
         copy("s", r("nbf", 16 * i, 16 * i + 192), (r("iot", 0, 2048), r("nbt", i, i + 12)))
     ts(col("cf", 25), col("cf", 1), 3.0, A.mult)
     ts(r("dbt", 0, 12), r("kk", 6, 18), col("cf", 25), A.add)
-    copy("v", r("dbz", 0, 192), (r("nbf", 0, 768), r("dbt", 0, 12)))
-    tr(r("dtz", 0, 192), r("dbz", 0, 192))
+    ts(r("ci", 7, 8), r("ci", 3, 4), 10.0, A.add)
+    ts(r("ci", 8, 9), r("ci", 7, 8), 15, A.bitwise_and)
+    copy("v", col("cf", 43), r("ci", 8, 9))
+    ts(col("cf", 45), col("cf", 1), col("cf", 2), A.subtract, col("cf", 43), A.add)
+    lin(col("cf", 46), col("cf", 45), 3.0, 0.0)
+    ts(r("frt", 12, 20), r("kk", 6, 14), col("cf", 46), A.add)
+    copy("v", r("dbz", 0, 128), (r("nbf", 0, 768), r("frt", 12, 20)))
+    tr(r("dtz", 0, 128), r("dbz", 0, 128))
     ts(r("of", 0, 8), r("dtz", 0, 128, 16), -256.0 * rank, A.add)
-    ts(r("gi", 0, 4), r("dtz", 128, 192, 16), 2048.0 - 256.0 * (rank + 1), A.add)
-    ts(r("gi", 4, 8), r("gi", 0, 4), 2, A.arith_shift_right, 480, A.bitwise_and)
-    ts(r("gi", 8, 12), r("gi", 0, 4), 127, A.bitwise_and)
-    ts(col("cf", 42), col("cf", 26), -0.5, A.mult, 128.0, A.add)
-    ts(r("gi", 12, 16), r("gi", 8, 12), col("cf", 42), A.add)
-    ts(r("gi", 16, 20), r("gi", 12, 16), 127, A.bitwise_and)
-    ts(r("gi", 20, 24), r("gi", 12, 16), 5, A.arith_shift_right, 3, A.bitwise_and)
-    tt(r("fa", 16, 20), r("gi", 4, 8), r("gi", 16, 20), A.add)
-    ts(r("fa", 20, 24), r("gi", 20, 24), 416.0, A.mult)
-    tt(r("fa", 24, 28), r("fa", 16, 20), r("fa", 20, 24), A.add)
-    copy("v", r("of", 8, 12), r("fa", 24, 28))
+    ts(r("gi", 0, 16), r("kk", 218, 264, 3), 2048.0 - 256.0 * (rank + 1), A.add)
+    ts(r("gi", 16, 32), r("gi", 0, 16), 2, A.arith_shift_right, 480, A.bitwise_and)
+    ts(r("gi", 32, 48), r("gi", 0, 16), 31, A.bitwise_and)
+    ts(r("gi", 48, 64), r("gi", 0, 16), 96, A.bitwise_and)
+    lin(col("cf", 49), col("cf", 26), 0.5, 0.0)
+    tt(r("gi", 64, 80), r("gi", 16, 32), r("gi", 32, 48), A.add)
+    ts(r("gi", 80, 96), r("gi", 48, 64), col("cf", 49), A.not_equal, 1024.0, A.mult)
+    tt(r("gi", 96, 112), r("gi", 64, 80), r("gi", 80, 96), A.add)
+    ts(r("frt", 20, 36), r("gi", 96, 112), 448.0, A.min)
 
     fill(CONE, 1.0)
     for c in range(14):
         o = r("es", 32 * c, 32 * c + 32)
-        if c % 2:
-            ts(o, CONE, col("er", c), A.mult)
-        else:
-            act(o, CONE, F.Copy, scale=col("er", c))
-    tr(r("est", 0, 448), r("es", 0, 448))
-    mv = []
-    for d in range(1, 4):
-        mv.append(("y", r("est", 448 * d, 448 * d + 448, 1, 0, 128 - 32 * d), r("est", 0, 448, 1, 32 * d, 128)))
-        mv.append(("y", r("est", 448 * d, 448 * d + 448, 1, 128 - 32 * d, 128), r("est", 0, 448, 1, 0, 32 * d)))
-    dma(mv, LOAD + 1.2)
+        times(o, CONE, col("er", c))
+    const(r("est", 448, 480), 0.0)
+    for h in range(0, 448, 224):
+        tr(r("est", h, h + 224), r("es", h, h + 224))
+    copy("s", r("d1r", 2, 448, 7), (r("est", 0, 480), r("frt", 20, 24)))
+    copy("v", r("fz", 64, 256), (r("est", 0, 480), r("frt", 24, 36)))
+    for d in (1, 3):
+        for a in range(4):
+            copy("vs"[a % 2], r("d1r", 2 + d, 448, 7, 32 * a, 32 * a + 32), blk("fz", 64 * (4 - d), 64 * (4 - d) + 64, (a + d) % 4))
+    copy("v", r("d1r", 4, 448, 7, 0, 64), r("fz", 128, 192, 1, 64, 128))
+    copy("s", r("d1r", 4, 448, 7, 64, 128), r("fz", 128, 192, 1, 0, 64))
 
     for h in range(2):
         quant(r("qb", 128 * h, 128 * h + 128), r("sb", 128 * h, 128 * h + 128), r("bb_t", 512 * h, 512 * h + 512))
     for i in range(4):
-        ts(r("vb", i, 512, 4), r("ones", 0, 128), col("v4", i), A.mult)
+        act(r("vb", i, 512, 4), r("iot", 0, 128), F.Identity, bias=col("v4", i), scale=0.0)
     quant(r("qv", 0, 128), r("sv", 0, 128), r("vb", 0, 512))
     mm(r("pf", 0, 256), r("qv", 0, 128), r("sv", 0, 128), r("qb", 0, 256), r("sb", 0, 256))
     copy("s", r("fn", 0, 256), r("pf", 0, 256))
     ts(col("cf", 27), col("cf", 26), col("cf", 2), A.add)
     ts(r("frt", 0, 4), r("iot", 0, 64, 16), col("cf", 27), A.add)
     act(r("d1z", 3, 256, 4), (r("fn", 0, 256), r("frt", 0, 4)), F.Copy, scale=-1.0)
+    lin(col("cf", 47), col("cf", 43), 1.0, col("cf", 26))
+    ts(r("frt", 4, 8), r("iot", 0, 64, 16), col("cf", 47), A.add)
+    act(r("d1r", 6, 448, 7), (r("fn", 0, 256), r("frt", 4, 8)), F.Copy, scale=-1.0)
+    copy("s", r("d1r", 0, 448, 7), (r("ea", 0, 256), r("of", 0, 4)))
+    copy("v", r("d1r", 1, 448, 7), (r("ea", 0, 256), r("of", 4, 8)))
+    const(r("d0r", 0, 448), 1.0)
+    act(r("d0r", 0, 448, 7), r("iot", 0, 64), F.Copy, scale=0.0)
     const(r("d0z", 0, 256), 1.0)
     act(r("d0z", 0, 256, 4), r("iot", 0, 64), F.Copy, scale=0.0)
     for i in range(4):
@@ -519,35 +510,36 @@ def rank_program(g, core, T, topo):
     tt(r("ac", 10, 12), r("ac", 8, 10), r("ac", 4, 6), A.subtract)
     ts(r("ac", 12, 14), r("ac", 10, 12), 0.5, A.mult)
     tt(r("ac", 14, 16), r("ac", 12, 14), r("fa", 14, 16), A.add)
-    ts(r("sp", 128, 160), CONE, col("ac", 14), A.mult)
-    act(r("sp", 160, 192), CONE, F.Copy, scale=col("ac", 15))
+    for h in range(2):
+        times(r("sp", 128 + 32 * h, 160 + 32 * h), CONE, col("ac", 14 + h))
     tr(r("ex", 512, 576), r("sp", 128, 192))
     exchange("ex", 64, 512)
     ts(r("ci", 5, 6), r("ci", 2, 3), 3.0, A.mult, 2.0, A.add)
     ts(r("ci", 6, 7), r("ci", 5, 6), 15, A.bitwise_and)
     copy("v", col("cf", 41), r("ci", 6, 7))
+    lin(col("cf", 48), col("cf", 41), 7.0, 6.0)
+    ts(r("frt", 8, 12), r("iot", 0, 448, 112), col("cf", 48), A.add)
     ts(r("pm", 0, 16), r("iot", 0, 256, 16), col("cf", 41), A.add)
     copy("s", r("nl", 2, 768, 3), (FL, r("pm", 0, 16)))
-    fill(r("rl2", 0, 128), 0)
 
-    copy("v", r("rl2", 0, 21), r("rl", 0, 21))
-    tr(r("rl2", 32, 64), r("rl2", 0, 32))
-    o = 32 + 16 * (rank % 2)
-    copy("v", r("rl2", 64, 80), r("rl2", o, o + 16))
-    copy("v", r("rl2", 80, 96), r("rl2", o, o + 16))
-    tr(r("rl2", 96, 128), r("rl2", 64, 96))
+    dma([("y", r("rl", 21, 32), r("iot", 0, 11))])
+    tr(r("rl2", 0, 32), r("rl", 0, 32))
+    o = 16 * (rank % 2)
+    for i in (32, 48):
+        ts(r("rl2", i, i + 16), r("rl2", o, o + 16), 255.0, A.min)
+    tr(r("rl2", 64, 96), r("rl2", 32, 64))
     for a in range(4):
-        copy("v", blk("rep", 0, 21, a), blk("rl2", 96, 117, rank // 2))
+        copy("v", blk("rep", 0, 21, a), blk("rl2", 64, 85, rank // 2))
     pick(r("slc", 0, 336), r("sls", 0, 336), r("qx", 0, 256), r("sx", 0, 256), r("rep", 0, 21))
     for s, l, arr in (("slc", "g0", "ac0"), ("sls", "h0", "as0")):
         send_each([(d, r(s, LC * i, LC * i + LC), r(l, *slot(d, LC, FAR0))) for i, d in enumerate(peers)], arr, [r(l, FAR0, NEW0)])
     w0 = 32 * ((rank + 1) % 8)
-    iota(r("ndv", w0, 256), [[1, 256 - w0]], NEW0, 0)
-    if w0:
-        iota(r("ndv", 0, w0), [[1, w0]], NEW0 + 256 - w0, 0)
+    w1 = w0 or 128
+    iota(r("ndv", w1, 256), [[1, 256 - w1]], NEW0 + w1 - w0, 0)
+    iota(r("ndv", 0, w1), [[1, w1]], NEW0 + (256 - w0) % 256, 0)
     for i in range(4):
         iota(r("np0", 512 * i, 512 * i + 512), [[0, 512]], 0, 0, after=[asked])
-    iota(r("od", 0, 96), [[128, 3], [1, 32]], P, 0)
+    iota(r("od", 0, 96), [[1, 96]], P, 0)
 
     for i in range(0, 768, 256):
         copy("s", r("nl", 768 + i, 1024 + i), r("nl", i, i + 256))
@@ -555,8 +547,10 @@ def rank_program(g, core, T, topo):
     fill(r("xt", 0, 512), 0.0)
     for b in range(4):
         quant(r("qa", 128 * b, 128 * b + 128), r("sa", 128 * b, 128 * b + 128), r("at", 512 * b, 512 * b + 512))
-    for t in range(3):
-        quant(r("nq%d" % t, 0, 128), r("ns%d" % t, 0, 128), r("xb", 0, 512))
+    dma([("y", r(n % t, 96, 128), r(s, 0, 32)) for t in range(3) for n, s in (("nq%d", "qx"), ("ns%d", "sx"))])
+    quant(r("qw", 0, 128), r("sw", 0, 128), r("wt", 0, 512))
+    mm(r("py", 0, 256), r("qw", 0, 128), r("sw", 0, 128), r("qx", 0, 256), r("sx", 0, 256))
+    copy("s", r("yw", 0, 256), r("py", 0, 256))
     for k in range(3):
         tr(r("dt_", 64 * k, 64 * k + 64), r("nbf", k, 192, 3))
     copy("v", r("dnb", 0, 12), r("dt_", 0, 192, 16))
@@ -574,14 +568,16 @@ def rank_program(g, core, T, topo):
         em = (e0 + e1) // 2
         mm(r("pe", 0, em - e0), r("qu", 0, 128), r("su", 0, 128), r(gq, e0, em), r(gs, e0, em))
         mm(r("pf", 0, e1 - em), r("qu", 0, 128), r("su", 0, 128), r(gq, em, e1), r(gs, em, e1))
-        copy("v", r("ea", e0, em), r("pe", 0, em - e0))
+        copy("v" if t else "s", r("ea", e0, em), r("pe", 0, em - e0))
         copy("s", r("ea", em, e1), r("pf", 0, e1 - em))
-        win = r("ea", 0, W) if t else r("ea", 0, 256)
-        copy("s", r("d1z", 0, 256, 4), (win, r("of", oz, oz + 4)))
-        copy("v", r("d1z", 1, 256, 4), (win, r("of", oz + 4, oz + 8)))
-        copy("v", r("d1z", 2, 256, 4), (win if t else r("est", 0, 1792), r("of", oz + 8, oz + 12)))
-        scan(r("zs", 0, 256), r("d0z", 0, 256), r("d1z", 0, 256), 0.0, A.mult, A.add)
-        act(r("z", 0, 64), r("zs", 3, 256, 4), F.Abs)
+        if t:
+            for k in range(3):
+                copy("svv"[k], r("d1z", k, 256, 4), (r("ea", 0, W), r("of", oz + 4 * k, oz + 4 * k + 4)))
+            scan(r("zs", 0, 256), r("d0z", 0, 256), r("d1z", 0, 256), 0.0, A.mult, A.add)
+            act(r("z", 0, 64), r("zs", 3, 256, 4), F.Abs)
+        else:
+            scan(r("zr", 0, 448), r("d0r", 0, 448), r("d1r", 0, 448), 0.0, A.mult, A.add)
+            act(r("z", 0, 64), (r("zr", 0, 448), r("frt", 8, 12)), F.Abs)
         exchange("z")
         tr(r("zt", 0, 64), r("z", 0, 64))
         ts(r("dd", 0, 64), r("z", 0, 64), col("zt", 0), A.subtract)
@@ -639,17 +635,22 @@ def rank_program(g, core, T, topo):
             tt(r("xt", b, 128, 4), q32(3, b), r("bbs", 32 * b, 32 * b + 32), A.add)
         if t == 2:
             copy("s", r("og", 0, 256), (r("ol", 0, 256), r("d8", 0, 16)))
-        o0 = P + 128 * t
+        o0 = P + 32 * t
         if t < 2:
             nq, ns, at = "g%d" % (t + 1), "h%d" % (t + 1), W + 224
             quant(r(nq, at, at + 128), r(ns, at, at + 128), r("xt", 0, 512))
             for n, arr in ((nq, "ac%d" % (t + 1)), (ns, "as%d" % (t + 1))):
                 send_all(r(n, at, at + 32), lambda d: r(n, *slot(d, 32, W)), arr, [r(n, W, at)], 1.2)
-        quant(r("ow", o0, o0 + 128), r("os_", o0, o0 + 128), r("xt", 0, 512))
+            dma([("y", r("ow", o0, o0 + 32), r(nq, at, at + 32)), ("y", r("os_", o0, o0 + 32), r(ns, at, at + 32))])
+        else:
+            nq, ns, at = "ow", "os_", o0
+            quant(r(nq, at, at + 128), r(ns, at, at + 128), r("xt", 0, 512))
+        mm(r("py", 0, 128), r("qw", 0, 128), r("sw", 0, 128), r(nq, at, at + 128), r(ns, at, at + 128))
+        copy("s", r("yw", o0, o0 + 32), r("py", 0, 32))
         if t == 0:
             dma([("y", r("g1", 0, NEW0), r("g0", 0, NEW0)), ("y", r("h1", 0, NEW0), r("h0", 0, NEW0))])
             dma([("y", r("g2", 0, NEW0), r("g0", 0, NEW0)), ("y", r("h2", 0, NEW0), r("h0", 0, NEW0))])
-            ts(r("ndv", 256, 512), r("ndv", 0, 256), 256.0, A.add)
+            lin(r("ndv", 256, 512), r("ndv", 0, 256), 1.0, 256.0)
         ts(col("sel", 0), col("sa_", 0), col("sa_", 1), A.add, col("sa_", 2), A.add)
         ts(col("nd_", 8 + t), col("sel", 0), col("cf", 12), A.add, THIRD, A.mult)
         dma([("y", T.nd[t:t + 1, 0:32], r("nd_", 8 + t, 9 + t, 1, 0, 32))])
@@ -657,7 +658,6 @@ def rank_program(g, core, T, topo):
             places(t)
         if t == 1:
             dma([("y", r("g2", NEW0, NEW0 + 256), r("g1", NEW0, NEW0 + 256)), ("y", r("h2", NEW0, NEW0 + 256), r("h1", NEW0, NEW0 + 256))])
-            quant(r("qw", 0, 128), r("sw", 0, 128), r("wt", 0, 512))
             ts(r("frf", 0, 16), r("iot", 0, 256, 16), 0.0, A.add)
             ts(r("frf", 0, 16), r("frf", 0, 16), 224, A.bitwise_and)
             ts(r("d8", 0, 16), r("frf", 0, 16), col("cf", 1), A.add)
@@ -675,13 +675,11 @@ def rank_program(g, core, T, topo):
 
     tr(r("ogt", 0, 256), r("og", 0, 256))
     copy("v", r("oo", 0, 16), r("ogt", 0, 256, 16))
-    pick(r("occ", 0, 256), r("ocs", 0, 256), r("ow", 0, 640), r("os_", 0, 640), r("oo", 0, 16))
+    pick(r("occ", 0, 256), r("ocs", 0, 256), r("ow", 0, 352), r("os_", 0, 352), r("oo", 0, 16))
     dma([("y", T.oc[:], r("occ", 0, 256))])
     dma([("y", T.osc[4 * k:4 * k + 4, :], r("ocs", 0, 256, 1, 32 * k, 32 * k + 4)) for k in range(4)])
-    for h, ps in ((0, "pe"), (1, "pf")):
-        mm(r(ps, 0, 128), r("qw", 0, 128), r("sw", 0, 128), r("occ", 128 * h, 128 * h + 128), r("ocs", 128 * h, 128 * h + 128))
-    copy("v", r("yt", 0, 128), r("pe", 0, 128))
-    copy("s", r("yt", 128, 256), r("pf", 0, 128))
+    copy("v", r("yt", 0, 128), (r("yw", 0, 352), r("oo", 0, 8)))
+    copy("s", r("yt", 128, 256), (r("yw", 0, 352), r("oo", 8, 16)))
     dma([("s", T.y[:], r("yt", 0, 256))])
     flush()
     for sem, c in cnt.items():

import numpy as np
from concourse.bass import DstId, RemoteDMATransfer
from concourse.mybir import dt, AluOpType, AxisListType, ActivationFunctionType

A = AluOpType
F = ActivationFunctionType
P, K, R, LC = 256, 32, 3, 48
FAR0 = P
NEW0 = P + 7 * LC
C05 = 13421773 * 2.0 ** -28
THIRD = float(np.float32(1.0) / np.float32(3.0))
KC = 1024 * 255
TINY = 2.0 ** -110
CYC, HOLD, FLY, FIRST, LOAD = 0.001, 0.25, 2.4, 2.0, 2.2
ORDER = """
21 282 14 15 4 11 12 7 1 6 10 5 13 0 3 9 2 8 16 20 36 28 22 37 27 30 29 272 31 35 84 200 32 39 23 34 209 33 41 211 38 108 44 292 17 110
46 124 40 127 45 50 18 291 47 42 288 135 256 109 125 48 19 43 111 128 289 112 287 49 290 210 126 188 129 113 52 51 136 114 53 55 56 116
54 57 122 58 144 115 117 60 217 185 118 186 64 59 187 63 25 119 61 67 153 148 131 66 137 68 271 69 138 62 70 73 71v 72s 205 183 139 24
74 75 195 65 79 218 184 77 189 81 76 78 190 83 86 132 147 82 80 130 145 85 93 146 87s 88v 90 89 206 94 92v 91s 95 401 98 97 101 99 102
216 96 100 104 106 140 105 103 107 123 227 141 120 212 150 191 149 121 142 235 228 276 219 143 229 236 196 249 226v 202 151 284 230 199
232 152 197 250 198 273 165 158s 251 166s 160s 233 167s 162 164s 163 161s 154 159 156s 155 168 234 157s 224 170 231 169 213 204 252 283
201 220 172s 277 171 257 237 174 253 178 258 181s 26 259 175s 238 179s 254 177s 182 260 173s 180v 223 176v 203 261 214 264 263 262 304
266 265 305 208 269 306s 239 221 312 308s 270 309 267 307 240 241s 314 310 268 274 311 242 313 316 322 245s 318 243s 315 244 225 323 246
324 248 317 321 247s 319 207 255 325 320 275 298 133 222 326 280 134 327 279v 329 333 334 215 192 335s 336v 330 339 328 338 337 278 285
340 193 332 331 341 347 344 345 346s 342 296 349 348s 343 360 359 399 351 350 281 353 361 352 293 363 354 528 286 368 362 357 355 358
370 372 364 297 366 356 369 374 301 299 365 371 402 380 375 294 373 367 377 378 376 379 300 405 384 381 382 386 295 385 383 387 302 388
303 406 194 389 394 398 400 391 390 392 407 403 408 529 417 409 410 414 527 413 421 526 393 411 404 422 397 423 395 416 424 425v 427s
426s 412 428 530 415 429 436 432s 431 433v 430s 437 438 434s 440 435 445 420 439 441 442 418 446 448 447 443 419 449 444 450 451 454 452
453 456 458v 457s 459s 460v 463 461 462 455 464 468s 470 469v 471v 465s 473v 472s 466 521 474 475 467 522 476 483 484 477 485 478 488
479 482 481 396 523 492 486 489 480 495 487 496 493 501 490 494 503 497 498 499 510 491 500 502 504 506 511 508 505 507 509 512 513 517
518 515 514 516 531 532 533 537 540 534 535 536 545 539 546 547 519 541 548 550 551s 549 538 542 552 544v 553 560 557 554s 555v 556s 562
561 559 570 558s 563 543 569 571 572 566 565 564 573 567 574 568 575 578 576 577 580 582v 581s 583s 584v 579 587 585 586 592 594s 593v
595 588 597 596 589 599 598 590 601 639 600 591 524 602 604 605 525 603 520 608 625 609 626 615 606 616 620 607 635 610 611 622 623 640
624 613 612v 614 633 617 631 618 634 619 621 642 627 629 632 628 630 643 636 637 644 645 638 648 651 652 647 649 641 646 650 653
"""
CODE, U8, BF, F32, I32, U16 = "float8_e4m3fn_x4", "uint8", "bfloat16", "float32", "int32", "uint16"


def _sbuf(dtype, **cols):
    return {n: ("sbuf", [128, c], dtype) for n, c in cols.items()}


SCRATCH = {"pe": ("psum", [128, 512], F32), "pf": ("psum", [128, 512], F32), "ps": ("psum", [128, 2048], F32), "py": ("psum", [128, 512], F32)}
SCRATCH.update(_sbuf(F32, nbf=768, iot=2048, jr=256, jf=256, cf=64, jo=6, ka=256, kat=64, junk=2560, cq=1024, cz=512, ac=32, fa=28,
                     sp=192, ex=768, cc=128, lo=16, ea=1104, fn=256, z=256, zt=64, dd=128, jj=128, zs=256, d0z=256, d1z=256, cx=320, cr=64,
                     cl=256, sa_=4, sb_=8, sel=24, kk=264, ng=96, nt=96, nd_=12, bbs=128, sc4=512, nda0=16, nda1=16,
                     np0=2048, ndv=512, nl=1536, db=192, dbz=192, dt_=192, dtz=192, ol=256, od=96, og=256, ogt=256, yt=256,
                     ep=2, er=14, es=448, est=480, fz=256, d0r=448, d1r=448, zr=448, rl=32, rl2=96, lst=4, yw=352))
SCRATCH.update(_sbuf(I32, nb32=48, ci=16, fi=16, frf=256, gi=128))
SCRATCH.update(_sbuf(U16, nbt=48, far16=16, pm=16, rep=24, so=6, po=6, ndl=2, nai=16, bo=8, dbt=12, dnb=12, of=36, frt=36, d8=16, oo=16))
SCRATCH.update(_sbuf(BF, xb=1024, bb_t=1024, at=2048, wt=512, u4=4, v4=4, ub=512, vb=512, mm_=640, xt=512))
for _c, _s, _n in (("qx", "sx", 256), ("qb", "sb", 256), ("qu", "su", 128), ("qv", "sv", 128), ("qa", "sa", 512), ("qw", "sw", 128), ("slc", "sls", 336),
                   ("g0", "h0", 592), ("g1", "h1", 944), ("g2", "h2", 1200), ("nq0", "ns0", 128), ("nq1", "ns1", 128), ("nq2", "ns2", 128),
                   ("ow", "os_", 448), ("occ", "ocs", 256)):
    SCRATCH.update({_c: ("sbuf", [128, _n], CODE), _s: ("sbuf", [128, _n], U8)})
SEMAPHORES = ["cv", "cs", "ct", "cg"] + ["q%d" % i for i in range(60)] + ["aer", "arl", "ac0", "as0", "an0", "an1", "ac1", "as1", "ac2", "as2"]


def r(name, c0, c1, step=1, p0=0, p1=128):
    return (name, c0, c1, step, p0, p1)


def rank_program(g, core, T, topo):
    rank = T.rank_of(core)
    if rank is None:
        return
    eng = {"v": g.vector, "s": g.scalar, "t": g.tensor, "g": g, "y": g.sync}
    csem = {"v": "cv", "s": "cs", "t": "ct", "g": "cg"}
    cnt, known, log, pool, snaps, ops = {}, {q: {} for q in eng}, {}, [0], {}, []

    def ap(x):
        return T[x[0]][x[4]:x[5], x[1]:x[2]:x[3]] if x[3] != 1 else T[x[0]][x[4]:x[5], x[1]:x[2]]

    def span(x):
        if SCRATCH[x[0]][0] == "psum":
            return x[1] // 512 * 512, (x[2] + 511) // 512 * 512, 0, 128
        return x[1], x[2], x[4], x[5]

    def learn(q, tok):
        k, (sem, c) = known[q], tok
        if k.get(sem, 0) >= c:
            return
        k[sem] = c
        for n, m in snaps.get(tok, {}).items():
            if k.get(n, 0) < m:
                k[n] = m

    def clash(a, b):
        return not (a[3] == b[3] and a[3] > 1 and (a[1] - b[1]) % a[3])

    def meets(reads, writes, q):
        deps = set()
        for x, w in [(x, 0) for x in reads] + [(x, 1) for x in writes]:
            s = span(x)
            bank = SCRATCH[x[0]][0] == "psum"
            for y, t, w2, i, q2 in log.get(x[0], []):
                if (w or w2 or (bank and q2 != q)) and s[0] < t[1] and t[0] < s[1] and s[2] < t[3] and t[2] < s[3] and clash(x, y):
                    deps.add(i)
        return deps

    def note(q, reads, writes, i):
        for x in writes:
            s = span(x)
            if x[3] == 1:
                log[x[0]] = [e for e in log.get(x[0], []) if not (s[0] <= e[1][0] and e[1][1] <= s[1] and s[2] <= e[1][2] and e[1][3] <= s[3])]
            log.setdefault(x[0], []).append((x, s, 1, i, q))
        for x in reads:
            log.setdefault(x[0], []).append((x, span(x), 0, i, q))

    def put(q, fn, reads, writes, cost, late=0.0, sem=None, inc=1, deps=(), alt=False):
        i = len(ops)
        ops.append({"q": q, "fn": fn, "deps": meets(reads, writes, q) | set(deps), "cost": cost, "late": late, "sem": sem, "inc": inc, "alt": alt, "peers": [i]})
        note(q, reads, writes, i)
        return i

    def emit(q, fn, reads, writes, cycles, fixed=0.0, deps=(), alt=False):
        put(q, fn, reads, writes, fixed + max(64, cycles) * CYC, deps=deps, alt=alt)

    def width(x):
        return -(-(x[2] - x[1]) // x[3])

    def flush():
        for i, o in enumerate(ops):
            for k in list(o["deps"]):
                o["deps"] |= set(ops[k]["peers"])
            o["deps"].discard(i)
        out = [int(x.rstrip("vs")) for x in ORDER.split()] or list(range(len(ops)))
        for x in ORDER.split():
            if x[-1] in "vs":
                ops[int(x[:-1])]["q"] = x[-1]
        tok = {}
        for i in out:
            o = ops[i]
            q = o["q"]
            need = {}
            if q == "g" and o["sem"] is None and "cg" in cnt:
                need["cg"] = cnt["cg"]
            for k in o["deps"]:
                need[tok[k][0]] = max(need.get(tok[k][0], 0), tok[k][1])
            if q != "r":
                for sem, c in sorted(need.items(), key=lambda e: -sum(snaps.get(e, {}).values())):
                    if known[q].get(sem, 0) < c:
                        eng[q].wait_ge(T.sem[sem], c)
                        learn(q, (sem, c))
            sem = o["sem"] or csem[q]
            cnt[sem] = cnt.get(sem, 0) + 1 if o["sem"] is None else o["inc"]
            tok[i] = (sem, cnt[sem])
            if q != "r":
                s = snaps.setdefault(tok[i], {})
                for n, m in known[q].items():
                    s[n] = max(s.get(n, 0), m)
                c = o["fn"](q) if o["alt"] else o["fn"]()
                if o["sem"] is None:
                    c.then_inc(T.sem[sem], 1)

    def newsem():
        pool[0] += 1
        return "q%d" % (pool[0] - 1)

    def src(x):
        if len(x) == 2:
            return ap(x[0]).indirect(ap(x[1])), [x[0], x[1]]
        return ap(x), [x]

    def sc(x):
        return (ap(x), [x]) if isinstance(x, tuple) else (x, [])

    def by(in_):
        return 1.5 if len(in_) == 2 else 1

    def copy(q, out, in_):
        i, rd = src(in_)
        n = width(out) * by(in_)
        names = [out[0]] + [x[0] for x in rd]
        flex = all(SCRATCH[k][0] == "sbuf" and SCRATCH[k][2] in (F32, BF) for k in names[:2])
        fns = {"v": lambda: g.vector.tensor_copy(ap(out), i), "s": lambda: g.scalar.activation(ap(out), i, F.Copy)}
        emit(q, (lambda e: fns[e]()) if flex else fns[q], rd, [out], n, alt=flex)

    def times(out, in_, c):
        fns = {"v": lambda: g.vector.tensor_scalar(ap(out), ap(in_), ap(c), None, A.mult), "s": lambda: g.scalar.activation(ap(out), ap(in_), F.Copy, scale=ap(c))}
        emit("v", lambda e: fns[e](), [in_, c], [out], width(out), alt=True)

    def scatter(win, off, in_):
        emit("v", lambda: g.vector.tensor_copy(ap(win).indirect(ap(off)), ap(in_)), [in_, off], [win], 3 * width(in_))

    def act(out, in_, func, bias=0.0, scale=1.0, acc=None):
        i, rd = src(in_)
        b, rb = sc(bias)
        s, rs = sc(scale)
        n = width(out) * by(in_)
        if acc is None:
            emit("s", lambda: g.scalar.activation(ap(out), i, func, bias=b, scale=s), rd + rb + rs, [out], n)
        else:
            emit("s", lambda: g.scalar.activation(ap(out), i, func, bias=b, scale=s, accum_out=ap(acc)), rd + rb + rs, [out, acc], n)

    def const(out, val):
        act(out, r("iot", 0, width(out), 1, out[4], out[5]), F.Copy, bias=val, scale=0.0)

    def lin(out, in_, scale, bias):
        act(out, in_, F.Identity if isinstance(bias, tuple) else F.Copy, bias=bias, scale=scale)

    def ts(out, in_, s1, op0, s2=None, op1=None):
        i, rd = src(in_)
        a, ra = sc(s1)
        b, rb = sc(s2)
        if op1 is None:
            emit("v", lambda: g.vector.tensor_scalar(ap(out), i, a, None, op0), rd + ra, [out], width(out))
        else:
            emit("v", lambda: g.vector.tensor_scalar(ap(out), i, a, b, op0, op1), rd + ra + rb, [out], width(out))

    def tt(out, in0, in1, op):
        i, rd = src(in0)
        emit("v", lambda: g.vector.tensor_tensor(ap(out), i, ap(in1), op), rd + [in1], [out], (1.5 if len(in0) == 2 else 2) * width(out))

    def scan(out, d0, d1, initial, op0, op1):
        a, ra = sc(initial)
        emit("v", lambda: g.vector.tensor_tensor_scan(ap(out), ap(d0), ap(d1), a, op0, op1), [d0, d1] + ra, [out], width(out))

    def least(out, in_):
        emit("v", lambda: g.vector.tensor_reduce(ap(out), ap(in_), AxisListType.X, A.min, apply_absolute_value=True), [in_], [out], width(in_))

    def tr(out, in_):
        emit("v", lambda: g.vector.transpose(ap(out), ap(in_)), [in_], [out], width(out))

    def fill(out, val):
        emit("v", lambda: g.vector.memset(ap(out), val), [], [out], width(out))

    def quant(q, s, in_):
        emit("v", lambda: g.vector.quantize_mx(ap(q), ap(s), ap(in_)), [in_], [q, s], width(in_) // 4)

    def mm(out, wq, ws, xq, xs):
        emit("t", lambda: g.tensor.matmul_mx(ap(out), ap(wq), ap(ws), ap(xq), ap(xs), True, True), [wq, ws, xq, xs], [out], width(out))

    def iota(out, pattern, base, cm, flag=True, after=()):
        if flag:
            emit("g", lambda: g.iota(ap(out), pattern, base, cm, allow_small_or_imprecise_dtypes=True), [], [out], 2 * width(out), 0.13, after)
        else:
            emit("g", lambda: g.iota(ap(out), pattern, base, cm), [], [out], 2 * width(out), 0.13, after)

    def pick(qo, so, win, wins, off):
        emit("v", lambda: g.vector.tensor_copy(ap(qo).bitcast(dt.uint32), ap(win).bitcast(dt.uint32).indirect(ap(off))), [win, off], [qo], 1.5 * width(qo))
        emit("s", lambda: g.scalar.activation(ap(so), ap(wins).indirect(ap(off)), F.Copy), [wins, off], [so], 1.5 * width(so))

    def side(x):
        return ap(x).bitcast(dt.uint8) if SCRATCH[x[0]][2] == CODE else ap(x)

    def dma(moves, late=LOAD):
        sem = newsem()
        made = []
        for q, out, in_ in moves:
            wr = [out] if isinstance(out, tuple) else []
            rd = [in_] if isinstance(in_, tuple) else []
            o, i = side(out) if wr else out, side(in_) if rd else in_
            made.append(put(q, lambda q=q, o=o, i=i: eng[q].dma_start(o, i).then_inc(T.sem[sem], 16), rd, wr, 0.07, late, sem, 16 * len(moves)))
        for k in made:
            ops[k]["peers"] = made

    peers = [(rank + 1 + i) % 8 for i in range(7)]
    ids = {}
    for d in peers:
        rid, pid, _ = topo.addr(T.cores[d])
        ids[d] = DstId(rid=rid, pnc=pid)
    full = topo.engines(core, T.cores[peers[0]])
    across = [d for d in peers if topo.die(T.cores[d]) != topo.die(core)]
    masks = {}
    for d in peers:
        e = topo.engines(core, T.cores[d])
        lane = e[0::2] if d in across else e[1::2]
        k = (across if d in across else [s for s in peers if s not in across]).index(d)
        masks[d] = sum(1 << x for x in lane[2 * k:2 * k + 2])

    def issue(trs, reads, total):
        sem = newsem()
        return put("g", lambda: g.remote_dma_fused(trs, local_sem=T.sem[sem]), reads, [], HOLD, FLY - 0.5, sem, total)

    def send_each(moves, arr, regions):
        i = issue([RemoteDMATransfer(dst_ids=[ids[d]], dma_engine_mask=masks[d], remote_sem=T.sem[arr], srcs=[side(s)], dsts=[side(l)]) for d, s, l in moves],
                  [m[1] for m in moves], 2 * len(moves))
        put("r", None, [], regions, 0.0, 2.0, arr, 2 * 7, [i])

    def send_all(s, land, arr, regions, more=0.0):
        i = issue([RemoteDMATransfer(dst_ids=[ids[d] for d in peers], dma_engine_mask=sum(1 << x for x in full), remote_sem=T.sem[arr], srcs=[side(s)],
                                     dsts=[side(land(d)) for d in peers])], [s], len(full))
        put("r", None, [], regions, 0.0, 0.5 + more, arr, len(full) * 7, [i])
        return i

    def exchange(n, w=64, o=0):
        for a in range(4):
            b = (a + 1) % 4
            copy("vs"[a % 2], r(n, o + w, o + 2 * w, 1, 32 * a, 32 * a + 32), r(n, o, o + w, 1, 32 * b, 32 * b + 32))
        copy("v", r(n, o + 2 * w, o + 4 * w, 1, 0, 64), r(n, o, o + 2 * w, 1, 64, 128))
        copy("s", r(n, o + 2 * w, o + 4 * w, 1, 64, 128), r(n, o, o + 2 * w, 1, 0, 64))

    def col(n, c, w=1):
        return r(n, c, c + w)

    def blk(n, c0, c1, a):
        return r(n, c0, c1, 1, 32 * a, 32 * a + 32)

    def junk(i):
        return r("junk", 256 * i, 256 * i + 256)

    def total(i, x, c):
        scan(r("cz", 128 * i, 128 * i + 128), r(x, c, c + 128), r(x, c + 128, c + 256), 0.0, A.add, A.add)
        return col("cz", 128 * i + 127)

    mv = []
    for gr in range(8):
        a = gr // 2
        q = "ys"[gr % 2]
        mv.append((q, r("nb32", 0, 48 - 12 * a, 1, 16 * gr, 16 * gr + 16), T.nb[:, 12 * a:48]))
        if a:
            mv.append((q, r("nb32", 48 - 12 * a, 48, 1, 16 * gr, 16 * gr + 16), T.nb[:, 0:12 * a]))
    dma(mv)
    dma([("y", r("xb", 0, 1024), T.x[:])])
    dma([("s", r("u4", 0, 4), T.u[:, 0:4]), ("s", r("v4", 0, 4), T.v[:, 0:4])])
    dma([("y", r("bb_t", 0, 1024), T.bb[:])])
    dma([("y", r("at", 0, 2048), T.a[:])])
    dma([("y", r("wt", 0, 512), T.w[:])])

    C4096, CM128, C1024, CONE = r("cc", 0, 32), r("cc", 32, 64), r("cc", 64, 96), r("cc", 96, 128)
    iota(r("ci", 0, 1), [[0, 1]], 0, 1, False)
    iota(r("iot", 0, 256), [[1, 256]], 0, 0)
    iota(r("kk", 24, 72), [[0, 16], [1, 3]], 0, 0)
    iota(r("iot", 1536, 2048), [[1, 512]], 1536, 0)
    iota(r("lo", 8, 11), [[4096, 3]], 0, 0)
    iota(r("kk", 6, 18), [[1, 3], [96, 2], [0, 2]], 0, 0)
    iota(r("kk", 0, 6), [[1, 3], [0, 2]], 768, 0)
    ts(r("ci", 1, 2), r("ci", 0, 1), 31, A.bitwise_and)
    ts(r("ci", 2, 3), r("ci", 0, 1), 15, A.bitwise_and)
    copy("v", r("cf", 0, 3), r("ci", 0, 3))
    ts(r("ci", 3, 4), r("ci", 2, 3), 11.0, A.mult)
    ts(r("ci", 4, 5), r("ci", 3, 4), 5, A.arith_shift_right)
    ts(col("cf", 40), r("ci", 4, 5), -3.0, A.mult, col("cf", 2), A.add)
    ts(r("kk", 72, 120), r("kk", 24, 72), col("cf", 40), A.add, 2.0, A.is_equal)
    ts(r("kk", 120, 168), r("kk", 24, 72), 0.5, A.is_gt)
    ts(col("cf", 26), col("cf", 0), col("cf", 1), A.subtract, 2.0, A.mult)
    ts(r("iot", 256, 512), r("iot", 0, 256), 256.0, A.add)
    act(r("iot", 512, 1024), r("iot", 0, 512), F.Copy, bias=512.0)
    act(r("iot", 1024, 1536), r("iot", 0, 512), F.Copy, bias=1024.0)
    ts(r("frf", 0, 256), r("iot", 0, 256), col("cf", 26), A.add)
    tt(col("jo", 0), col("cf", 26), col("cf", 1), A.add)
    ts(r("frf", 0, 256), r("frf", 0, 256), 255, A.bitwise_and)
    ts(col("jo", 1), col("jo", 0), 32.0, A.add)
    ts(r("jo", 2, 4), r("jo", 0, 2), 1.0 / 512, A.mult)
    copy("v", r("jr", 0, 256), r("frf", 0, 256))
    lin(r("jf", 0, 256), r("jr", 0, 256), 1.0 / 512, 0.0)

    tt(r("kk", 168, 216), r("nb32", 0, 48), r("kk", 72, 120), A.mult)
    scan(r("kk", 216, 264), r("kk", 120, 168), r("kk", 168, 216), 0.0, A.mult, A.add)
    copy("v", r("far16", 0, 16), r("kk", 218, 264, 3))
    tt(r("ka", 0, 256), (r("iot", 0, 2048), r("far16", 0, 16)), r("jf", 0, 256), A.add)
    fill(C4096, 4096.0)
    fill(CM128, -128.0)
    tr(r("kat", 0, 64), r("ka", 0, 64))
    tt(r("jo", 4, 6), r("jo", 2, 4), r("kat", 0, 64, 32), A.subtract)
    ts(junk(0), r("ka", 0, 256), col("jo", 4), A.add)
    act(junk(6), r("ka", 0, 256), F.Sign, bias=col("kat", 32), scale=-1.0, acc=col("ac", 1))
    ts(col("ac", 17), col("kat", 32), -0.5, A.add)
    act(junk(8), r("ka", 0, 256), F.Sign, bias=col("ac", 17), scale=-1.0, acc=col("ac", 18))
    ts(r("fa", 0, 2), r("jo", 4, 6), -1.0, A.mult)
    ts(r("fa", 2, 4), r("jo", 4, 6), 0.5, A.add)
    least(col("ac", 0), junk(0))
    copy("v", r("fi", 0, 2), r("fa", 0, 2))
    ts(r("fi", 2, 4), r("fi", 0, 2), 255, A.bitwise_and)
    tt(col("ac", 6), col("ac", 0), col("jo", 2), A.not_equal)
    ts(col("ac", 7), col("ac", 1), col("ac", 18), A.subtract, 1.0, A.not_equal)
    copy("v", r("fa", 4, 6), r("fi", 2, 4))
    ts(r("sp", 0, 32), C4096, col("ac", 6), A.mult, col("fa", 0), A.add)
    act(r("sp", 32, 64), C4096, F.Identity, bias=col("fa", 1), scale=col("ac", 7))
    ts(col("cf", 17), col("cf", 0), col("cf", 2), A.subtract, 16.0, A.mult)
    tr(r("ex", 0, 64), r("sp", 0, 64))
    exchange("ex", 64, 0)
    FR, CR2, FL = r("ex", 0, 256), r("ex", 256, 512), r("ex", 512, 768)
    for h in range(2):
        act(junk(1 + h), FR, F.Sign, bias=col("fa", 2 + h), acc=col("ac", 4 + h))
    ts(r("cq", 768, 1024), FR, col("cf", 17), A.is_ge)
    ts(r("fa", 6, 8), r("ac", 6, 8), 1048576.0, A.mult)
    below = total(3, "cq", 768)
    tt(r("fa", 8, 10), r("fa", 6, 8), r("fa", 4, 6), A.add)
    ts(r("sp", 64, 96), CM128, col("ac", 4), A.mult, col("fa", 8), A.add)
    act(r("sp", 96, 128), CM128, F.Identity, bias=col("fa", 9), scale=col("ac", 5))
    ts(col("cf", 18), col("cf", 2), 256.0, A.mult)
    tr(r("ex", 256, 320), r("sp", 64, 128))
    ts(r("lo", 0, 3), r("lo", 8, 11), col("cf", 18), A.add, 32768.0, A.add)
    exchange("ex", 64, 256)
    ts(col("cf", 19), below, -256.0, A.mult)
    ts(r("lo", 3, 6), r("lo", 0, 3), col("cf", 19), A.add)
    ts(r("lo", 11, 14), r("lo", 3, 6), 256.0, A.add)
    ts(r("cf", 21, 24), r("lo", 3, 6), -255.0, A.mult, -32512.0, A.add)
    ts(col("lo", 14), col("lo", 3), -1.0, A.mult)
    ts(col("lo", 15), col("lo", 3), 33024.0, A.add)
    act(junk(5), CR2, F.Relu, bias=col("lo", 14))
    act(r("cq", 0, 256), junk(5), F.Relu, bias=256.0, scale=-1.0, acc=col("ac", 16))
    for c in (1, 2):
        ts(r("cq", 256 * c, 256 * c + 256), CR2, col("lo", 3 + c), A.max, col("lo", 11 + c), A.min)
    act(col("lst", 0), col("ac", 16), F.Identity, bias=col("lo", 15), scale=-1.0)
    for c in (1, 2):
        ts(col("lst", c), total(c, "cq", 256 * c), col("cf", 21 + c), A.add)

    def slot(d, w, base=0):
        q = base + w * ((rank - d - 1) % 8)
        return q, q + w

    quant(r("qx", 0, 256), r("sx", 0, 256), r("xb", 0, 1024))
    for i in range(4):
        act(r("ub", i, 512, 4), r("iot", 0, 128), F.Identity, bias=col("u4", i), scale=0.0)
    quant(r("qu", 0, 128), r("su", 0, 128), r("ub", 0, 512))
    for h in range(2):
        mm(r("ps", 512 * h, 512 * h + 128), r("qx", 128 * h, 128 * h + 128), r("sx", 128 * h, 128 * h + 128), r("qu", 0, 128), r("su", 0, 128))
        copy("s", col("ep", h), col("ps", 512 * h))
    send_all(r("ep", 0, 2), lambda d: r("er", *slot(d, 2)), "aer", [r("er", 0, 14)], FIRST)
    asked = send_all(r("lst", 0, 3), lambda d: r("rl", *slot(d, 3)), "arl", [r("rl", 0, 21)])
    mm(r("pe", 0, 256), r("qu", 0, 128), r("su", 0, 128), r("qx", 0, 256), r("sx", 0, 256))
    copy("s", r("ea", 0, 256), r("pe", 0, 256))
    dma([("y", r("g0", 0, 256), r("qx", 0, 256)), ("y", r("h0", 0, 256), r("sx", 0, 256))])
    dma([("y", r("ow", 0, 256), r("qx", 0, 256)), ("y", r("os_", 0, 256), r("sx", 0, 256))])

    copy("v", r("nbt", 0, 48), r("nb32", 0, 48))
    for i in range(0, 48, 12):
        copy("s", r("nbf", 16 * i, 16 * i + 192), (r("iot", 0, 2048), r("nbt", i, i + 12)))
    ts(col("cf", 25), col("cf", 1), 3.0, A.mult)
    ts(r("dbt", 0, 12), r("kk", 6, 18), col("cf", 25), A.add)
    ts(r("ci", 7, 8), r("ci", 3, 4), 10.0, A.add)
    ts(r("ci", 8, 9), r("ci", 7, 8), 15, A.bitwise_and)
    copy("v", col("cf", 43), r("ci", 8, 9))
    ts(col("cf", 45), col("cf", 1), col("cf", 2), A.subtract, col("cf", 43), A.add)
    lin(col("cf", 46), col("cf", 45), 3.0, 0.0)
    ts(r("frt", 12, 20), r("kk", 6, 14), col("cf", 46), A.add)
    copy("v", r("dbz", 0, 128), (r("nbf", 0, 768), r("frt", 12, 20)))
    tr(r("dtz", 0, 128), r("dbz", 0, 128))
    ts(r("of", 0, 8), r("dtz", 0, 128, 16), -256.0 * rank, A.add)
    ts(r("gi", 0, 16), r("kk", 218, 264, 3), 2048.0 - 256.0 * (rank + 1), A.add)
    ts(r("gi", 16, 32), r("gi", 0, 16), 2, A.arith_shift_right, 480, A.bitwise_and)
    ts(r("gi", 32, 48), r("gi", 0, 16), 31, A.bitwise_and)
    ts(r("gi", 48, 64), r("gi", 0, 16), 96, A.bitwise_and)
    lin(col("cf", 49), col("cf", 26), 0.5, 0.0)
    tt(r("gi", 64, 80), r("gi", 16, 32), r("gi", 32, 48), A.add)
    ts(r("gi", 80, 96), r("gi", 48, 64), col("cf", 49), A.not_equal, 1024.0, A.mult)
    tt(r("gi", 96, 112), r("gi", 64, 80), r("gi", 80, 96), A.add)
    ts(r("frt", 20, 36), r("gi", 96, 112), 448.0, A.min)

    fill(CONE, 1.0)
    for c in range(14):
        o = r("es", 32 * c, 32 * c + 32)
        times(o, CONE, col("er", c))
    const(r("est", 448, 480), 0.0)
    for h in range(0, 448, 224):
        tr(r("est", h, h + 224), r("es", h, h + 224))
    copy("s", r("d1r", 2, 448, 7), (r("est", 0, 480), r("frt", 20, 24)))
    copy("v", r("fz", 64, 256), (r("est", 0, 480), r("frt", 24, 36)))
    for d in (1, 3):
        for a in range(4):
            copy("vs"[a % 2], r("d1r", 2 + d, 448, 7, 32 * a, 32 * a + 32), blk("fz", 64 * (4 - d), 64 * (4 - d) + 64, (a + d) % 4))
    copy("v", r("d1r", 4, 448, 7, 0, 64), r("fz", 128, 192, 1, 64, 128))
    copy("s", r("d1r", 4, 448, 7, 64, 128), r("fz", 128, 192, 1, 0, 64))

    for h in range(2):
        quant(r("qb", 128 * h, 128 * h + 128), r("sb", 128 * h, 128 * h + 128), r("bb_t", 512 * h, 512 * h + 512))
    for i in range(4):
        act(r("vb", i, 512, 4), r("iot", 0, 128), F.Identity, bias=col("v4", i), scale=0.0)
    quant(r("qv", 0, 128), r("sv", 0, 128), r("vb", 0, 512))
    mm(r("pf", 0, 256), r("qv", 0, 128), r("sv", 0, 128), r("qb", 0, 256), r("sb", 0, 256))
    copy("s", r("fn", 0, 256), r("pf", 0, 256))
    ts(col("cf", 27), col("cf", 26), col("cf", 2), A.add)
    ts(r("frt", 0, 4), r("iot", 0, 64, 16), col("cf", 27), A.add)
    act(r("d1z", 3, 256, 4), (r("fn", 0, 256), r("frt", 0, 4)), F.Copy, scale=-1.0)
    lin(col("cf", 47), col("cf", 43), 1.0, col("cf", 26))
    ts(r("frt", 4, 8), r("iot", 0, 64, 16), col("cf", 47), A.add)
    act(r("d1r", 6, 448, 7), (r("fn", 0, 256), r("frt", 4, 8)), F.Copy, scale=-1.0)
    copy("s", r("d1r", 0, 448, 7), (r("ea", 0, 256), r("of", 0, 4)))
    copy("v", r("d1r", 1, 448, 7), (r("ea", 0, 256), r("of", 4, 8)))
    const(r("d0r", 0, 448), 1.0)
    act(r("d0r", 0, 448, 7), r("iot", 0, 64), F.Copy, scale=0.0)
    const(r("d0z", 0, 256), 1.0)
    act(r("d0z", 0, 256, 4), r("iot", 0, 64), F.Copy, scale=0.0)
    for i in range(4):
        const(r("mm_", 160 * i + 128, 160 * i + 160), 0.0)
    const(col("cf", 35), 1024.0)
    const(r("cf", 32, 35), 0.0)
    const(r("cf", 32, 33, 1, 96, 128), -TINY)
    const(r("cf", 33, 34, 1, 64, 128), -TINY)
    const(r("cf", 34, 35, 1, 64, 128), -TINY)
    const(r("cf", 34, 35, 1, 32, 64), -TINY)
    lin(col("cf", 4), col("cf", 1), 1.0, 1.0)
    lin(col("cf", 6), col("cf", 2), 1.0, 1.0)
    lin(col("cf", 7), col("cf", 2), -1.0, -16.0)
    lin(col("cf", 12), col("cf", 1), -float(KC), -float(KC))
    lin(r("cf", 15, 17), r("jo", 0, 2), 3.0 / 1024, 0.0)
    ts(r("jj", 0, 64), r("jr", 0, 64), col("jo", 0), A.is_lt, -TINY, A.mult)
    ts(r("jj", 64, 128), r("jr", 0, 64), col("jo", 1), A.is_lt, TINY, A.mult)
    lin(col("cf", 28), col("cf", 26), -3.0, col("cf", 12))
    SOC = r("kk", 0, 6)
    lin(SOC, SOC, 1.0, col("cf", 28))
    lin(col("cf", 29), col("cf", 2), -float(KC), 768.0 * rank - KC)
    lin(col("cf", 30), col("cf", 2), 1024.0, 768.0 * rank + 17 * 1024)
    lin(r("kk", 18, 22), r("iot", 0, 4), 0.25, 0.0)
    copy("s", r("ol", 0, 256), r("iot", 0, 256))

    ts(r("fi", 4, 6), r("fi", 0, 2), 8, A.arith_shift_right)
    copy("v", r("fa", 10, 12), r("fi", 4, 6))
    ts(r("fa", 12, 14), r("fa", 10, 12), -256.0, A.mult, 0.5, A.add)
    for h in range(2):
        act(junk(3 + h), FR, F.Sign, bias=col("fa", 12 + h), acc=col("ac", 8 + h))
    ts(r("fi", 6, 8), r("fi", 4, 6), float(7 - rank), A.add)
    ts(r("fi", 8, 10), r("fi", 6, 8), 7, A.bitwise_and)
    ts(r("fa", 14, 16), r("fi", 8, 10), float(LC), A.mult, float(FAR0), A.add)
    for k in range(2):
        lin(r("nl", k, 768, 3), r("nbf", k, 768, 3), 1.0, -256.0 * rank)
    tt(r("ac", 10, 12), r("ac", 8, 10), r("ac", 4, 6), A.subtract)
    ts(r("ac", 12, 14), r("ac", 10, 12), 0.5, A.mult)
    tt(r("ac", 14, 16), r("ac", 12, 14), r("fa", 14, 16), A.add)
    for h in range(2):
        times(r("sp", 128 + 32 * h, 160 + 32 * h), CONE, col("ac", 14 + h))
    tr(r("ex", 512, 576), r("sp", 128, 192))
    exchange("ex", 64, 512)
    ts(r("ci", 5, 6), r("ci", 2, 3), 3.0, A.mult, 2.0, A.add)
    ts(r("ci", 6, 7), r("ci", 5, 6), 15, A.bitwise_and)
    copy("v", col("cf", 41), r("ci", 6, 7))
    lin(col("cf", 48), col("cf", 41), 7.0, 6.0)
    ts(r("frt", 8, 12), r("iot", 0, 448, 112), col("cf", 48), A.add)
    ts(r("pm", 0, 16), r("iot", 0, 256, 16), col("cf", 41), A.add)
    copy("s", r("nl", 2, 768, 3), (FL, r("pm", 0, 16)))

    dma([("y", r("rl", 21, 32), r("iot", 0, 11))])
    tr(r("rl2", 0, 32), r("rl", 0, 32))
    o = 16 * (rank % 2)
    for i in (32, 48):
        ts(r("rl2", i, i + 16), r("rl2", o, o + 16), 255.0, A.min)
    tr(r("rl2", 64, 96), r("rl2", 32, 64))
    for a in range(4):
        copy("v", blk("rep", 0, 21, a), blk("rl2", 64, 85, rank // 2))
    pick(r("slc", 0, 336), r("sls", 0, 336), r("qx", 0, 256), r("sx", 0, 256), r("rep", 0, 21))
    for s, l, arr in (("slc", "g0", "ac0"), ("sls", "h0", "as0")):
        send_each([(d, r(s, LC * i, LC * i + LC), r(l, *slot(d, LC, FAR0))) for i, d in enumerate(peers)], arr, [r(l, FAR0, NEW0)])
    w0 = 32 * ((rank + 1) % 8)
    w1 = w0 or 128
    iota(r("ndv", w1, 256), [[1, 256 - w1]], NEW0 + w1 - w0, 0)
    iota(r("ndv", 0, w1), [[1, w1]], NEW0 + (256 - w0) % 256, 0)
    for i in range(4):
        iota(r("np0", 512 * i, 512 * i + 512), [[0, 512]], 0, 0, after=[asked])
    iota(r("od", 0, 96), [[1, 96]], P, 0)

    for i in range(0, 768, 256):
        copy("s", r("nl", 768 + i, 1024 + i), r("nl", i, i + 256))
    copy("v", r("db", 0, 192), (r("nl", 0, 768), r("dbt", 0, 12)))
    fill(r("xt", 0, 512), 0.0)
    for b in range(4):
        quant(r("qa", 128 * b, 128 * b + 128), r("sa", 128 * b, 128 * b + 128), r("at", 512 * b, 512 * b + 512))
    dma([("y", r(n % t, 96, 128), r(s, 0, 32)) for t in range(3) for n, s in (("nq%d", "qx"), ("ns%d", "sx"))])
    quant(r("qw", 0, 128), r("sw", 0, 128), r("wt", 0, 512))
    mm(r("py", 0, 256), r("qw", 0, 128), r("sw", 0, 128), r("qx", 0, 256), r("sx", 0, 256))
    copy("s", r("yw", 0, 256), r("py", 0, 256))
    for k in range(3):
        tr(r("dt_", 64 * k, 64 * k + 64), r("nbf", k, 192, 3))
    copy("v", r("dnb", 0, 12), r("dt_", 0, 192, 16))

    def places(t):
        copy("v", r("ndl", 0, 2), r("nd_", 0, 2))
        scatter(r("ol", 0, 256), r("ndl", 0, 2), r("od", 32 * t, 32 * t + 32))

    def q32(i, b):
        return r("sc4", 128 * i + 32 * b, 128 * i + 32 * b + 32)

    for t in range(R):
        gq, gs, W, oz = "g%d" % t, "h%d" % t, NEW0 + 256 * t, 12 * t
        e0, e1 = (W - 256, W) if t else (FAR0, NEW0)
        em = (e0 + e1) // 2
        mm(r("pe", 0, em - e0), r("qu", 0, 128), r("su", 0, 128), r(gq, e0, em), r(gs, e0, em))
        mm(r("pf", 0, e1 - em), r("qu", 0, 128), r("su", 0, 128), r(gq, em, e1), r(gs, em, e1))
        copy("v" if t else "s", r("ea", e0, em), r("pe", 0, em - e0))
        copy("s", r("ea", em, e1), r("pf", 0, e1 - em))
        if t:
            for k in range(3):
                copy("svv"[k], r("d1z", k, 256, 4), (r("ea", 0, W), r("of", oz + 4 * k, oz + 4 * k + 4)))
            scan(r("zs", 0, 256), r("d0z", 0, 256), r("d1z", 0, 256), 0.0, A.mult, A.add)
            act(r("z", 0, 64), r("zs", 3, 256, 4), F.Abs)
        else:
            scan(r("zr", 0, 448), r("d0r", 0, 448), r("d1r", 0, 448), 0.0, A.mult, A.add)
            act(r("z", 0, 64), (r("zr", 0, 448), r("frt", 8, 12)), F.Abs)
        exchange("z")
        tr(r("zt", 0, 64), r("z", 0, 64))
        ts(r("dd", 0, 64), r("z", 0, 64), col("zt", 0), A.subtract)
        act(r("dd", 64, 128), r("z", 0, 64), F.Identity, bias=col("zt", 32), scale=-1.0)
        for h in range(2):
            o = 320 * h
            tt(r("mm_", o, o + 64), r("dd", 64 * h, 64 * h + 64), r("jj", 64 * h, 64 * h + 64), A.is_lt if h else A.is_gt)
            for d in range(1, 4):
                o2 = o + (0, 64, 160, 224)[d]
                ts(r("mm_", o2, o2 + 64), r("z", 64 * d, 64 * d + 64), col("zt", 32 * h), A.subtract, col("cf", 31 + d), A.is_gt)
            scan(r("cx", 160 * h, 160 * h + 160), r("mm_", o, o + 160), r("mm_", o + 160, o + 320), col("cf", 15 + h), A.add, A.add)
            tr(r("cr", 32 * h, 32 * h + 32), r("cx", 160 * h + 128, 160 * h + 160))
        ts(r("cl", 0, 64), r("cr", 0, 64), col("cf", 1), A.max, col("cf", 4), A.min)
        ts(r("cl", 64, 128), r("cr", 0, 64), col("cf", 2), A.max, col("cf", 6), A.min)
        act(r("junk", 1792, 1856), r("cl", 0, 64), F.Copy, scale=1024.0, acc=col("sa_", 0))
        act(r("cl", 128, 192), r("cr", 0, 64), F.Relu, bias=col("cf", 7))
        act(r("junk", 1856, 1920), r("cl", 64, 128), F.Copy, scale=1024.0, acc=col("sb_", 0))
        act(r("cl", 192, 256), r("cl", 128, 192), F.Relu, bias=col("cf", 35), scale=-1024.0, acc=col("sb_", 1))
        for a in range(4):
            copy("vs"[a % 2], blk("sa_", 1, 2, a), blk("sa_", 0, 1, (a + 1) % 4))
        PRE = r("sel", 16, 22)
        ts(PRE, SOC, col("sa_", 0), A.add, col("sa_", 1), A.add)
        act(r("sa_", 2, 3, 1, 0, 64), r("sa_", 0, 1, 1, 64, 128), F.Identity, bias=r("sa_", 1, 2, 1, 64, 128))
        ts(r("sa_", 2, 3, 1, 64, 128), r("sa_", 0, 1, 1, 0, 64), r("sa_", 1, 2, 1, 0, 64), A.add)
        ts(r("so", 0, 6), PRE, col("sa_", 2), A.add)
        copy("v", r("ng", 0, 96), (r("nl", 0, 1536), r("so", 0, 6)))
        tr(r("nt", 0, 96), r("ng", 0, 96))
        copy("v", r("po", 0, 6), r("nt", 0, 96, 16))
        exchange("sb_", 2)
        act(r("sel", 4, 8), r("sb_", 0, 8, 2), F.Copy, acc=col("sel", 1))
        act(r("sel", 8, 12), r("sb_", 1, 8, 2), F.Copy, acc=col("sel", 2))
        act(col("sel", 12), col("sel", 1), F.Identity, bias=col("cf", 29))
        act(col("sel", 13), col("sel", 2), F.Identity, bias=col("cf", 30), scale=-1.0)
        nd, na = r("nd_", 4 + 2 * (t % 2), 6 + 2 * (t % 2)), "nda%d" % t
        act(nd, r("sel", 12, 14), F.Copy, scale=THIRD)
        if t < 2:
            send_all(nd, lambda d: r(na, 2 * rank, 2 * rank + 2), "an%d" % t, [r(na, 2 * s, 2 * s + 2) for s in peers])
            dma([("y", r(na, 2 * rank, 2 * rank + 2), nd)])
        act(r("nd_", 0, 2), nd, F.Copy, bias=-256.0 * rank)
        nq, ns = "nq%d" % t, "ns%d" % t
        pick(r(nq, 0, 96), r(ns, 0, 96), r(gq, 0, W), r(gs, 0, W), r("po", 0, 6))
        for b in range(4):
            mm(r("ps", 512 * b, 512 * b + 128), r("qa", 128 * b, 128 * b + 128), r("sa", 128 * b, 128 * b + 128), r(nq, 0, 128), r(ns, 0, 128))
        for c in range(2):
            ts(r("bo", c, 8, 2), r("kk", 18, 22), col("nd_", c), A.add, 4.0, A.mult)
        copy("s", r("bbs", 0, 128), (r("bb_t", 0, 1024), r("bo", 0, 8)))
        for b in range(4):
            copy("s", q32(0, b), r("ps", 512 * b, 512 * b + 32))
        for k, b in ((1, 0), (1, 1), (2, 0), (1, 2), (2, 1), (1, 3), (2, 2), (2, 3)):
            tt(q32(k, b), q32(k - 1, b), r("ps", 512 * b + 32 * k, 512 * b + 32 * k + 32), A.add)
        if t == 2:
            places(t)
        for b in range(4):
            act(q32(3, b), q32(2, b), F.Copy, scale=C05)
            tt(r("xt", b, 128, 4), q32(3, b), r("bbs", 32 * b, 32 * b + 32), A.add)
        if t == 2:
            copy("s", r("og", 0, 256), (r("ol", 0, 256), r("d8", 0, 16)))
        o0 = P + 32 * t
        if t < 2:
            nq, ns, at = "g%d" % (t + 1), "h%d" % (t + 1), W + 224
            quant(r(nq, at, at + 128), r(ns, at, at + 128), r("xt", 0, 512))
            for n, arr in ((nq, "ac%d" % (t + 1)), (ns, "as%d" % (t + 1))):
                send_all(r(n, at, at + 32), lambda d: r(n, *slot(d, 32, W)), arr, [r(n, W, at)], 1.2)
            dma([("y", r("ow", o0, o0 + 32), r(nq, at, at + 32)), ("y", r("os_", o0, o0 + 32), r(ns, at, at + 32))])
        else:
            nq, ns, at = "ow", "os_", o0
            quant(r(nq, at, at + 128), r(ns, at, at + 128), r("xt", 0, 512))
        mm(r("py", 0, 128), r("qw", 0, 128), r("sw", 0, 128), r(nq, at, at + 128), r(ns, at, at + 128))
        copy("s", r("yw", o0, o0 + 32), r("py", 0, 32))
        if t == 0:
            dma([("y", r("g1", 0, NEW0), r("g0", 0, NEW0)), ("y", r("h1", 0, NEW0), r("h0", 0, NEW0))])
            dma([("y", r("g2", 0, NEW0), r("g0", 0, NEW0)), ("y", r("h2", 0, NEW0), r("h0", 0, NEW0))])
            lin(r("ndv", 256, 512), r("ndv", 0, 256), 1.0, 256.0)
        ts(col("sel", 0), col("sa_", 0), col("sa_", 1), A.add, col("sa_", 2), A.add)
        ts(col("nd_", 8 + t), col("sel", 0), col("cf", 12), A.add, THIRD, A.mult)
        dma([("y", T.nd[t:t + 1, 0:32], r("nd_", 8 + t, 9 + t, 1, 0, 32))])
        if t < 2:
            places(t)
        if t == 1:
            dma([("y", r("g2", NEW0, NEW0 + 256), r("g1", NEW0, NEW0 + 256)), ("y", r("h2", NEW0, NEW0 + 256), r("h1", NEW0, NEW0 + 256))])
            ts(r("frf", 0, 16), r("iot", 0, 256, 16), 0.0, A.add)
            ts(r("frf", 0, 16), r("frf", 0, 16), 224, A.bitwise_and)
            ts(r("d8", 0, 16), r("frf", 0, 16), col("cf", 1), A.add)
        if t < 2:
            npn = r("np0", 0, 2048)
            copy("v", r("nai", 0, 16), r(na, 0, 16))
            scatter(npn, r("nai", 0, 16), r("ndv", 256 * t, 256 * t + 256))
            tt(r("db", 0, 192), (npn, r("dnb", 0, 12)), r("db", 0, 192), A.max)
            tr(r("dt_", 0, 192), r("db", 0, 192))
            copy("v", r("of", 12 * t + 12, 12 * t + 24), r("dt_", 0, 192, 16))
            for i in range(0, 48, 8):
                tt(r("nl", 16 * i, 16 * i + 128), (npn, r("nbt", i, i + 8)), r("nl", 16 * i, 16 * i + 128), A.max)
            for i in range(0, 768, 256):
                copy("s", r("nl", 768 + i, 1024 + i), r("nl", i, i + 256))

    tr(r("ogt", 0, 256), r("og", 0, 256))
    copy("v", r("oo", 0, 16), r("ogt", 0, 256, 16))
    pick(r("occ", 0, 256), r("ocs", 0, 256), r("ow", 0, 352), r("os_", 0, 352), r("oo", 0, 16))
    dma([("y", T.oc[:], r("occ", 0, 256))])
    dma([("y", T.osc[4 * k:4 * k + 4, :], r("ocs", 0, 256, 1, 32 * k, 32 * k + 4)) for k in range(4)])
    copy("v", r("yt", 0, 128), (r("yw", 0, 352), r("oo", 0, 8)))
    copy("s", r("yt", 128, 256), (r("yw", 0, 352), r("oo", 8, 16)))
    dma([("s", T.y[:], r("yt", 0, 256))])
    flush()
    for sem, c in cnt.items():
        if known["g"].get(sem, 0) < c:
            g.wait_ge(T.sem[sem], c)
